import numpy as np
import ml_dtypes


def mxq(x, axis, fmt="e4m3"):
    dtype, down = {"e4m3": (ml_dtypes.float8_e4m3fn, 7), "e5m2": (ml_dtypes.float8_e5m2, 14)}[fmt]
    v = np.moveaxis(np.asarray(x, np.float32).astype(ml_dtypes.bfloat16).astype(np.float64), axis, -1)
    blocks = v.reshape(v.shape[:-1] + (-1, 32))
    amax = np.abs(blocks).max(-1, keepdims=True)
    byte = np.maximum(np.where(amax > 0, np.frexp(amax)[1] - 1 + 127, 0) - down, 1)
    scale = np.exp2(byte - 127.0)
    codes = (blocks / scale).astype(np.float32).astype(dtype).astype(np.float64)
    return np.moveaxis((codes * scale).reshape(v.shape), -1, axis)


WIDE = False


def mx_kscale(k):
    if not WIDE:
        return np.ones(k)
    levels = np.array([10, -10, 5, -5, 0])
    if k % 512:
        return np.exp2(np.random.permutation(np.resize(levels, k // 32))).repeat(32)
    a = np.empty((k // 512, 16))
    for p in range(k // 512):
        a[p, :8] = np.random.permutation(np.resize(levels, 8))
        for g in range(8):
            far = levels[np.abs(levels - a[p, g]) >= 10]
            a[p, g + 8] = far[np.random.randint(len(far))]
    return np.exp2(a.ravel()).repeat(32)


def f64(x):
    return np.asarray(x).astype(np.float64)


def striped(idx):
    return np.tile(idx.reshape(-1, 16).T, (8, 1)).astype(np.uint16)


def unstriped(offs):
    return offs[:16].T.reshape(-1).astype(np.int64)


E2M1 = np.array([0.0, 0.5, 1.0, 1.5, 2.0, 3.0, 4.0, 6.0, -0.0, -0.5, -1.0, -1.5, -2.0, -3.0, -4.0, -6.0])


def pack_weight(w, fmt):
    k, n = w.shape
    w = f64(np.asarray(w, np.float32).astype(ml_dtypes.bfloat16)).reshape(k // 32, 32, n)
    amax = np.abs(w).max(1)
    if fmt == "e4m3":
        byte = np.frexp(amax)[1] - 1 + 127 - 7
    else:
        mant, ex = np.frexp(amax / 6.0)
        byte = np.where(mant > 0.5, ex, ex - 1) + 127
    byte = np.clip(np.where(amax > 0, byte, 1), 1, 254)
    scaled = (w * np.exp2(127.0 - byte)[:, None, :]).reshape(k, n).astype(np.float32)
    by_word = np.ascontiguousarray(scaled.reshape(k // 512, 128, 4, n).transpose(0, 1, 3, 2))
    if fmt == "e4m3":
        words = by_word.astype(ml_dtypes.float8_e4m3fn).view(np.uint8)
    else:
        c = by_word.astype(ml_dtypes.float4_e2m1fn).view(np.uint8) & 0xF
        words = (c[..., 0::2] | (c[..., 1::2] << 4)).reshape(k // 512, 128, 2 * n)
    return np.ascontiguousarray(words), np.ascontiguousarray(byte.astype(np.uint8).reshape(k // 512, 16, n))


def unpack_weight(words, scales, fmt):
    g, _, n = scales.shape
    words = np.ascontiguousarray(words).reshape(g, 128, n, -1)
    if fmt == "e4m3":
        vals = words.view(ml_dtypes.float8_e4m3fn).astype(np.float64)
    else:
        nib = np.empty((g, 128, n, 4), np.uint8)
        nib[..., 0::2] = words & 0xF
        nib[..., 1::2] = words >> 4
        vals = E2M1[nib]
    vals = vals * np.repeat(np.exp2(scales.astype(np.float64) - 127.0), 8, axis=1)[..., None]
    return vals.transpose(0, 1, 3, 2).reshape(g * 512, n)


def gelu(v):
    return 0.5 * v * (1.0 + np.tanh(np.sqrt(2.0 / np.pi) * (v + 0.044715 * v**3)))


K, M, H, N, T, S = 1024, 512, 1024, 512, 4096, 1024

def setup_inputs():
    n = np.random.standard_normal
    s = mx_kscale(K)[:, None]
    s2 = mx_kscale(M)[:, None]
    u = mx_kscale(H)[:, None]
    tab_words, tab_scales = pack_weight(n((K, T)) * s, "e4m3")
    w4_words, w4_scales = pack_weight(n((K, H)) / np.sqrt(K) / s, "e2m1")
    w8_words, w8_scales = pack_weight(1.5 * n((H, N)) / np.sqrt(H) / u, "e4m3")
    return {
        "tab_words": tab_words, "tab_scales": tab_scales,
        "offs": striped(np.random.permutation(T)[:S]),
        "w4_words": w4_words, "w4_scales": w4_scales,
        "adj": (n((M, S)) * s2).astype(np.float32),
        "w2": (n((M, H)) / np.sqrt(M) / s2 * u.T).astype(np.float32),
        "w8_words": w8_words, "w8_scales": w8_scales,
        "offs2": striped(np.random.permutation(S)),
        "wgo": np.exp(0.3 * n((128, S))).astype(np.float32),
        "x0": n((N, S)).astype(np.float32),
    }

def reference(tab_words, tab_scales, offs, w4_words, w4_scales, adj, w2, w8_words, w8_scales, offs2, wgo, x0):
    v = unpack_weight(tab_words, tab_scales, "e4m3")[:, unstriped(offs)]
    w4 = unpack_weight(w4_words, w4_scales, "e2m1")
    w8 = unpack_weight(w8_words, w8_scales, "e4m3")
    x = np.tanh(w4.T @ v)
    b = mxq(f64(w2), 0, "e4m3").T @ mxq(f64(adj), 0, "e4m3")
    h = (1.0 - np.square(x)) * b
    y = w8.T @ mxq(h, 0, "e4m3")
    page = np.zeros((N, S))
    page[:, unstriped(offs2)] = np.tile(f64(wgo), (N // 128, 1)) * y
    return f64(x0) - page

@@ -1,0 +1,297 @@
+from contextlib import ExitStack
+
+import concourse.mybir as mybir
+from concourse.masks import make_identity
+
+K, M, H, N, T, S = 1024, 512, 1024, 512, 4096, 1024
+FLOPS = 2 * (K * H * S + M * H * S + H * N * S)
+
+F32 = mybir.dt.float32
+BF16 = mybir.dt.bfloat16
+I32 = mybir.dt.int32
+U32 = mybir.dt.uint32
+U16 = mybir.dt.uint16
+U8 = mybir.dt.uint8
+FP8X4 = mybir.dt.float8_e4m3fn_x4
+FP4X4 = mybir.dt.float4_e2m1fn_x4
+ALU = mybir.AluOpType
+ACT = mybir.ActivationFunctionType
+
+P = 128
+G = 256
+U = 128
+
+
+def tile_list_delay_sensitivity_rows_kernel(
+    tc, tab_words, tab_scales, offs, w4_words, w4_scales, adj, w2, w8_words, w8_scales, offs2, wgo, x0, out
+):
+    nc = tc.nc
+    with ExitStack() as ctx:
+        keep = ctx.enter_context(tc.tile_pool(name="keep", bufs=1))
+        turns = ctx.enter_context(tc.tile_pool(name="turns", bufs=1))
+        ring = ctx.enter_context(tc.tile_pool(name="ring", bufs=2))
+        psum = ctx.enter_context(tc.psum_pool(name="psum", bufs=2))
+
+        def held(shape, dtype, name):
+            return keep.tile(shape, dtype, name=name, align_bytes=64)
+
+        idx = keep.tile([P, S // 16], U16, name="idx")
+        idx2 = keep.tile([P, S // 16], U16, name="idx2")
+
+        ROW = S + H + N
+        tab_sc = held([P, T], U8, "tab_sc")
+        w4_sc_raw = held([P, H], U8, "w4_sc_raw")
+        staged = held([P, ROW], U8, "staged")
+        planes = held([P, 2 * ROW], U8, "planes")
+        nc.sync.dma_start(idx[:], offs)
+        nc.sync.dma_start(out=tab_sc[0:32, :].bitcast(I32), in_=tab_scales.bitcast(I32).rearrange("a q t -> q a t"))
+        nc.sync.dma_start(out=w4_sc_raw[0:32, :].bitcast(I32), in_=w4_scales.bitcast(I32).rearrange("a q t -> q a t"))
+        nc.sync.dma_start(
+            out=staged[0:32, S + H : ROW].bitcast(I32), in_=w8_scales.bitcast(I32).rearrange("a q t -> q a t")
+        )
+        nc.sync.dma_start(idx2[:], offs2)
+        for tile in (tab_sc, w4_sc_raw):
+            nc.vector.memset(tile[32:64, :].bitcast(I32), 0)
+            nc.vector.memset(tile[64:P, :].bitcast(I32), 0)
+        nc.vector.memset(planes[:].bitcast(I32), 0)
+
+        def reused(shape, dtype, name, kib):
+            return turns.tile(shape, dtype, name=name, offset=1024 * kib, align_bytes=64)
+
+        w4_raw = reused([P, 2, 2 * H], U8, "w4_raw", 32)
+        nc.sync.dma_start(out=w4_raw[:].bitcast(I32), in_=w4_words.bitcast(I32).rearrange("a p c -> p a c"))
+        tab = [reused([P, T], U32, f"tab{a}", 16 * a) for a in range(2)]
+        for a in range(2):
+            nc.sync.dma_start(
+                out=tab[a][:].bitcast(I32), in_=tab_words[a].rearrange("p t i -> p (t i)").bitcast(I32)
+            )
+
+        picked_sc = held([P, S], U8, "picked_sc")
+        nc.vector.tensor_copy(picked_sc[:], tab_sc[:].indirect(idx[:]))
+        nc.vector.tensor_copy(
+            staged[:, S : S + H].rearrange("p (b t u m) -> p b u t m", b=2, t=4, m=16),
+            w4_sc_raw[:].rearrange("p (b u m t) -> p b u t m", b=2, t=4, m=16),
+        )
+        nc.vector.tensor_copy(staged[0:32, 0:S].bitcast(I32), picked_sc[0:32, :].bitcast(I32))
+        for q in range(4):
+            nc.scalar.dma_start(
+                out=planes[32 * q : 32 * q + 4, :].bitcast(I32).rearrange("r (a c) -> r a c", a=2),
+                in_=staged[8 * q : 8 * q + 8, :].bitcast(I32),
+            )
+        w4 = held([P, 4 * H], U8, "w4")
+        nc.vector.tensor_copy(
+            w4[:].bitcast(U16).rearrange("p (b t u m) -> p b u t m", b=4, t=4, m=8),
+            w4_raw[:].rearrange("p a c -> p (a c)").bitcast(U16).rearrange("p (b u m t) -> p b u t m", b=4, t=4, m=8),
+        )
+        v = [[held([P, 512], U32, f"v{a}_{e}") for e in range(2)] for a in range(2)]
+        for a in range(2):
+            for e in range(2):
+                nc.vector.tensor_copy(v[a][e][:], tab[a][:].indirect(idx[:, 32 * e : 32 * (e + 1)]))
+
+        w2_raw = [reused([P, 4, 512], F32, f"w2_raw{a}", 8 * a) for a in range(2)]
+        adj_raw = [reused([P, 4, G], F32, f"adj_raw{g}", kib) for g, kib in enumerate((32, 16, 28, 32))]
+        w8 = reused([P, 2, N], U32, "w8", 20)
+        step = reused([P, S], F32, "step", 24)
+        base2 = [reused([P, 2, S], F32, f"base{a}", 8 * a) for a in range(2)]
+
+        def load_w2(a):
+            nc.sync.dma_start(
+                out=w2_raw[a][:], in_=w2[:, 512 * a : 512 * (a + 1)].rearrange("(p i) c -> p i c", i=4)
+            )
+
+        def load_adj(g):
+            nc.sync.dma_start(
+                out=adj_raw[g][:], in_=adj[:, G * g : G * (g + 1)].rearrange("(p i) c -> p i c", i=4)
+            )
+
+        def load_base(a):
+            nc.sync.dma_start(out=base2[a][:], in_=x0[256 * a : 256 * (a + 1), :].rearrange("(c p) j -> p c j", p=P))
+
+        load_adj(0)
+        load_w2(0)
+        load_w2(1)
+        load_adj(1)
+        nc.sync.dma_start(
+            out=w8[:].bitcast(I32), in_=w8_words.rearrange("a p c i -> p a (c i)").bitcast(I32)
+        )
+        nc.sync.dma_start(out=step[:], in_=wgo)
+        load_adj(2)
+
+        ident = held([P, P], F32, "ident")
+        make_identity(nc, ident[:])
+        warm = held([P, 1], F32, "warm")
+        nc.scalar.activation(warm[:], ident[:, 0:1], ACT.Tanh)
+
+        w2_q = [held([P, 512], U32, f"w2_q{a}") for a in range(2)]
+        w2_sc = [held([P, 512], U8, f"w2_sc{a}") for a in range(2)]
+        adj_q = [held([P, G], U32, f"adj_q{g}") for g in range(4)]
+        adj_sc = [held([P, G], U8, f"adj_sc{g}") for g in range(4)]
+        h_q = [[held([P, G], U32, f"h_q{g}_{a}") for a in range(2)] for g in range(4)]
+        h_sc = [[held([P, G], U8, f"h_sc{g}_{a}") for a in range(2)] for g in range(4)]
+        page = [held([P, S], F32, f"page{c}") for c in range(4)]
+
+        def quantise_w2(a):
+            rounded = ring.tile([P, 2048], BF16, name="w2_bf", align_bytes=64)
+            nc.vector.tensor_copy(
+                rounded[:].rearrange("p (t m i) -> p m t i", t=4, i=4),
+                w2_raw[a][:].rearrange("p i (m t) -> p m t i", t=4),
+            )
+            nc.vector.quantize_mx(out=w2_q[a][:].bitcast(FP8X4), scales=w2_sc[a][:], in_=rounded[:])
+
+        def quantise_adj(g, on_scalar):
+            rounded = ring.tile([P, 4 * G], BF16, name="adj_bf", align_bytes=64)
+            dst = rounded[:].rearrange("p (c e i) -> p c i e", e=4, i=4)
+            src = adj_raw[g][:].rearrange("p i (c e) -> p c i e", e=4)
+            if on_scalar:
+                nc.scalar.copy(dst, src)
+            else:
+                nc.vector.tensor_copy(dst, src)
+            nc.vector.quantize_mx(out=adj_q[g][:].bitcast(FP8X4), scales=adj_sc[g][:], in_=rounded[:])
+
+        def squares(g, a):
+            made = []
+            for u in range(2):
+                j0 = G * g + U * u
+                bank = psum.tile([P, 4, U], F32, name="xbank", tag="x", bufs=2)
+                for k in range(2):
+                    for t in range(4):
+                        c0 = 512 * a + P * t
+                        nc.tensor.matmul_mx(
+                            out=bank[:, t, :],
+                            lhsT=w4[:, 2 * (H * k + c0) : 2 * (H * k + c0 + P)].bitcast(FP4X4),
+                            lhsT_scale=planes[:, ROW * k + S + c0 : ROW * k + S + c0 + P],
+                            rhs=v[k][j0 // 512][:, j0 % 512 : j0 % 512 + U].bitcast(FP8X4),
+                            rhs_scale=planes[:, ROW * k + j0 : ROW * k + j0 + U],
+                            start=(k == 0 and t == 0),
+                            stop=(k == 1 and t == 3),
+                        )
+                state = ring.tile([P, U, 4], F32, name="state")
+                nc.scalar.activation(state[:], bank[:].rearrange("p t j -> p j t"), ACT.Tanh)
+                sq = ring.tile([P, U, 4], F32, name="sq", bufs=8)
+                nc.scalar.activation(sq[:], state[:], ACT.Square)
+                made.append(sq)
+            return made
+
+        def hidden(g, a, sqs):
+            rounded = ring.tile([P, G, 4], BF16, name="h_bf", align_bytes=64, bufs=3)
+            for u in range(2):
+                bank = psum.tile([P, 4, U], F32, name="bbank", tag="b", bufs=4)
+                for t in range(4):
+                    nc.tensor.matmul_mx(
+                        out=bank[:, t, :],
+                        lhsT=w2_q[a][:, P * t : P * (t + 1)].bitcast(FP8X4),
+                        lhsT_scale=w2_sc[a][:, P * t : P * (t + 1)],
+                        rhs=adj_q[g][:, U * u : U * (u + 1)].bitcast(FP8X4),
+                        rhs_scale=adj_sc[g][:, U * u : U * (u + 1)],
+                        start=True,
+                        stop=True,
+                    )
+                nc.vector.scalar_tensor_tensor(
+                    out=rounded[:, U * u : U * (u + 1), :],
+                    in0=sqs[u][:],
+                    scalar=1.0,
+                    in1=bank[:].rearrange("p t j -> p j t"),
+                    op0=ALU.subtract,
+                    op1=ALU.mult,
+                )
+            return rounded
+
+        def quantise_h(g, a, rounded):
+            nc.vector.quantize_mx(
+                out=h_q[g][a][:].bitcast(FP8X4), scales=h_sc[g][a][:], in_=rounded[:].rearrange("p j t -> p (j t)")
+            )
+
+        def product(pairs, tag="y", bufs=2):
+            bank = psum.tile([P, 2, G], F32, name="ybank", tag=tag, bufs=bufs)
+            for e, (c, g) in enumerate(pairs):
+                for a in range(2):
+                    nc.tensor.matmul_mx(
+                        out=bank[:, e, :],
+                        lhsT=w8[:, a, P * c : P * (c + 1)].bitcast(FP8X4),
+                        lhsT_scale=planes[:, ROW * a + S + H + P * c : ROW * a + S + H + P * (c + 1)],
+                        rhs=h_q[g][a][:].bitcast(FP8X4),
+                        rhs_scale=h_sc[g][a][:],
+                        start=(a == 0),
+                        stop=(a == 1),
+                    )
+            y = ring.tile([P, 2 * G], F32, name="y", bufs=6)
+            nc.scalar.copy(y[:], bank[:].rearrange("p e j -> p (e j)"))
+            return y
+
+        def place(c, y, j0, width):
+            nc.vector.tensor_tensor(
+                page[c][:].indirect(idx2[:, j0 // 16 : (j0 + width) // 16]), y, step[:, j0 : j0 + width], ALU.mult
+            )
+
+        def place_group(g):
+            ys = [product([(0, g), (1, g)]), product([(2, g), (3, g)])]
+            return ys
+
+        def scatter_group(g, ys):
+            for c in range(4):
+                place(c, ys[c // 2][:, G * (c % 2) : G * (c % 2 + 1)], G * g, G)
+
+        def finish_on_tensor(c):
+            for e in range(2):
+                turned = psum.tile([P, 4, P], F32, name="turned", tag="x", bufs=2)
+                for b in range(4):
+                    cols = slice(512 * e + P * b, 512 * e + P * (b + 1))
+                    nc.tensor.matmul(turned[:, b, :], base2[c // 2][:, c % 2, cols], ident[:], start=True, stop=False, is_transpose=True)
+                    nc.tensor.matmul(turned[:, b, :], page[c][:, cols], ident[:], start=False, stop=True, is_transpose=True)
+                total_t = ring.tile([P, 4, P], F32, name="total_t")
+                nc.scalar.copy(total_t[:], turned[:])
+                back = psum.tile([P, 4, P], F32, name="back", tag="b", bufs=4)
+                for b in range(4):
+                    nc.tensor.transpose(back[:, b, :], total_t[:, b, :], ident[:])
+                total = ring.tile([P, 512], F32, name="total", bufs=3)
+                nc.scalar.copy(total[:], back[:].rearrange("p b j -> p (b j)"))
+                nc.sync.dma_start(out=out[P * c : P * (c + 1), 512 * e : 512 * (e + 1)], in_=total[:])
+
+        def finish_on_vector(c):
+            for e in range(2):
+                cols = slice(512 * e, 512 * (e + 1))
+                total = ring.tile([P, 512], F32, name="total", bufs=3)
+                nc.vector.tensor_tensor(total[:], base2[c // 2][:, c % 2, cols], page[c][:, cols], ALU.add)
+                nc.sync.dma_start(out=out[P * c : P * (c + 1), cols], in_=total[:])
+
+        def hidden_group(g, sqs):
+            r0 = hidden(g, 0, sqs[0])
+            r1 = hidden(g, 1, sqs[1])
+            quantise_h(g, 0, r0)
+            quantise_h(g, 1, r1)
+            return r1
+
+        def scatter_pair(g, first, y):
+            for e in range(2):
+                place(first + e, y[:, G * e : G * (e + 1)], G * g, G)
+
+        sq0 = [squares(0, a) for a in range(2)]
+        quantise_adj(0, False)
+        load_adj(3)
+        quantise_w2(0)
+        load_base(0)
+        quantise_w2(1)
+        load_base(1)
+        sq1 = [squares(1, a) for a in range(2)]
+        hidden_group(0, sq0)
+        quantise_adj(1, False)
+        y0 = place_group(0)
+        hidden_group(1, sq1)
+        quantise_adj(2, False)
+        quantise_adj(3, True)
+        sq2 = [squares(2, a) for a in range(2)]
+        scatter_group(0, y0)
+        y1a = product([(0, 1), (1, 1)])
+        hidden_group(2, sq2)
+        sq3 = [squares(3, a) for a in range(2)]
+        scatter_pair(1, 0, y1a)
+        hidden_group(3, sq3)
+        y1b = product([(2, 1), (3, 1)], "b", 4)
+        ys = [product([(c, 2), (c, 3)]) for c in range(4)]
+        scatter_pair(1, 2, y1b)
+        for c in range(4):
+            place(c, ys[c][:], 2 * G, 2 * G)
+            if c < 3:
+                finish_on_tensor(c)
+            else:
+                finish_on_vector(c)

@@ -58,7 +58,7 @@ def tile_list_delay_sensitivity_rows_kernel(
         def reused(shape, dtype, name, kib):
             return turns.tile(shape, dtype, name=name, offset=1024 * kib, align_bytes=64)
 
-        w4_raw = reused([P, 2, 2 * H], U8, "w4_raw", 32)
+        w4_raw = reused([P, 2, 2 * H], U8, "w4_raw", 34)
         nc.sync.dma_start(out=w4_raw[:].bitcast(I32), in_=w4_words.bitcast(I32).rearrange("a p c -> p a c"))
         tab = [reused([P, T], U32, f"tab{a}", 16 * a) for a in range(2)]
         for a in range(2):
@@ -83,16 +83,16 @@ def tile_list_delay_sensitivity_rows_kernel(
             w4[:].bitcast(U16).rearrange("p (b t u m) -> p b u t m", b=4, t=4, m=8),
             w4_raw[:].rearrange("p a c -> p (a c)").bitcast(U16).rearrange("p (b u m t) -> p b u t m", b=4, t=4, m=8),
         )
-        v = [[held([P, 512], U32, f"v{a}_{e}") for e in range(2)] for a in range(2)]
-        for a in range(2):
-            for e in range(2):
-                nc.vector.tensor_copy(v[a][e][:], tab[a][:].indirect(idx[:, 32 * e : 32 * (e + 1)]))
+        v = [held([P, S], U32, f"v{a}") for a in range(2)]
+        nc.vector.tensor_copy(v[0][:], tab[0][:].indirect(idx[:]))
+        for e in range(2):
+            nc.vector.tensor_copy(v[1][:, 512 * e : 512 * (e + 1)], tab[1][:].indirect(idx[:, 32 * e : 32 * (e + 1)]))
 
-        w2_raw = [reused([P, 4, 512], F32, f"w2_raw{a}", 8 * a) for a in range(2)]
+        w2_raw = [reused([P, 4, 512], F32, f"w2_raw{a}", kib) for a, kib in enumerate((36, 0))]
         adj_raw = [reused([P, 4, G], F32, f"adj_raw{g}", kib) for g, kib in enumerate((32, 16, 28, 32))]
         w8 = reused([P, 2, N], U32, "w8", 20)
         step = reused([P, S], F32, "step", 24)
-        base2 = [reused([P, 2, S], F32, f"base{a}", 8 * a) for a in range(2)]
+        base = reused([P, 4, S], F32, "base", 0)
 
         def load_w2(a):
             nc.sync.dma_start(
@@ -104,9 +104,6 @@ def tile_list_delay_sensitivity_rows_kernel(
                 out=adj_raw[g][:], in_=adj[:, G * g : G * (g + 1)].rearrange("(p i) c -> p i c", i=4)
             )
 
-        def load_base(a):
-            nc.sync.dma_start(out=base2[a][:], in_=x0[256 * a : 256 * (a + 1), :].rearrange("(c p) j -> p c j", p=P))
-
         load_adj(0)
         load_w2(0)
         load_w2(1)
@@ -114,8 +111,6 @@ def tile_list_delay_sensitivity_rows_kernel(
         nc.sync.dma_start(
             out=w8[:].bitcast(I32), in_=w8_words.rearrange("a p c i -> p a (c i)").bitcast(I32)
         )
-        nc.sync.dma_start(out=step[:], in_=wgo)
-        load_adj(2)
 
         ident = held([P, P], F32, "ident")
         make_identity(nc, ident[:])
@@ -131,7 +126,10 @@ def tile_list_delay_sensitivity_rows_kernel(
         page = [held([P, S], F32, f"page{c}") for c in range(4)]
 
         def quantise_w2(a):
-            rounded = ring.tile([P, 2048], BF16, name="w2_bf", align_bytes=64)
+            if a == 0:
+                rounded = reused([P, 2048], BF16, "w2_bf0", 24)
+            else:
+                rounded = held([P, 2048], BF16, "w2_bf1")
             nc.vector.tensor_copy(
                 rounded[:].rearrange("p (t m i) -> p m t i", t=4, i=4),
                 w2_raw[a][:].rearrange("p i (m t) -> p m t i", t=4),
@@ -139,7 +137,10 @@ def tile_list_delay_sensitivity_rows_kernel(
             nc.vector.quantize_mx(out=w2_q[a][:].bitcast(FP8X4), scales=w2_sc[a][:], in_=rounded[:])
 
         def quantise_adj(g, on_scalar):
-            rounded = ring.tile([P, 4 * G], BF16, name="adj_bf", align_bytes=64)
+            if g == 0:
+                rounded = reused([P, 4 * G], BF16, "adj_bf0", 28)
+            else:
+                rounded = held([P, 4 * G], BF16, f"adj_bf{g}")
             dst = rounded[:].rearrange("p (c e i) -> p c i e", e=4, i=4)
             src = adj_raw[g][:].rearrange("p i (c e) -> p c i e", e=4)
             if on_scalar:
@@ -149,10 +150,10 @@ def tile_list_delay_sensitivity_rows_kernel(
             nc.vector.quantize_mx(out=adj_q[g][:].bitcast(FP8X4), scales=adj_sc[g][:], in_=rounded[:])
 
         def squares(g, a):
-            made = []
+            state = ring.tile([P, G, 4], F32, name="state")
             for u in range(2):
                 j0 = G * g + U * u
-                bank = psum.tile([P, 4, U], F32, name="xbank", tag="x", bufs=2)
+                bank = psum.tile([P, 4, U], F32, name="xbank", tag="x", bufs=3)
                 for k in range(2):
                     for t in range(4):
                         c0 = 512 * a + P * t
@@ -160,17 +161,15 @@ def tile_list_delay_sensitivity_rows_kernel(
                             out=bank[:, t, :],
                             lhsT=w4[:, 2 * (H * k + c0) : 2 * (H * k + c0 + P)].bitcast(FP4X4),
                             lhsT_scale=planes[:, ROW * k + S + c0 : ROW * k + S + c0 + P],
-                            rhs=v[k][j0 // 512][:, j0 % 512 : j0 % 512 + U].bitcast(FP8X4),
+                            rhs=v[k][:, j0 : j0 + U].bitcast(FP8X4),
                             rhs_scale=planes[:, ROW * k + j0 : ROW * k + j0 + U],
                             start=(k == 0 and t == 0),
                             stop=(k == 1 and t == 3),
                         )
-                state = ring.tile([P, U, 4], F32, name="state")
-                nc.scalar.activation(state[:], bank[:].rearrange("p t j -> p j t"), ACT.Tanh)
-                sq = ring.tile([P, U, 4], F32, name="sq", bufs=8)
-                nc.scalar.activation(sq[:], state[:], ACT.Square)
-                made.append(sq)
-            return made
+                nc.scalar.activation(state[:, U * u : U * (u + 1), :], bank[:].rearrange("p t j -> p j t"), ACT.Tanh)
+            sq = ring.tile([P, G, 4], F32, name="sq", bufs=4)
+            nc.scalar.activation(sq[:], state[:], ACT.Square)
+            return sq
 
         def hidden(g, a, sqs):
             rounded = ring.tile([P, G, 4], BF16, name="h_bf", align_bytes=64, bufs=3)
@@ -188,7 +187,7 @@ def tile_list_delay_sensitivity_rows_kernel(
                     )
                 nc.vector.scalar_tensor_tensor(
                     out=rounded[:, U * u : U * (u + 1), :],
-                    in0=sqs[u][:],
+                    in0=sqs[:, U * u : U * (u + 1), :],
                     scalar=1.0,
                     in1=bank[:].rearrange("p t j -> p j t"),
                     op0=ALU.subtract,
@@ -201,7 +200,7 @@ def tile_list_delay_sensitivity_rows_kernel(
                 out=h_q[g][a][:].bitcast(FP8X4), scales=h_sc[g][a][:], in_=rounded[:].rearrange("p j t -> p (j t)")
             )
 
-        def product(pairs, tag="y", bufs=2):
+        def product(pairs, tag="y", bufs=1):
             bank = psum.tile([P, 2, G], F32, name="ybank", tag=tag, bufs=bufs)
             for e, (c, g) in enumerate(pairs):
                 for a in range(2):
@@ -214,7 +213,7 @@ def tile_list_delay_sensitivity_rows_kernel(
                         start=(a == 0),
                         stop=(a == 1),
                     )
-            y = ring.tile([P, 2 * G], F32, name="y", bufs=6)
+            y = ring.tile([P, 2 * G], F32, name="y", bufs=8)
             nc.scalar.copy(y[:], bank[:].rearrange("p e j -> p (e j)"))
             return y
 
@@ -231,28 +230,38 @@ def tile_list_delay_sensitivity_rows_kernel(
             for c in range(4):
                 place(c, ys[c // 2][:, G * (c % 2) : G * (c % 2 + 1)], G * g, G)
 
-        def finish_on_tensor(c):
+        def open_sums(c):
+            banks = []
             for e in range(2):
-                turned = psum.tile([P, 4, P], F32, name="turned", tag="x", bufs=2)
+                turned = psum.tile([P, 4, P], F32, name="turned", tag="b", bufs=4)
                 for b in range(4):
                     cols = slice(512 * e + P * b, 512 * e + P * (b + 1))
-                    nc.tensor.matmul(turned[:, b, :], base2[c // 2][:, c % 2, cols], ident[:], start=True, stop=False, is_transpose=True)
-                    nc.tensor.matmul(turned[:, b, :], page[c][:, cols], ident[:], start=False, stop=True, is_transpose=True)
+                    nc.tensor.matmul(turned[:, b, :], base[:, c, cols], ident[:], start=(b == 0), stop=False, is_transpose=True)
+                banks.append(turned)
+            return banks
+
+        def finish_on_tensor(c, banks):
+            sums = []
+            for e in range(2):
+                for b in range(4):
+                    cols = slice(512 * e + P * b, 512 * e + P * (b + 1))
+                    nc.tensor.matmul(banks[e][:, b, :], page[c][:, cols], ident[:], start=False, stop=(b == 3), is_transpose=True)
                 total_t = ring.tile([P, 4, P], F32, name="total_t")
-                nc.scalar.copy(total_t[:], turned[:])
+                nc.scalar.copy(total_t[:], banks[e][:])
+                sums.append(total_t)
+            for e in range(2):
                 back = psum.tile([P, 4, P], F32, name="back", tag="b", bufs=4)
                 for b in range(4):
-                    nc.tensor.transpose(back[:, b, :], total_t[:, b, :], ident[:])
-                total = ring.tile([P, 512], F32, name="total", bufs=3)
+                    nc.tensor.transpose(back[:, b, :], sums[e][:, b, :], ident[:])
+                total = ring.tile([P, 512], F32, name="total", bufs=4)
                 nc.scalar.copy(total[:], back[:].rearrange("p b j -> p (b j)"))
-                nc.sync.dma_start(out=out[P * c : P * (c + 1), 512 * e : 512 * (e + 1)], in_=total[:])
+                nc.scalar.dma_start(out=out[P * c : P * (c + 1), 512 * e : 512 * (e + 1)], in_=total[:])
 
         def finish_on_vector(c):
-            for e in range(2):
-                cols = slice(512 * e, 512 * (e + 1))
-                total = ring.tile([P, 512], F32, name="total", bufs=3)
-                nc.vector.tensor_tensor(total[:], base2[c // 2][:, c % 2, cols], page[c][:, cols], ALU.add)
-                nc.sync.dma_start(out=out[P * c : P * (c + 1), cols], in_=total[:])
+            total = held([P, S], F32, "last_total")
+            for cols in (slice(0, 640), slice(640, S)):
+                nc.vector.tensor_tensor(total[:, cols], base[:, c, cols], page[c][:, cols], ALU.add)
+                nc.sync.dma_start(out=out[P * c : P * (c + 1), cols], in_=total[:, cols])
 
         def hidden_group(g, sqs):
             r0 = hidden(g, 0, sqs[0])
@@ -267,11 +276,12 @@ def tile_list_delay_sensitivity_rows_kernel(
 
         sq0 = [squares(0, a) for a in range(2)]
         quantise_adj(0, False)
+        load_adj(2)
         load_adj(3)
         quantise_w2(0)
-        load_base(0)
+        nc.sync.dma_start(out=step[:], in_=wgo)
         quantise_w2(1)
-        load_base(1)
+        nc.sync.dma_start(out=base[:], in_=x0.rearrange("(c p) j -> p c j", p=P))
         sq1 = [squares(1, a) for a in range(2)]
         hidden_group(0, sq0)
         quantise_adj(1, False)
@@ -287,11 +297,15 @@ def tile_list_delay_sensitivity_rows_kernel(
         scatter_pair(1, 0, y1a)
         hidden_group(3, sq3)
         y1b = product([(2, 1), (3, 1)], "b", 4)
-        ys = [product([(c, 2), (c, 3)]) for c in range(4)]
-        scatter_pair(1, 2, y1b)
+        ys = [product([(c, 2), (c, 3)], "x", 3) for c in range(4)]
+        place(2, y1b[:, 0:G], G, G)
         for c in range(4):
+            if c == 3:
+                place(3, y1b[:, G : 2 * G], G, G)
+            if c < 3:
+                banks = open_sums(c)
             place(c, ys[c][:], 2 * G, 2 * G)
             if c < 3:
-                finish_on_tensor(c)
+                finish_on_tensor(c, banks)
             else:
                 finish_on_vector(c)

@@ -123,7 +123,7 @@ def tile_list_delay_sensitivity_rows_kernel(
         adj_sc = [held([P, G], U8, f"adj_sc{g}") for g in range(4)]
         h_q = [[held([P, G], U32, f"h_q{g}_{a}") for a in range(2)] for g in range(4)]
         h_sc = [[held([P, G], U8, f"h_sc{g}_{a}") for a in range(2)] for g in range(4)]
-        page = [held([P, S], F32, f"page{c}") for c in range(4)]
+        page = [held([P, S], F32, f"page{c}") for c in range(3)]
 
         def quantise_w2(a):
             if a == 0:
@@ -172,7 +172,10 @@ def tile_list_delay_sensitivity_rows_kernel(
             return sq
 
         def hidden(g, a, sqs):
-            rounded = ring.tile([P, G, 4], BF16, name="h_bf", align_bytes=64, bufs=3)
+            if g == 3:
+                rounded = reused([P, G, 4], BF16, f"h_bf_last{a}", (48, 44)[a])
+            else:
+                rounded = ring.tile([P, G, 4], BF16, name="h_bf", align_bytes=64, bufs=3)
             for u in range(2):
                 bank = psum.tile([P, 4, U], F32, name="bbank", tag="b", bufs=4)
                 for t in range(4):
@@ -200,7 +203,7 @@ def tile_list_delay_sensitivity_rows_kernel(
                 out=h_q[g][a][:].bitcast(FP8X4), scales=h_sc[g][a][:], in_=rounded[:].rearrange("p j t -> p (j t)")
             )
 
-        def product(pairs, tag="y", bufs=1):
+        def product(pairs, tag="y", bufs=1, kib=None):
             bank = psum.tile([P, 2, G], F32, name="ybank", tag=tag, bufs=bufs)
             for e, (c, g) in enumerate(pairs):
                 for a in range(2):
@@ -213,8 +216,12 @@ def tile_list_delay_sensitivity_rows_kernel(
                         start=(a == 0),
                         stop=(a == 1),
                     )
-            y = ring.tile([P, 2 * G], F32, name="y", bufs=8)
-            nc.scalar.copy(y[:], bank[:].rearrange("p e j -> p (e j)"))
+            if kib is None:
+                y = ring.tile([P, 2 * G], F32, name="y", bufs=7)
+            else:
+                y = reused([P, 2 * G], F32, f"y_at{kib}", kib)
+            width = G * len(pairs)
+            nc.scalar.copy(y[:, 0:width], bank[:].rearrange("p e j -> p (e j)")[:, 0:width])
             return y
 
         def place(c, y, j0, width):
@@ -222,12 +229,8 @@ def tile_list_delay_sensitivity_rows_kernel(
                 page[c][:].indirect(idx2[:, j0 // 16 : (j0 + width) // 16]), y, step[:, j0 : j0 + width], ALU.mult
             )
 
-        def place_group(g):
-            ys = [product([(0, g), (1, g)]), product([(2, g), (3, g)])]
-            return ys
-
         def scatter_group(g, ys):
-            for c in range(4):
+            for c in range(3):
                 place(c, ys[c // 2][:, G * (c % 2) : G * (c % 2 + 1)], G * g, G)
 
         def open_sums(c):
@@ -249,17 +252,17 @@ def tile_list_delay_sensitivity_rows_kernel(
                 total_t = ring.tile([P, 4, P], F32, name="total_t")
                 nc.scalar.copy(total_t[:], banks[e][:])
                 sums.append(total_t)
+            total = ring.tile([P, S], F32, name="total", bufs=3)
             for e in range(2):
                 back = psum.tile([P, 4, P], F32, name="back", tag="b", bufs=4)
                 for b in range(4):
                     nc.tensor.transpose(back[:, b, :], sums[e][:, b, :], ident[:])
-                total = ring.tile([P, 512], F32, name="total", bufs=4)
-                nc.scalar.copy(total[:], back[:].rearrange("p b j -> p (b j)"))
-                nc.scalar.dma_start(out=out[P * c : P * (c + 1), 512 * e : 512 * (e + 1)], in_=total[:])
+                nc.scalar.copy(total[:, 512 * e : 512 * (e + 1)], back[:].rearrange("p b j -> p (b j)"))
+            nc.scalar.dma_start(out=out[P * c : P * (c + 1), :], in_=total[:])
 
         def finish_on_vector(c):
             total = held([P, S], F32, "last_total")
-            for cols in (slice(0, 640), slice(640, S)):
+            for cols in (slice(0, 384), slice(384, 768), slice(768, S)):
                 nc.vector.tensor_tensor(total[:, cols], base[:, c, cols], page[c][:, cols], ALU.add)
                 nc.sync.dma_start(out=out[P * c : P * (c + 1), cols], in_=total[:, cols])
 
@@ -269,10 +272,6 @@ def tile_list_delay_sensitivity_rows_kernel(
             quantise_h(g, 0, r0)
             quantise_h(g, 1, r1)
             return r1
-
-        def scatter_pair(g, first, y):
-            for e in range(2):
-                place(first + e, y[:, G * e : G * (e + 1)], G * g, G)
 
         sq0 = [squares(0, a) for a in range(2)]
         quantise_adj(0, False)
@@ -285,27 +284,29 @@ def tile_list_delay_sensitivity_rows_kernel(
         sq1 = [squares(1, a) for a in range(2)]
         hidden_group(0, sq0)
         quantise_adj(1, False)
-        y0 = place_group(0)
+        y0 = [product([(0, 0), (1, 0)]), product([(2, 0), (3, 0)])]
         hidden_group(1, sq1)
         quantise_adj(2, False)
         quantise_adj(3, True)
         sq2 = [squares(2, a) for a in range(2)]
         scatter_group(0, y0)
-        y1a = product([(0, 1), (1, 1)])
+        y1 = product([(0, 1), (1, 1)], kib=48)
         hidden_group(2, sq2)
         sq3 = [squares(3, a) for a in range(2)]
-        scatter_pair(1, 0, y1a)
+        for c in range(2):
+            place(c, y1[:, G * c : G * (c + 1)], G, G)
         hidden_group(3, sq3)
-        y1b = product([(2, 1), (3, 1)], "b", 4)
-        ys = [product([(c, 2), (c, 3)], "x", 3) for c in range(4)]
-        place(2, y1b[:, 0:G], G, G)
-        for c in range(4):
-            if c == 3:
-                place(3, y1b[:, G : 2 * G], G, G)
-            if c < 3:
-                banks = open_sums(c)
+        page.append(reused([P, S], F32, "page3", 44))
+        y1_late = product([(2, 1)], kib=48)
+        ys = [product([(c, 2), (c, 3)], "x", 3) for c in range(3)]
+        y_mid = product([(3, 1), (3, 2)], "x", 3)
+        y_end = product([(3, 3)], "x", 3)
+        place(3, y0[1][:, G : 2 * G], 0, G)
+        place(2, y1_late[:, 0:G], G, G)
+        for c in range(3):
+            banks = open_sums(c)
             place(c, ys[c][:], 2 * G, 2 * G)
-            if c < 3:
-                finish_on_tensor(c, banks)
-            else:
-                finish_on_vector(c)
+            finish_on_tensor(c, banks)
+        place(3, y_mid[:], G, 2 * G)
+        place(3, y_end[:, 0:G], 3 * G, G)
+        finish_on_vector(3)

@@ -89,9 +89,9 @@ def tile_list_delay_sensitivity_rows_kernel(
             nc.vector.tensor_copy(v[1][:, 512 * e : 512 * (e + 1)], tab[1][:].indirect(idx[:, 32 * e : 32 * (e + 1)]))
 
         w2_raw = [reused([P, 4, 512], F32, f"w2_raw{a}", kib) for a, kib in enumerate((36, 0))]
-        adj_raw = [reused([P, 4, G], F32, f"adj_raw{g}", kib) for g, kib in enumerate((32, 16, 28, 32))]
+        adj_raw = [reused([P, 4, G], F32, f"adj_raw{g}", kib) for g, kib in enumerate((32, 16, 28, 24))]
         w8 = reused([P, 2, N], U32, "w8", 20)
-        step = reused([P, S], F32, "step", 24)
+        step = reused([P, S], F32, "step", 36)
         base = reused([P, 4, S], F32, "base", 0)
 
         def load_w2(a):
@@ -114,8 +114,6 @@ def tile_list_delay_sensitivity_rows_kernel(
 
         ident = held([P, P], F32, "ident")
         make_identity(nc, ident[:])
-        warm = held([P, 1], F32, "warm")
-        nc.scalar.activation(warm[:], ident[:, 0:1], ACT.Tanh)
 
         w2_q = [held([P, 512], U32, f"w2_q{a}") for a in range(2)]
         w2_sc = [held([P, 512], U8, f"w2_sc{a}") for a in range(2)]
@@ -123,7 +121,7 @@ def tile_list_delay_sensitivity_rows_kernel(
         adj_sc = [held([P, G], U8, f"adj_sc{g}") for g in range(4)]
         h_q = [[held([P, G], U32, f"h_q{g}_{a}") for a in range(2)] for g in range(4)]
         h_sc = [[held([P, G], U8, f"h_sc{g}_{a}") for a in range(2)] for g in range(4)]
-        page = [held([P, S], F32, f"page{c}") for c in range(3)]
+        page = [held([P, S], F32, "page0")]
 
         def quantise_w2(a):
             if a == 0:
@@ -139,6 +137,8 @@ def tile_list_delay_sensitivity_rows_kernel(
         def quantise_adj(g, on_scalar):
             if g == 0:
                 rounded = reused([P, 4 * G], BF16, "adj_bf0", 28)
+            elif g == 2:
+                rounded = reused([P, 4 * G], BF16, "adj_bf2", 55)
             else:
                 rounded = held([P, 4 * G], BF16, f"adj_bf{g}")
             dst = rounded[:].rearrange("p (c e i) -> p c i e", e=4, i=4)
@@ -276,20 +276,21 @@ def tile_list_delay_sensitivity_rows_kernel(
         sq0 = [squares(0, a) for a in range(2)]
         quantise_adj(0, False)
         load_adj(2)
-        load_adj(3)
         quantise_w2(0)
         nc.sync.dma_start(out=step[:], in_=wgo)
+        load_adj(3)
         quantise_w2(1)
         nc.sync.dma_start(out=base[:], in_=x0.rearrange("(c p) j -> p c j", p=P))
+        quantise_adj(1, True)
         sq1 = [squares(1, a) for a in range(2)]
         hidden_group(0, sq0)
-        quantise_adj(1, False)
         y0 = [product([(0, 0), (1, 0)]), product([(2, 0), (3, 0)])]
         hidden_group(1, sq1)
-        quantise_adj(2, False)
-        quantise_adj(3, True)
+        quantise_adj(2, True)
+        page.extend(reused([P, S], F32, f"page{c}", 48 + 4 * c) for c in (1, 2))
         sq2 = [squares(2, a) for a in range(2)]
         scatter_group(0, y0)
+        quantise_adj(3, True)
         y1 = product([(0, 1), (1, 1)], kib=48)
         hidden_group(2, sq2)
         sq3 = [squares(3, a) for a in range(2)]

@@ -38,25 +38,27 @@ def tile_list_delay_sensitivity_rows_kernel(
         idx = keep.tile([P, S // 16], U16, name="idx")
         idx2 = keep.tile([P, S // 16], U16, name="idx2")
 
-        ROW = S + H + N
-        tab_sc = held([P, T], U8, "tab_sc")
-        w4_sc_raw = held([P, H], U8, "w4_sc_raw")
-        staged = held([P, ROW], U8, "staged")
-        planes = held([P, 2 * ROW], U8, "planes")
-        nc.sync.dma_start(idx[:], offs)
-        nc.sync.dma_start(out=tab_sc[0:32, :].bitcast(I32), in_=tab_scales.bitcast(I32).rearrange("a q t -> q a t"))
-        nc.sync.dma_start(out=w4_sc_raw[0:32, :].bitcast(I32), in_=w4_scales.bitcast(I32).rearrange("a q t -> q a t"))
-        nc.sync.dma_start(
-            out=staged[0:32, S + H : ROW].bitcast(I32), in_=w8_scales.bitcast(I32).rearrange("a q t -> q a t")
-        )
-        nc.sync.dma_start(idx2[:], offs2)
-        for tile in (tab_sc, w4_sc_raw):
-            nc.vector.memset(tile[32:64, :].bitcast(I32), 0)
-            nc.vector.memset(tile[64:P, :].bitcast(I32), 0)
-        nc.vector.memset(planes[:].bitcast(I32), 0)
-
         def reused(shape, dtype, name, kib):
             return turns.tile(shape, dtype, name=name, offset=1024 * kib, align_bytes=64)
+
+        HALF = S // 2
+        rows = (HALF + H, HALF + N)
+        tab_sc = held([P, T], U8, "tab_sc")
+        w4_sc_raw = held([P, H], U8, "w4_sc_raw")
+        staged = [held([P, rows[e]], U8, f"staged{e}") for e in range(2)]
+        planes = [held([P, 2 * rows[e]], U8, f"planes{e}") for e in range(2)]
+        nc.sync.dma_start(idx[:], offs)
+        nc.sync.dma_start(out=w4_sc_raw[0:32, :].bitcast(I32), in_=w4_scales.bitcast(I32).rearrange("a q t -> q a t"))
+        nc.sync.dma_start(out=tab_sc[0:32, :].bitcast(I32), in_=tab_scales.bitcast(I32).rearrange("a q t -> q a t"))
+        nc.sync.dma_start(
+            out=staged[1][0:32, HALF:].bitcast(I32), in_=w8_scales.bitcast(I32).rearrange("a q t -> q a t")
+        )
+        nc.sync.dma_start(idx2[:], offs2)
+        for tile in (w4_sc_raw, tab_sc):
+            nc.vector.memset(tile[32:64, :].bitcast(I32), 0)
+            nc.vector.memset(tile[64:P, :].bitcast(I32), 0)
+        for e in range(2):
+            nc.vector.memset(planes[e][:].bitcast(I32), 0)
 
         w4_raw = reused([P, 2, 2 * H], U8, "w4_raw", 34)
         nc.sync.dma_start(out=w4_raw[:].bitcast(I32), in_=w4_words.bitcast(I32).rearrange("a p c -> p a c"))
@@ -66,18 +68,21 @@ def tile_list_delay_sensitivity_rows_kernel(
                 out=tab[a][:].bitcast(I32), in_=tab_words[a].rearrange("p t i -> p (t i)").bitcast(I32)
             )
 
-        picked_sc = held([P, S], U8, "picked_sc")
-        nc.vector.tensor_copy(picked_sc[:], tab_sc[:].indirect(idx[:]))
+        def carry_scales(e, kib, queue):
+            picked_sc = reused([P, HALF], U8, f"picked_sc{e}", kib)
+            nc.vector.tensor_copy(picked_sc[:], tab_sc[:].indirect(idx[:, 32 * e : 32 * (e + 1)]))
+            nc.vector.tensor_copy(staged[e][0:32, 0:HALF].bitcast(I32), picked_sc[0:32, :].bitcast(I32))
+            for q in range(4):
+                queue.dma_start(
+                    out=planes[e][32 * q : 32 * q + 4, :].bitcast(I32).rearrange("r (a c) -> r a c", a=2),
+                    in_=staged[e][8 * q : 8 * q + 8, :].bitcast(I32),
+                )
+
         nc.vector.tensor_copy(
-            staged[:, S : S + H].rearrange("p (b t u m) -> p b u t m", b=2, t=4, m=16),
+            staged[0][:, HALF:].rearrange("p (b t u m) -> p b u t m", b=2, t=4, m=16),
             w4_sc_raw[:].rearrange("p (b u m t) -> p b u t m", b=2, t=4, m=16),
         )
-        nc.vector.tensor_copy(staged[0:32, 0:S].bitcast(I32), picked_sc[0:32, :].bitcast(I32))
-        for q in range(4):
-            nc.scalar.dma_start(
-                out=planes[32 * q : 32 * q + 4, :].bitcast(I32).rearrange("r (a c) -> r a c", a=2),
-                in_=staged[8 * q : 8 * q + 8, :].bitcast(I32),
-            )
+        carry_scales(0, 60, nc.scalar)
         w4 = held([P, 4 * H], U8, "w4")
         nc.vector.tensor_copy(
             w4[:].bitcast(U16).rearrange("p (b t u m) -> p b u t m", b=4, t=4, m=8),
@@ -89,7 +94,7 @@ def tile_list_delay_sensitivity_rows_kernel(
             nc.vector.tensor_copy(v[1][:, 512 * e : 512 * (e + 1)], tab[1][:].indirect(idx[:, 32 * e : 32 * (e + 1)]))
 
         w2_raw = [reused([P, 4, 512], F32, f"w2_raw{a}", kib) for a, kib in enumerate((36, 0))]
-        adj_raw = [reused([P, 4, G], F32, f"adj_raw{g}", kib) for g, kib in enumerate((32, 16, 28, 24))]
+        adj_raw = [reused([P, 4, G], F32, f"adj_raw{g}", kib) for g, kib in enumerate((32, 8, 28, 24))]
         w8 = reused([P, 2, N], U32, "w8", 20)
         step = reused([P, S], F32, "step", 36)
         base = reused([P, 4, S], F32, "base", 0)
@@ -108,6 +113,7 @@ def tile_list_delay_sensitivity_rows_kernel(
         load_w2(0)
         load_w2(1)
         load_adj(1)
+        carry_scales(1, 12, nc.sync)
         nc.sync.dma_start(
             out=w8[:].bitcast(I32), in_=w8_words.rearrange("a p c i -> p a (c i)").bitcast(I32)
         )
@@ -153,6 +159,7 @@ def tile_list_delay_sensitivity_rows_kernel(
             state = ring.tile([P, G, 4], F32, name="state")
             for u in range(2):
                 j0 = G * g + U * u
+                e, j1 = divmod(j0, HALF)
                 bank = psum.tile([P, 4, U], F32, name="xbank", tag="x", bufs=3)
                 for k in range(2):
                     for t in range(4):
@@ -160,9 +167,9 @@ def tile_list_delay_sensitivity_rows_kernel(
                         nc.tensor.matmul_mx(
                             out=bank[:, t, :],
                             lhsT=w4[:, 2 * (H * k + c0) : 2 * (H * k + c0 + P)].bitcast(FP4X4),
-                            lhsT_scale=planes[:, ROW * k + S + c0 : ROW * k + S + c0 + P],
+                            lhsT_scale=planes[0][:, rows[0] * k + HALF + c0 : rows[0] * k + HALF + c0 + P],
                             rhs=v[k][:, j0 : j0 + U].bitcast(FP8X4),
-                            rhs_scale=planes[:, ROW * k + j0 : ROW * k + j0 + U],
+                            rhs_scale=planes[e][:, rows[e] * k + j1 : rows[e] * k + j1 + U],
                             start=(k == 0 and t == 0),
                             stop=(k == 1 and t == 3),
                         )
@@ -210,7 +217,7 @@ def tile_list_delay_sensitivity_rows_kernel(
                     nc.tensor.matmul_mx(
                         out=bank[:, e, :],
                         lhsT=w8[:, a, P * c : P * (c + 1)].bitcast(FP8X4),
-                        lhsT_scale=planes[:, ROW * a + S + H + P * c : ROW * a + S + H + P * (c + 1)],
+                        lhsT_scale=planes[1][:, rows[1] * a + HALF + P * c : rows[1] * a + HALF + P * (c + 1)],
                         rhs=h_q[g][a][:].bitcast(FP8X4),
                         rhs_scale=h_sc[g][a][:],
                         start=(a == 0),

@@ -82,7 +82,7 @@ def tile_list_delay_sensitivity_rows_kernel(
             staged[0][:, HALF:].rearrange("p (b t u m) -> p b u t m", b=2, t=4, m=16),
             w4_sc_raw[:].rearrange("p (b u m t) -> p b u t m", b=2, t=4, m=16),
         )
-        carry_scales(0, 60, nc.scalar)
+        carry_scales(0, 60, nc.sync)
         w4 = held([P, 4 * H], U8, "w4")
         nc.vector.tensor_copy(
             w4[:].bitcast(U16).rearrange("p (b t u m) -> p b u t m", b=4, t=4, m=8),

@@ -30,7 +30,7 @@ def tile_list_delay_sensitivity_rows_kernel(
         keep = ctx.enter_context(tc.tile_pool(name="keep", bufs=1))
         turns = ctx.enter_context(tc.tile_pool(name="turns", bufs=1))
         ring = ctx.enter_context(tc.tile_pool(name="ring", bufs=2))
-        psum = ctx.enter_context(tc.psum_pool(name="psum", bufs=2))
+        psum = ctx.enter_context(tc.psum_pool(name="psum", bufs=1))
 
         def held(shape, dtype, name):
             return keep.tile(shape, dtype, name=name, align_bytes=64)
@@ -40,6 +40,9 @@ def tile_list_delay_sensitivity_rows_kernel(
 
         def reused(shape, dtype, name, kib):
             return turns.tile(shape, dtype, name=name, offset=1024 * kib, align_bytes=64)
+
+        def in_bank(shape, name, bank):
+            return psum.tile(shape, F32, name=name, offset=2048 * bank)
 
         HALF = S // 2
         rows = (HALF + H, HALF + N)
@@ -82,7 +85,7 @@ def tile_list_delay_sensitivity_rows_kernel(
             staged[0][:, HALF:].rearrange("p (b t u m) -> p b u t m", b=2, t=4, m=16),
             w4_sc_raw[:].rearrange("p (b u m t) -> p b u t m", b=2, t=4, m=16),
         )
-        carry_scales(0, 60, nc.sync)
+        carry_scales(0, 64, nc.sync)
         w4 = held([P, 4 * H], U8, "w4")
         nc.vector.tensor_copy(
             w4[:].bitcast(U16).rearrange("p (b t u m) -> p b u t m", b=4, t=4, m=8),
@@ -94,9 +97,13 @@ def tile_list_delay_sensitivity_rows_kernel(
             nc.vector.tensor_copy(v[1][:, 512 * e : 512 * (e + 1)], tab[1][:].indirect(idx[:, 32 * e : 32 * (e + 1)]))
 
         w2_raw = [reused([P, 4, 512], F32, f"w2_raw{a}", kib) for a, kib in enumerate((36, 0))]
-        adj_raw = [reused([P, 4, G], F32, f"adj_raw{g}", kib) for g, kib in enumerate((32, 8, 28, 24))]
+        adj_cols = (slice(0, 256), slice(256, 640), slice(640, S))
+        adj_raw = [
+            reused([P, 4, cols.stop - cols.start], F32, f"adj_raw{g}", kib)
+            for g, (cols, kib) in enumerate(zip(adj_cols, (32, 8, 36)))
+        ]
         w8 = reused([P, 2, N], U32, "w8", 20)
-        step = reused([P, S], F32, "step", 36)
+        step = reused([P, S], F32, "step", 24)
         base = reused([P, 4, S], F32, "base", 0)
 
         def load_w2(a):
@@ -106,14 +113,14 @@ def tile_list_delay_sensitivity_rows_kernel(
 
         def load_adj(g):
             nc.sync.dma_start(
-                out=adj_raw[g][:], in_=adj[:, G * g : G * (g + 1)].rearrange("(p i) c -> p i c", i=4)
+                out=adj_raw[g][:], in_=adj[:, adj_cols[g]].rearrange("(p i) c -> p i c", i=4)
             )
 
         load_adj(0)
         load_w2(0)
         load_w2(1)
         load_adj(1)
-        carry_scales(1, 12, nc.sync)
+        carry_scales(1, 14, nc.sync)
         nc.sync.dma_start(
             out=w8[:].bitcast(I32), in_=w8_words.rearrange("a p c i -> p a (c i)").bitcast(I32)
         )
@@ -123,44 +130,48 @@ def tile_list_delay_sensitivity_rows_kernel(
 
         w2_q = [held([P, 512], U32, f"w2_q{a}") for a in range(2)]
         w2_sc = [held([P, 512], U8, f"w2_sc{a}") for a in range(2)]
-        adj_q = [held([P, G], U32, f"adj_q{g}") for g in range(4)]
-        adj_sc = [held([P, G], U8, f"adj_sc{g}") for g in range(4)]
-        h_q = [[held([P, G], U32, f"h_q{g}_{a}") for a in range(2)] for g in range(4)]
-        h_sc = [[held([P, G], U8, f"h_sc{g}_{a}") for a in range(2)] for g in range(4)]
-        page = [held([P, S], F32, "page0")]
+        adj_q = held([P, S], U32, "adj_q")
+        adj_sc = held([P, S], U8, "adj_sc")
+        h_q = [held([P, 2 * G], U32, f"h_q{g}") for g in range(4)]
+        h_sc = [held([P, 2 * G], U8, f"h_sc{g}") for g in range(4)]
+        page = {}
 
         def quantise_w2(a):
-            if a == 0:
-                rounded = reused([P, 2048], BF16, "w2_bf0", 24)
-            else:
-                rounded = held([P, 2048], BF16, "w2_bf1")
+            rounded = reused([P, 2048], BF16, f"w2_bf{a}", (24, 66)[a])
             nc.vector.tensor_copy(
                 rounded[:].rearrange("p (t m i) -> p m t i", t=4, i=4),
                 w2_raw[a][:].rearrange("p i (m t) -> p m t i", t=4),
             )
             nc.vector.quantize_mx(out=w2_q[a][:].bitcast(FP8X4), scales=w2_sc[a][:], in_=rounded[:])
 
-        def quantise_adj(g, on_scalar):
+        def round_adj(g):
+            width = adj_cols[g].stop - adj_cols[g].start
+            rounded = reused([P, 4 * width], BF16, f"adj_bf{g}", (28, 65, 67)[g])
             if g == 0:
-                rounded = reused([P, 4 * G], BF16, "adj_bf0", 28)
-            elif g == 2:
-                rounded = reused([P, 4 * G], BF16, "adj_bf2", 55)
+                nc.vector.tensor_copy(
+                    rounded[:].rearrange("p (c e i) -> p c i e", e=4, i=4),
+                    adj_raw[g][:].rearrange("p i (c e) -> p c i e", e=4),
+                )
             else:
-                rounded = held([P, 4 * G], BF16, f"adj_bf{g}")
-            dst = rounded[:].rearrange("p (c e i) -> p c i e", e=4, i=4)
-            src = adj_raw[g][:].rearrange("p i (c e) -> p c i e", e=4)
-            if on_scalar:
-                nc.scalar.copy(dst, src)
-            else:
-                nc.vector.tensor_copy(dst, src)
-            nc.vector.quantize_mx(out=adj_q[g][:].bitcast(FP8X4), scales=adj_sc[g][:], in_=rounded[:])
+                nc.gpsimd.tensor_scalar(
+                    rounded[:].rearrange("p (c i) -> p c i", i=4),
+                    adj_raw[g][:].rearrange("p i c -> p c i"),
+                    1.0,
+                    0.0,
+                    ALU.mult,
+                    ALU.add,
+                )
+            return rounded
+
+        def quantise_adj(g, rounded):
+            nc.vector.quantize_mx(out=adj_q[:, adj_cols[g]].bitcast(FP8X4), scales=adj_sc[:, adj_cols[g]], in_=rounded[:])
 
         def squares(g, a):
             state = ring.tile([P, G, 4], F32, name="state")
             for u in range(2):
                 j0 = G * g + U * u
                 e, j1 = divmod(j0, HALF)
-                bank = psum.tile([P, 4, U], F32, name="xbank", tag="x", bufs=3)
+                bank = in_bank([P, 4, U], f"x{g}{a}{u}", (4 * g + 2 * a + u) % 3)
                 for k in range(2):
                     for t in range(4):
                         c0 = 512 * a + P * t
@@ -178,72 +189,81 @@ def tile_list_delay_sensitivity_rows_kernel(
             nc.scalar.activation(sq[:], state[:], ACT.Square)
             return sq
 
-        def hidden(g, a, sqs):
-            if g == 3:
-                rounded = reused([P, G, 4], BF16, f"h_bf_last{a}", (48, 44)[a])
-            else:
-                rounded = ring.tile([P, G, 4], BF16, name="h_bf", align_bytes=64, bufs=3)
-            for u in range(2):
-                bank = psum.tile([P, 4, U], F32, name="bbank", tag="b", bufs=4)
-                for t in range(4):
-                    nc.tensor.matmul_mx(
-                        out=bank[:, t, :],
-                        lhsT=w2_q[a][:, P * t : P * (t + 1)].bitcast(FP8X4),
-                        lhsT_scale=w2_sc[a][:, P * t : P * (t + 1)],
-                        rhs=adj_q[g][:, U * u : U * (u + 1)].bitcast(FP8X4),
-                        rhs_scale=adj_sc[g][:, U * u : U * (u + 1)],
-                        start=True,
-                        stop=True,
-                    )
-                nc.vector.scalar_tensor_tensor(
-                    out=rounded[:, U * u : U * (u + 1), :],
-                    in0=sqs[:, U * u : U * (u + 1), :],
-                    scalar=1.0,
-                    in1=bank[:].rearrange("p t j -> p j t"),
-                    op0=ALU.subtract,
-                    op1=ALU.mult,
+        def adjoint(g, a, u):
+            bank = in_bank([P, 4, U], f"b{g}{a}{u}", 3 + u + 2 * a if g < 3 else ((3, 0), (4, 3))[a][u])
+            j0 = G * g + U * u
+            for t in range(4):
+                nc.tensor.matmul_mx(
+                    out=bank[:, t, :],
+                    lhsT=w2_q[a][:, P * t : P * (t + 1)].bitcast(FP8X4),
+                    lhsT_scale=w2_sc[a][:, P * t : P * (t + 1)],
+                    rhs=adj_q[:, j0 : j0 + U].bitcast(FP8X4),
+                    rhs_scale=adj_sc[:, j0 : j0 + U],
+                    start=True,
+                    stop=True,
                 )
-            return rounded
+            return bank[:].rearrange("p t j -> p j t")
 
-        def quantise_h(g, a, rounded):
-            nc.vector.quantize_mx(
-                out=h_q[g][a][:].bitcast(FP8X4), scales=h_sc[g][a][:], in_=rounded[:].rearrange("p j t -> p (j t)")
+        def hidden_on_vector(g, a, u, sq, rounded):
+            nc.vector.scalar_tensor_tensor(
+                out=rounded[:, a, U * u : U * (u + 1), :],
+                in0=sq[:, U * u : U * (u + 1), :],
+                scalar=1.0,
+                in1=adjoint(g, a, u),
+                op0=ALU.subtract,
+                op1=ALU.mult,
             )
 
-        def product(pairs, tag="y", bufs=1, kib=None):
-            bank = psum.tile([P, 2, G], F32, name="ybank", tag=tag, bufs=bufs)
+        def less_one(out, sq):
+            nc.gpsimd.tensor_scalar(out, sq, 1.0, -1.0, ALU.mult, ALU.add)
+
+        def copied_adjoint(g, a, u):
+            b = ring.tile([P, U, 4], F32, name="b", bufs=5)
+            nc.scalar.copy(b[:], adjoint(g, a, u))
+            return b
+
+        def hidden_on_gpsimd(a, u, slope, b, rounded):
+            nc.gpsimd.tensor_tensor(rounded[:, a, U * u : U * (u + 1), :], slope[:, U * u : U * (u + 1), :], b[:], ALU.mult)
+
+        def rounded_h(g):
+            return reused([P, 2, G, 4], BF16, f"h_bf{g}", (69, 46, 54, 60)[g])
+
+        def quantise_h(g, rounded):
+            nc.vector.quantize_mx(
+                out=h_q[g][:].bitcast(FP8X4), scales=h_sc[g][:], in_=rounded[:].rearrange("p a j t -> p (a j t)")
+            )
+
+        def product(pairs, at, kib=None):
+            bank = in_bank([P, 2, G], f"y{pairs[0][0]}{pairs[0][1]}", at)
             for e, (c, g) in enumerate(pairs):
                 for a in range(2):
                     nc.tensor.matmul_mx(
                         out=bank[:, e, :],
                         lhsT=w8[:, a, P * c : P * (c + 1)].bitcast(FP8X4),
                         lhsT_scale=planes[1][:, rows[1] * a + HALF + P * c : rows[1] * a + HALF + P * (c + 1)],
-                        rhs=h_q[g][a][:].bitcast(FP8X4),
-                        rhs_scale=h_sc[g][a][:],
+                        rhs=h_q[g][:, G * a : G * (a + 1)].bitcast(FP8X4),
+                        rhs_scale=h_sc[g][:, G * a : G * (a + 1)],
                         start=(a == 0),
                         stop=(a == 1),
                     )
             if kib is None:
-                y = ring.tile([P, 2 * G], F32, name="y", bufs=7)
+                y = ring.tile([P, 2 * G], F32, name="y", bufs=9)
             else:
                 y = reused([P, 2 * G], F32, f"y_at{kib}", kib)
             width = G * len(pairs)
             nc.scalar.copy(y[:, 0:width], bank[:].rearrange("p e j -> p (e j)")[:, 0:width])
             return y
 
-        def place(c, y, j0, width):
-            nc.vector.tensor_tensor(
-                page[c][:].indirect(idx2[:, j0 // 16 : (j0 + width) // 16]), y, step[:, j0 : j0 + width], ALU.mult
-            )
+        def weigh(y, j0, width):
+            nc.gpsimd.tensor_tensor(y, y, step[:, j0 : j0 + width], ALU.mult)
 
-        def scatter_group(g, ys):
-            for c in range(3):
-                place(c, ys[c // 2][:, G * (c % 2) : G * (c % 2 + 1)], G * g, G)
+        def place(c, y, j0, width):
+            nc.vector.tensor_copy(page[c][:].indirect(idx2[:, j0 // 16 : (j0 + width) // 16]), y)
 
         def open_sums(c):
             banks = []
             for e in range(2):
-                turned = psum.tile([P, 4, P], F32, name="turned", tag="b", bufs=4)
+                turned = in_bank([P, 4, P], f"turned{c}{e}", ((0, 4), (3, 7))[c // 2][e])
                 for b in range(4):
                     cols = slice(512 * e + P * b, 512 * e + P * (b + 1))
                     nc.tensor.matmul(turned[:, b, :], base[:, c, cols], ident[:], start=(b == 0), stop=False, is_transpose=True)
@@ -256,15 +276,20 @@ def tile_list_delay_sensitivity_rows_kernel(
                 for b in range(4):
                     cols = slice(512 * e + P * b, 512 * e + P * (b + 1))
                     nc.tensor.matmul(banks[e][:, b, :], page[c][:, cols], ident[:], start=False, stop=(b == 3), is_transpose=True)
-                total_t = ring.tile([P, 4, P], F32, name="total_t")
+                total_t = ring.tile([P, 4, P], F32, name="total_t", bufs=4)
                 nc.scalar.copy(total_t[:], banks[e][:])
                 sums.append(total_t)
             total = ring.tile([P, S], F32, name="total", bufs=3)
             for e in range(2):
-                back = psum.tile([P, 4, P], F32, name="back", tag="b", bufs=4)
+                back = in_bank([P, 4, P], f"back{c}{e}", ((5, 6), (1, 2))[c // 2][e])
                 for b in range(4):
                     nc.tensor.transpose(back[:, b, :], sums[e][:, b, :], ident[:])
                 nc.scalar.copy(total[:, 512 * e : 512 * (e + 1)], back[:].rearrange("p b j -> p (b j)"))
+            nc.scalar.dma_start(out=out[P * c : P * (c + 1), :], in_=total[:])
+
+        def finish_on_gpsimd(c):
+            total = reused([P, S], F32, "total_over_step", 24)
+            nc.gpsimd.tensor_tensor(total[:], base[:, c, :], page[c][:], ALU.add)
             nc.scalar.dma_start(out=out[P * c : P * (c + 1), :], in_=total[:])
 
         def finish_on_vector(c):
@@ -273,48 +298,98 @@ def tile_list_delay_sensitivity_rows_kernel(
                 nc.vector.tensor_tensor(total[:, cols], base[:, c, cols], page[c][:, cols], ALU.add)
                 nc.sync.dma_start(out=out[P * c : P * (c + 1), cols], in_=total[:, cols])
 
-        def hidden_group(g, sqs):
-            r0 = hidden(g, 0, sqs[0])
-            r1 = hidden(g, 1, sqs[1])
-            quantise_h(g, 0, r0)
-            quantise_h(g, 1, r1)
-            return r1
+        first, second = slice(0, G), slice(G, 2 * G)
 
         sq0 = [squares(0, a) for a in range(2)]
-        quantise_adj(0, False)
-        load_adj(2)
+        quantise_adj(0, round_adj(0))
         quantise_w2(0)
+        load_adj(2)
         nc.sync.dma_start(out=step[:], in_=wgo)
-        load_adj(3)
         quantise_w2(1)
+        adj1 = round_adj(1)
         nc.sync.dma_start(out=base[:], in_=x0.rearrange("(c p) j -> p c j", p=P))
-        quantise_adj(1, True)
         sq1 = [squares(1, a) for a in range(2)]
-        hidden_group(0, sq0)
-        y0 = [product([(0, 0), (1, 0)]), product([(2, 0), (3, 0)])]
-        hidden_group(1, sq1)
-        quantise_adj(2, True)
-        page.extend(reused([P, S], F32, f"page{c}", 48 + 4 * c) for c in (1, 2))
-        sq2 = [squares(2, a) for a in range(2)]
-        scatter_group(0, y0)
-        quantise_adj(3, True)
-        y1 = product([(0, 1), (1, 1)], kib=48)
-        hidden_group(2, sq2)
-        sq3 = [squares(3, a) for a in range(2)]
-        for c in range(2):
-            place(c, y1[:, G * c : G * (c + 1)], G, G)
-        hidden_group(3, sq3)
-        page.append(reused([P, S], F32, "page3", 44))
-        y1_late = product([(2, 1)], kib=48)
-        ys = [product([(c, 2), (c, 3)], "x", 3) for c in range(3)]
-        y_mid = product([(3, 1), (3, 2)], "x", 3)
-        y_end = product([(3, 3)], "x", 3)
-        place(3, y0[1][:, G : 2 * G], 0, G)
-        place(2, y1_late[:, 0:G], G, G)
-        for c in range(3):
-            banks = open_sums(c)
-            place(c, ys[c][:], 2 * G, 2 * G)
-            finish_on_tensor(c, banks)
-        place(3, y_mid[:], G, 2 * G)
-        place(3, y_end[:, 0:G], 3 * G, G)
+        h0 = rounded_h(0)
+        for a in range(2):
+            for u in range(2):
+                hidden_on_vector(0, a, u, sq0[a], h0)
+        quantise_h(0, h0)
+        quantise_adj(1, adj1)
+        adj2 = round_adj(2)
+        ya_raw = product([(0, 0), (1, 0)], 7, 73)
+        ya = ring.tile([P, 2 * G], F32, name="y", bufs=9)
+        for half in (first, second):
+            nc.gpsimd.tensor_tensor(ya[:, half], ya_raw[:, half], step[:, 0:G], ALU.mult)
+        h1 = rounded_h(1)
+        for a in range(2):
+            for u in range(2):
+                hidden_on_vector(1, a, u, sq1[a], h1)
+        quantise_h(1, h1)
+        quantise_adj(2, adj2)
+
+        page[0] = reused([P, S], F32, "page0", 44)
+        page[1] = reused([P, S], F32, "page1", 48)
+        place(0, ya[:, first], 0, G)
+        place(1, ya[:, second], 0, G)
+        yb = product([(0, 1), (1, 1)], 7)
+        weigh(yb[:, first], G, G)
+        weigh(yb[:, second], G, G)
+        h2 = rounded_h(2)
+        sq = squares(2, 0)
+        slope = reused([P, G, 4], F32, "slope2", 73)
+        less_one(slope[:], sq[:])
+        for u in range(2):
+            hidden_on_gpsimd(0, u, slope, copied_adjoint(2, 0, u), h2)
+        place(0, yb[:, first], G, G)
+        place(1, yb[:, second], G, G)
+        sq = squares(2, 1)
+        yc = product([(2, 0), (2, 1)], 7)
+        weigh(yc[:], 0, 2 * G)
+        for u in range(2):
+            hidden_on_vector(2, 1, u, sq, h2)
+        quantise_h(2, h2)
+
+        page[2] = reused([P, S], F32, "page2", 52)
+        place(2, yc[:], 0, 2 * G)
+        h3 = rounded_h(3)
+        sq = squares(3, 0)
+        slope = reused([P, G, 4], F32, "slope", 56)
+        less_one(slope[:], sq[:])
+        hidden_on_gpsimd(0, 0, slope, copied_adjoint(3, 0, 0), h3)
+        sq = squares(3, 1)
+        yd = product([(0, 2), (1, 2)], 0)
+        weigh(yd[:, first], 2 * G, G)
+        weigh(yd[:, second], 2 * G, G)
+        hidden_on_gpsimd(0, 1, slope, copied_adjoint(3, 0, 1), h3)
+        ye = product([(2, 2), (3, 0)], 0)
+        b31 = copied_adjoint(3, 1, 0)
+        weigh(ye[:, first], 2 * G, G)
+        weigh(ye[:, second], 0, G)
+        place(0, yd[:, first], 2 * G, G)
+        place(1, yd[:, second], 2 * G, G)
+        place(2, ye[:, first], 2 * G, G)
+        less_one(sq[:, 0:U, :], sq[:, 0:U, :])
+        hidden_on_gpsimd(1, 0, sq, b31, h3)
+        hidden_on_vector(3, 1, 1, sq, h3)
+        quantise_h(3, h3)
+
+        page[3] = reused([P, S], F32, "page3", 60)
+        place(3, ye[:, second], 0, G)
+        yf = product([(0, 3)], 7)
+        yg = product([(1, 3), (2, 3)], 1)
+        yi = product([(3, 3)], 2)
+        yh = product([(3, 1), (3, 2)], 7)
+        for y in (yf[:, first], yg[:, first], yg[:, second], yi[:, first]):
+            weigh(y, 3 * G, G)
+        weigh(yh[:], G, 2 * G)
+        banks = open_sums(0)
+        place(0, yf[:, first], 3 * G, G)
+        finish_on_tensor(0, banks)
+        place(1, yg[:, first], 3 * G, G)
+        finish_on_gpsimd(1)
+        banks = open_sums(2)
+        place(2, yg[:, second], 3 * G, G)
+        finish_on_tensor(2, banks)
+        place(3, yi[:, first], 3 * G, G)
+        place(3, yh[:], G, 2 * G)
         finish_on_vector(3)

@@ -104,7 +104,7 @@ def tile_list_delay_sensitivity_rows_kernel(
         ]
         w8 = reused([P, 2, N], U32, "w8", 20)
         step = reused([P, S], F32, "step", 24)
-        base = reused([P, 4, S], F32, "base", 0)
+        base = reused([P, 4, S], F32, "base", 68)
 
         def load_w2(a):
             nc.sync.dma_start(
@@ -136,17 +136,20 @@ def tile_list_delay_sensitivity_rows_kernel(
         h_sc = [held([P, 2 * G], U8, f"h_sc{g}") for g in range(4)]
         page = {}
 
-        def quantise_w2(a):
+        def round_w2(a):
             rounded = reused([P, 2048], BF16, f"w2_bf{a}", (24, 66)[a])
             nc.vector.tensor_copy(
                 rounded[:].rearrange("p (t m i) -> p m t i", t=4, i=4),
                 w2_raw[a][:].rearrange("p i (m t) -> p m t i", t=4),
             )
+            return rounded
+
+        def quantise_w2(a, rounded):
             nc.vector.quantize_mx(out=w2_q[a][:].bitcast(FP8X4), scales=w2_sc[a][:], in_=rounded[:])
 
         def round_adj(g):
             width = adj_cols[g].stop - adj_cols[g].start
-            rounded = reused([P, 4 * width], BF16, f"adj_bf{g}", (28, 65, 67)[g])
+            rounded = reused([P, 4 * width], BF16, f"adj_bf{g}", (28, 66, 6)[g])
             if g == 0:
                 nc.vector.tensor_copy(
                     rounded[:].rearrange("p (c e i) -> p c i e", e=4, i=4),
@@ -226,14 +229,14 @@ def tile_list_delay_sensitivity_rows_kernel(
             nc.gpsimd.tensor_tensor(rounded[:, a, U * u : U * (u + 1), :], slope[:, U * u : U * (u + 1), :], b[:], ALU.mult)
 
         def rounded_h(g):
-            return reused([P, 2, G, 4], BF16, f"h_bf{g}", (69, 46, 54, 60)[g])
+            return reused([P, 2, G, 4], BF16, f"h_bf{g}", (4, 46, 54, 60)[g])
 
         def quantise_h(g, rounded):
             nc.vector.quantize_mx(
                 out=h_q[g][:].bitcast(FP8X4), scales=h_sc[g][:], in_=rounded[:].rearrange("p a j t -> p (a j t)")
             )
 
-        def product(pairs, at, kib=None):
+        def product(pairs, at):
             bank = in_bank([P, 2, G], f"y{pairs[0][0]}{pairs[0][1]}", at)
             for e, (c, g) in enumerate(pairs):
                 for a in range(2):
@@ -246,19 +249,24 @@ def tile_list_delay_sensitivity_rows_kernel(
                         start=(a == 0),
                         stop=(a == 1),
                     )
-            if kib is None:
-                y = ring.tile([P, 2 * G], F32, name="y", bufs=9)
-            else:
-                y = reused([P, 2 * G], F32, f"y_at{kib}", kib)
-            width = G * len(pairs)
-            nc.scalar.copy(y[:, 0:width], bank[:].rearrange("p e j -> p (e j)")[:, 0:width])
+            return bank[:].rearrange("p e j -> p (e j)")[:, 0 : G * len(pairs)]
+
+        def staging():
+            return ring.tile([P, 2 * G], F32, name="y", bufs=9)
+
+        def copied(bank, kib=None):
+            y = staging() if kib is None else reused([P, 2 * G], F32, f"y_at{kib}", kib)
+            nc.scalar.copy(y[:, 0 : bank.shape[1]], bank)
             return y
 
-        def weigh(y, j0, width):
-            nc.gpsimd.tensor_tensor(y, y, step[:, j0 : j0 + width], ALU.mult)
+        def weigh(engine, out, y, j0):
+            engine.tensor_tensor(out, y, step[:, j0 : j0 + y.shape[1]], ALU.mult)
 
-        def place(c, y, j0, width):
-            nc.vector.tensor_copy(page[c][:].indirect(idx2[:, j0 // 16 : (j0 + width) // 16]), y)
+        def window(c, j0, width):
+            return page[c][:].indirect(idx2[:, j0 // 16 : (j0 + width) // 16])
+
+        def place(c, y, j0):
+            nc.vector.tensor_copy(window(c, j0, y.shape[1]), y)
 
         def open_sums(c):
             banks = []
@@ -302,94 +310,99 @@ def tile_list_delay_sensitivity_rows_kernel(
 
         sq0 = [squares(0, a) for a in range(2)]
         quantise_adj(0, round_adj(0))
-        quantise_w2(0)
+        quantise_w2(0, round_w2(0))
         load_adj(2)
         nc.sync.dma_start(out=step[:], in_=wgo)
-        quantise_w2(1)
-        adj1 = round_adj(1)
-        nc.sync.dma_start(out=base[:], in_=x0.rearrange("(c p) j -> p c j", p=P))
-        sq1 = [squares(1, a) for a in range(2)]
+        w2_late = round_w2(1)
         h0 = rounded_h(0)
-        for a in range(2):
-            for u in range(2):
-                hidden_on_vector(0, a, u, sq0[a], h0)
-        quantise_h(0, h0)
+        hidden_on_vector(0, 0, 0, sq0[0], h0)
+        quantise_w2(1, w2_late)
+        adj1 = round_adj(1)
+        sq1 = [squares(1, a) for a in range(2)]
+        hidden_on_vector(0, 0, 1, sq0[0], h0)
+        for u in range(2):
+            hidden_on_vector(0, 1, u, sq0[1], h0)
         quantise_adj(1, adj1)
+        quantise_h(0, h0)
+        nc.sync.dma_start(out=base[:], in_=x0.rearrange("(c p) j -> p c j", p=P))
         adj2 = round_adj(2)
-        ya_raw = product([(0, 0), (1, 0)], 7, 73)
-        ya = ring.tile([P, 2 * G], F32, name="y", bufs=9)
+        bank = product([(0, 0), (1, 0)], 7)
+        ya = staging()
         for half in (first, second):
-            nc.gpsimd.tensor_tensor(ya[:, half], ya_raw[:, half], step[:, 0:G], ALU.mult)
+            weigh(nc.vector, ya[:, half], bank[:, half], 0)
         h1 = rounded_h(1)
         for a in range(2):
             for u in range(2):
                 hidden_on_vector(1, a, u, sq1[a], h1)
-        quantise_h(1, h1)
         quantise_adj(2, adj2)
+        quantise_h(1, h1)
 
         page[0] = reused([P, S], F32, "page0", 44)
-        page[1] = reused([P, S], F32, "page1", 48)
-        place(0, ya[:, first], 0, G)
-        place(1, ya[:, second], 0, G)
-        yb = product([(0, 1), (1, 1)], 7)
-        weigh(yb[:, first], G, G)
-        weigh(yb[:, second], G, G)
-        h2 = rounded_h(2)
+        page[1] = reused([P, S], F32, "page1", 8)
+        place(0, ya[:, first], 0)
+        place(1, ya[:, second], 0)
         sq = squares(2, 0)
-        slope = reused([P, G, 4], F32, "slope2", 73)
+        slope = reused([P, G, 4], F32, "slope2", 48)
         less_one(slope[:], sq[:])
+        raw = copied(product([(0, 1), (1, 1)], 7), 54)
+        yb = staging()
+        for half in (first, second):
+            weigh(nc.gpsimd, yb[:, half], raw[:, half], G)
+        h2 = rounded_h(2)
         for u in range(2):
             hidden_on_gpsimd(0, u, slope, copied_adjoint(2, 0, u), h2)
-        place(0, yb[:, first], G, G)
-        place(1, yb[:, second], G, G)
+        place(0, yb[:, first], G)
+        place(1, yb[:, second], G)
         sq = squares(2, 1)
-        yc = product([(2, 0), (2, 1)], 7)
-        weigh(yc[:], 0, 2 * G)
+        yc = copied(product([(2, 0), (2, 1)], 7))
+        weigh(nc.gpsimd, yc[:], yc[:], 0)
         for u in range(2):
             hidden_on_vector(2, 1, u, sq, h2)
         quantise_h(2, h2)
 
         page[2] = reused([P, S], F32, "page2", 52)
-        place(2, yc[:], 0, 2 * G)
-        h3 = rounded_h(3)
+        place(2, yc[:], 0)
         sq = squares(3, 0)
-        slope = reused([P, G, 4], F32, "slope", 56)
+        slope = reused([P, G, 4], F32, "slope3", 56)
         less_one(slope[:], sq[:])
-        hidden_on_gpsimd(0, 0, slope, copied_adjoint(3, 0, 0), h3)
+        b30 = copied_adjoint(3, 0, 0)
         sq = squares(3, 1)
-        yd = product([(0, 2), (1, 2)], 0)
-        weigh(yd[:, first], 2 * G, G)
-        weigh(yd[:, second], 2 * G, G)
+        raw = copied(product([(0, 2), (1, 2)], 0), 60)
+        yd = staging()
+        for half in (first, second):
+            weigh(nc.gpsimd, yd[:, half], raw[:, half], 2 * G)
+        h3 = rounded_h(3)
+        hidden_on_gpsimd(0, 0, slope, b30, h3)
         hidden_on_gpsimd(0, 1, slope, copied_adjoint(3, 0, 1), h3)
-        ye = product([(2, 2), (3, 0)], 0)
+        ye = copied(product([(2, 2), (3, 0)], 0))
         b31 = copied_adjoint(3, 1, 0)
-        weigh(ye[:, first], 2 * G, G)
-        weigh(ye[:, second], 0, G)
-        place(0, yd[:, first], 2 * G, G)
-        place(1, yd[:, second], 2 * G, G)
-        place(2, ye[:, first], 2 * G, G)
+        weigh(nc.gpsimd, ye[:, first], ye[:, first], 2 * G)
+        place(0, yd[:, first], 2 * G)
+        place(1, yd[:, second], 2 * G)
+        place(2, ye[:, first], 2 * G)
         less_one(sq[:, 0:U, :], sq[:, 0:U, :])
         hidden_on_gpsimd(1, 0, sq, b31, h3)
         hidden_on_vector(3, 1, 1, sq, h3)
         quantise_h(3, h3)
 
         page[3] = reused([P, S], F32, "page3", 60)
-        place(3, ye[:, second], 0, G)
-        yf = product([(0, 3)], 7)
-        yg = product([(1, 3), (2, 3)], 1)
-        yi = product([(3, 3)], 2)
-        yh = product([(3, 1), (3, 2)], 7)
-        for y in (yf[:, first], yg[:, first], yg[:, second], yi[:, first]):
-            weigh(y, 3 * G, G)
-        weigh(yh[:], G, 2 * G)
+        weigh(nc.vector, window(3, 0, G), ye[:, second], 0)
+        yf = staging()
+        weigh(nc.vector, yf[:, first], product([(0, 3)], 7), 3 * G)
+        yg = copied(product([(1, 3), (2, 3)], 1))
+        yi = copied(product([(3, 3)], 2))
+        yh = copied(product([(3, 1), (3, 2)], 7))
+        for y in (yg[:, first], yg[:, second], yi[:, first]):
+            weigh(nc.gpsimd, y, y, 3 * G)
+        weigh(nc.gpsimd, yh[:], yh[:], G)
         banks = open_sums(0)
-        place(0, yf[:, first], 3 * G, G)
+        place(0, yf[:, first], 3 * G)
         finish_on_tensor(0, banks)
-        place(1, yg[:, first], 3 * G, G)
+        place(1, yg[:, first], 3 * G)
         finish_on_gpsimd(1)
         banks = open_sums(2)
-        place(2, yg[:, second], 3 * G, G)
+        place(2, yg[:, second], 3 * G)
         finish_on_tensor(2, banks)
-        place(3, yi[:, first], 3 * G, G)
-        place(3, yh[:], G, 2 * G)
+        place(3, yi[:, first], 3 * G)
+        place(3, yh[:], G)
         finish_on_vector(3)

@@ -97,14 +97,14 @@ def tile_list_delay_sensitivity_rows_kernel(
             nc.vector.tensor_copy(v[1][:, 512 * e : 512 * (e + 1)], tab[1][:].indirect(idx[:, 32 * e : 32 * (e + 1)]))
 
         w2_raw = [reused([P, 4, 512], F32, f"w2_raw{a}", kib) for a, kib in enumerate((36, 0))]
-        adj_cols = (slice(0, 256), slice(256, 640), slice(640, S))
+        adj_cols = [slice(G * g, G * (g + 1)) for g in range(4)]
         adj_raw = [
             reused([P, 4, cols.stop - cols.start], F32, f"adj_raw{g}", kib)
-            for g, (cols, kib) in enumerate(zip(adj_cols, (32, 8, 36)))
+            for g, (cols, kib) in enumerate(zip(adj_cols, (32, 8, 36, 40)))
         ]
         w8 = reused([P, 2, N], U32, "w8", 20)
         step = reused([P, S], F32, "step", 24)
-        base = reused([P, 4, S], F32, "base", 68)
+        base = reused([P, 4, S], F32, "base", 0)
 
         def load_w2(a):
             nc.sync.dma_start(
@@ -149,12 +149,13 @@ def tile_list_delay_sensitivity_rows_kernel(
 
         def round_adj(g):
             width = adj_cols[g].stop - adj_cols[g].start
-            rounded = reused([P, 4 * width], BF16, f"adj_bf{g}", (28, 66, 6)[g])
+            rounded = reused([P, 4 * width], BF16, f"adj_bf{g}", (28, 65, 70, 30)[g])
+            dst = rounded[:].rearrange("p (c e i) -> p c i e", e=4, i=4)
+            src = adj_raw[g][:].rearrange("p i (c e) -> p c i e", e=4)
             if g == 0:
-                nc.vector.tensor_copy(
-                    rounded[:].rearrange("p (c e i) -> p c i e", e=4, i=4),
-                    adj_raw[g][:].rearrange("p i (c e) -> p c i e", e=4),
-                )
+                nc.vector.tensor_copy(dst, src)
+            elif g == 3:
+                nc.scalar.copy(dst, src)
             else:
                 nc.gpsimd.tensor_scalar(
                     rounded[:].rearrange("p (c i) -> p c i", i=4),
@@ -174,7 +175,7 @@ def tile_list_delay_sensitivity_rows_kernel(
             for u in range(2):
                 j0 = G * g + U * u
                 e, j1 = divmod(j0, HALF)
-                bank = in_bank([P, 4, U], f"x{g}{a}{u}", (4 * g + 2 * a + u) % 3)
+                bank = in_bank([P, 4, U], f"x{g}{a}{u}", 3 if (g, a, u) == (3, 1, 1) else (4 * g + 2 * a + u) % 3)
                 for k in range(2):
                     for t in range(4):
                         c0 = 512 * a + P * t
@@ -193,7 +194,7 @@ def tile_list_delay_sensitivity_rows_kernel(
             return sq
 
         def adjoint(g, a, u):
-            bank = in_bank([P, 4, U], f"b{g}{a}{u}", 3 + u + 2 * a if g < 3 else ((3, 0), (4, 3))[a][u])
+            bank = in_bank([P, 4, U], f"b{g}{a}{u}", 2 if (g, a, u) == (3, 0, 0) else 3 + u + 2 * a)
             j0 = G * g + U * u
             for t in range(4):
                 nc.tensor.matmul_mx(
@@ -217,19 +218,13 @@ def tile_list_delay_sensitivity_rows_kernel(
                 op1=ALU.mult,
             )
 
-        def less_one(out, sq):
-            nc.gpsimd.tensor_scalar(out, sq, 1.0, -1.0, ALU.mult, ALU.add)
-
         def copied_adjoint(g, a, u):
             b = ring.tile([P, U, 4], F32, name="b", bufs=5)
             nc.scalar.copy(b[:], adjoint(g, a, u))
             return b
 
-        def hidden_on_gpsimd(a, u, slope, b, rounded):
-            nc.gpsimd.tensor_tensor(rounded[:, a, U * u : U * (u + 1), :], slope[:, U * u : U * (u + 1), :], b[:], ALU.mult)
-
         def rounded_h(g):
-            return reused([P, 2, G, 4], BF16, f"h_bf{g}", (4, 46, 54, 60)[g])
+            return reused([P, 2, G, 4], BF16, f"h_bf{g}", (69, 46, 54, 60)[g])
 
         def quantise_h(g, rounded):
             nc.vector.quantize_mx(
@@ -259,19 +254,14 @@ def tile_list_delay_sensitivity_rows_kernel(
             nc.scalar.copy(y[:, 0 : bank.shape[1]], bank)
             return y
 
-        def weigh(engine, out, y, j0):
-            engine.tensor_tensor(out, y, step[:, j0 : j0 + y.shape[1]], ALU.mult)
-
-        def window(c, j0, width):
-            return page[c][:].indirect(idx2[:, j0 // 16 : (j0 + width) // 16])
-
         def place(c, y, j0):
-            nc.vector.tensor_copy(window(c, j0, y.shape[1]), y)
+            j1 = j0 + y.shape[1]
+            nc.vector.tensor_tensor(page[c][:].indirect(idx2[:, j0 // 16 : j1 // 16]), y, step[:, j0:j1], ALU.mult)
 
         def open_sums(c):
             banks = []
             for e in range(2):
-                turned = in_bank([P, 4, P], f"turned{c}{e}", ((0, 4), (3, 7))[c // 2][e])
+                turned = in_bank([P, 4, P], f"turned{c}{e}", ((0, 3), (4, 7))[c % 2][e])
                 for b in range(4):
                     cols = slice(512 * e + P * b, 512 * e + P * (b + 1))
                     nc.tensor.matmul(turned[:, b, :], base[:, c, cols], ident[:], start=(b == 0), stop=False, is_transpose=True)
@@ -289,15 +279,10 @@ def tile_list_delay_sensitivity_rows_kernel(
                 sums.append(total_t)
             total = ring.tile([P, S], F32, name="total", bufs=3)
             for e in range(2):
-                back = in_bank([P, 4, P], f"back{c}{e}", ((5, 6), (1, 2))[c // 2][e])
+                back = in_bank([P, 4, P], f"back{c}{e}", ((5, 6), (1, 2))[c % 2][e])
                 for b in range(4):
                     nc.tensor.transpose(back[:, b, :], sums[e][:, b, :], ident[:])
                 nc.scalar.copy(total[:, 512 * e : 512 * (e + 1)], back[:].rearrange("p b j -> p (b j)"))
-            nc.scalar.dma_start(out=out[P * c : P * (c + 1), :], in_=total[:])
-
-        def finish_on_gpsimd(c):
-            total = reused([P, S], F32, "total_over_step", 24)
-            nc.gpsimd.tensor_tensor(total[:], base[:, c, :], page[c][:], ALU.add)
             nc.scalar.dma_start(out=out[P * c : P * (c + 1), :], in_=total[:])
 
         def finish_on_vector(c):
@@ -308,28 +293,36 @@ def tile_list_delay_sensitivity_rows_kernel(
 
         first, second = slice(0, G), slice(G, 2 * G)
 
+        def hidden_shared(g, h, early, sq_late):
+            slope, b, sq = early
+            nc.gpsimd.tensor_tensor(h[:, 0, 0:U, :], slope[:], b[:], ALU.mult)
+            hidden_on_vector(g, 0, 1, sq, h)
+            for u in range(2):
+                hidden_on_vector(g, 1, u, sq_late, h)
+
+        def for_gpsimd(g, sq):
+            slope = ring.tile([P, U, 4], F32, name="slope")
+            nc.scalar.activation(slope[:], sq[:, 0:U, :], ACT.Copy, bias=-1.0)
+            return slope, copied_adjoint(g, 0, 0), sq
+
         sq0 = [squares(0, a) for a in range(2)]
         quantise_adj(0, round_adj(0))
         quantise_w2(0, round_w2(0))
         load_adj(2)
         nc.sync.dma_start(out=step[:], in_=wgo)
-        w2_late = round_w2(1)
-        h0 = rounded_h(0)
-        hidden_on_vector(0, 0, 0, sq0[0], h0)
-        quantise_w2(1, w2_late)
+        load_adj(3)
+        quantise_w2(1, round_w2(1))
         adj1 = round_adj(1)
         sq1 = [squares(1, a) for a in range(2)]
-        hidden_on_vector(0, 0, 1, sq0[0], h0)
-        for u in range(2):
-            hidden_on_vector(0, 1, u, sq0[1], h0)
+        h0 = rounded_h(0)
+        for a in range(2):
+            for u in range(2):
+                hidden_on_vector(0, a, u, sq0[a], h0)
         quantise_adj(1, adj1)
         quantise_h(0, h0)
         nc.sync.dma_start(out=base[:], in_=x0.rearrange("(c p) j -> p c j", p=P))
         adj2 = round_adj(2)
-        bank = product([(0, 0), (1, 0)], 7)
-        ya = staging()
-        for half in (first, second):
-            weigh(nc.vector, ya[:, half], bank[:, half], 0)
+        ya = copied(product([(0, 0), (1, 0)], 7))
         h1 = rounded_h(1)
         for a in range(2):
             for u in range(2):
@@ -338,71 +331,46 @@ def tile_list_delay_sensitivity_rows_kernel(
         quantise_h(1, h1)
 
         page[0] = reused([P, S], F32, "page0", 44)
-        page[1] = reused([P, S], F32, "page1", 8)
+        page[1] = reused([P, S], F32, "page1", 48)
         place(0, ya[:, first], 0)
         place(1, ya[:, second], 0)
-        sq = squares(2, 0)
-        slope = reused([P, G, 4], F32, "slope2", 48)
-        less_one(slope[:], sq[:])
-        raw = copied(product([(0, 1), (1, 1)], 7), 54)
-        yb = staging()
-        for half in (first, second):
-            weigh(nc.gpsimd, yb[:, half], raw[:, half], G)
-        h2 = rounded_h(2)
-        for u in range(2):
-            hidden_on_gpsimd(0, u, slope, copied_adjoint(2, 0, u), h2)
+        yb = copied(product([(0, 1), (1, 1)], 7), 54)
+        early = for_gpsimd(2, squares(2, 0))
         place(0, yb[:, first], G)
         place(1, yb[:, second], G)
         sq = squares(2, 1)
         yc = copied(product([(2, 0), (2, 1)], 7))
-        weigh(nc.gpsimd, yc[:], yc[:], 0)
-        for u in range(2):
-            hidden_on_vector(2, 1, u, sq, h2)
+        adj3 = round_adj(3)
+        h2 = rounded_h(2)
+        hidden_shared(2, h2, early, sq)
+        quantise_adj(3, adj3)
         quantise_h(2, h2)
 
         page[2] = reused([P, S], F32, "page2", 52)
         place(2, yc[:], 0)
-        sq = squares(3, 0)
-        slope = reused([P, G, 4], F32, "slope3", 56)
-        less_one(slope[:], sq[:])
-        b30 = copied_adjoint(3, 0, 0)
+        sq30 = squares(3, 0)
         sq = squares(3, 1)
-        raw = copied(product([(0, 2), (1, 2)], 0), 60)
-        yd = staging()
-        for half in (first, second):
-            weigh(nc.gpsimd, yd[:, half], raw[:, half], 2 * G)
-        h3 = rounded_h(3)
-        hidden_on_gpsimd(0, 0, slope, b30, h3)
-        hidden_on_gpsimd(0, 1, slope, copied_adjoint(3, 0, 1), h3)
-        ye = copied(product([(2, 2), (3, 0)], 0))
-        b31 = copied_adjoint(3, 1, 0)
-        weigh(nc.gpsimd, ye[:, first], ye[:, first], 2 * G)
+        early = for_gpsimd(3, sq30)
+        bank = product([(0, 2), (3, 0)], 3)
+        yd = copied(bank[:, first], 60)
+        ye = copied(bank[:, second])
         place(0, yd[:, first], 2 * G)
-        place(1, yd[:, second], 2 * G)
-        place(2, ye[:, first], 2 * G)
-        less_one(sq[:, 0:U, :], sq[:, 0:U, :])
-        hidden_on_gpsimd(1, 0, sq, b31, h3)
-        hidden_on_vector(3, 1, 1, sq, h3)
+        h3 = rounded_h(3)
+        hidden_shared(3, h3, early, sq)
         quantise_h(3, h3)
 
         page[3] = reused([P, S], F32, "page3", 60)
-        weigh(nc.vector, window(3, 0, G), ye[:, second], 0)
-        yf = staging()
-        weigh(nc.vector, yf[:, first], product([(0, 3)], 7), 3 * G)
-        yg = copied(product([(1, 3), (2, 3)], 1))
-        yi = copied(product([(3, 3)], 2))
-        yh = copied(product([(3, 1), (3, 2)], 7))
-        for y in (yg[:, first], yg[:, second], yi[:, first]):
-            weigh(nc.gpsimd, y, y, 3 * G)
-        weigh(nc.gpsimd, yh[:], yh[:], G)
-        banks = open_sums(0)
-        place(0, yf[:, first], 3 * G)
-        finish_on_tensor(0, banks)
-        place(1, yg[:, first], 3 * G)
-        finish_on_gpsimd(1)
-        banks = open_sums(2)
-        place(2, yg[:, second], 3 * G)
-        finish_on_tensor(2, banks)
-        place(3, yi[:, first], 3 * G)
-        place(3, yh[:], G)
+        place(3, ye[:, first], 0)
+        rest = held([P, 3 * G], F32, "rest")
+        bank = product([(0, 3), (3, 3)], 7)
+        yf = copied(bank[:, first])
+        nc.scalar.copy(rest[:, 2 * G :], bank[:, second])
+        ys = [copied(product([(c, 2), (c, 3)], c)) for c in (1, 2)]
+        nc.scalar.copy(rest[:, 0 : 2 * G], product([(3, 1), (3, 2)], 7))
+        for c, (y, j0) in enumerate(((yf[:, first], 3 * G), (ys[0][:], 2 * G), (ys[1][:], 2 * G))):
+            banks = open_sums(c)
+            place(c, y, j0)
+            finish_on_tensor(c, banks)
+        place(3, rest[:, 0 : 2 * G], G)
+        place(3, rest[:, 2 * G :], 3 * G)
         finish_on_vector(3)

@@ -116,8 +116,8 @@ def tile_list_delay_sensitivity_rows_kernel(
                 out=adj_raw[g][:], in_=adj[:, adj_cols[g]].rearrange("(p i) c -> p i c", i=4)
             )
 
-        load_adj(0)
         load_w2(0)
+        load_adj(0)
         load_w2(1)
         load_adj(1)
         carry_scales(1, 14, nc.sync)
@@ -149,22 +149,13 @@ def tile_list_delay_sensitivity_rows_kernel(
 
         def round_adj(g):
             width = adj_cols[g].stop - adj_cols[g].start
-            rounded = reused([P, 4 * width], BF16, f"adj_bf{g}", (28, 65, 70, 30)[g])
+            rounded = reused([P, 4 * width], BF16, f"adj_bf{g}", (28, 70, 72, 30)[g])
             dst = rounded[:].rearrange("p (c e i) -> p c i e", e=4, i=4)
             src = adj_raw[g][:].rearrange("p i (c e) -> p c i e", e=4)
             if g == 0:
                 nc.vector.tensor_copy(dst, src)
-            elif g == 3:
-                nc.scalar.copy(dst, src)
             else:
-                nc.gpsimd.tensor_scalar(
-                    rounded[:].rearrange("p (c i) -> p c i", i=4),
-                    adj_raw[g][:].rearrange("p i c -> p c i"),
-                    1.0,
-                    0.0,
-                    ALU.mult,
-                    ALU.add,
-                )
+                nc.scalar.copy(dst, src)
             return rounded
 
         def quantise_adj(g, rounded):
@@ -218,13 +209,8 @@ def tile_list_delay_sensitivity_rows_kernel(
                 op1=ALU.mult,
             )
 
-        def copied_adjoint(g, a, u):
-            b = ring.tile([P, U, 4], F32, name="b", bufs=5)
-            nc.scalar.copy(b[:], adjoint(g, a, u))
-            return b
-
         def rounded_h(g):
-            return reused([P, 2, G, 4], BF16, f"h_bf{g}", (69, 46, 54, 60)[g])
+            return reused([P, 2, G, 4], BF16, f"h_bf{g}", (74, 78, 54, 60)[g])
 
         def quantise_h(g, rounded):
             nc.vector.quantize_mx(
@@ -293,74 +279,66 @@ def tile_list_delay_sensitivity_rows_kernel(
 
         first, second = slice(0, G), slice(G, 2 * G)
 
-        def hidden_shared(g, h, early, sq_late):
-            slope, b, sq = early
-            nc.gpsimd.tensor_tensor(h[:, 0, 0:U, :], slope[:], b[:], ALU.mult)
-            hidden_on_vector(g, 0, 1, sq, h)
-            for u in range(2):
-                hidden_on_vector(g, 1, u, sq_late, h)
-
-        def for_gpsimd(g, sq):
-            slope = ring.tile([P, U, 4], F32, name="slope")
-            nc.scalar.activation(slope[:], sq[:, 0:U, :], ACT.Copy, bias=-1.0)
-            return slope, copied_adjoint(g, 0, 0), sq
+        def hidden_group(g, h, sqs):
+            for a in range(2):
+                for u in range(2):
+                    hidden_on_vector(g, a, u, sqs[a], h)
 
         sq0 = [squares(0, a) for a in range(2)]
-        quantise_adj(0, round_adj(0))
         quantise_w2(0, round_w2(0))
+        quantise_adj(0, round_adj(0))
         load_adj(2)
         nc.sync.dma_start(out=step[:], in_=wgo)
         load_adj(3)
-        quantise_w2(1, round_w2(1))
+        h0 = rounded_h(0)
+        hidden_on_vector(0, 0, 0, sq0[0], h0)
+        w2_late = round_w2(1)
+        hidden_on_vector(0, 0, 1, sq0[0], h0)
+        quantise_w2(1, w2_late)
         adj1 = round_adj(1)
         sq1 = [squares(1, a) for a in range(2)]
-        h0 = rounded_h(0)
-        for a in range(2):
-            for u in range(2):
-                hidden_on_vector(0, a, u, sq0[a], h0)
         quantise_adj(1, adj1)
+        for u in range(2):
+            hidden_on_vector(0, 1, u, sq0[1], h0)
+        h1 = rounded_h(1)
+        hidden_on_vector(1, 0, 0, sq1[0], h1)
         quantise_h(0, h0)
         nc.sync.dma_start(out=base[:], in_=x0.rearrange("(c p) j -> p c j", p=P))
         adj2 = round_adj(2)
         ya = copied(product([(0, 0), (1, 0)], 7))
-        h1 = rounded_h(1)
-        for a in range(2):
-            for u in range(2):
-                hidden_on_vector(1, a, u, sq1[a], h1)
+        hidden_on_vector(1, 0, 1, sq1[0], h1)
+        for u in range(2):
+            hidden_on_vector(1, 1, u, sq1[1], h1)
         quantise_adj(2, adj2)
         quantise_h(1, h1)
 
-        page[0] = reused([P, S], F32, "page0", 44)
-        page[1] = reused([P, S], F32, "page1", 48)
+        page[0] = reused([P, S], F32, "page0", 76)
+        page[1] = reused([P, S], F32, "page1", 80)
         place(0, ya[:, first], 0)
         place(1, ya[:, second], 0)
-        yb = copied(product([(0, 1), (1, 1)], 7), 54)
-        early = for_gpsimd(2, squares(2, 0))
+        yb = copied(product([(0, 1), (1, 1)], 7))
+        sq2 = [squares(2, a) for a in range(2)]
         place(0, yb[:, first], G)
         place(1, yb[:, second], G)
-        sq = squares(2, 1)
         yc = copied(product([(2, 0), (2, 1)], 7))
         adj3 = round_adj(3)
         h2 = rounded_h(2)
-        hidden_shared(2, h2, early, sq)
+        hidden_group(2, h2, sq2)
         quantise_adj(3, adj3)
         quantise_h(2, h2)
 
         page[2] = reused([P, S], F32, "page2", 52)
         place(2, yc[:], 0)
-        sq30 = squares(3, 0)
-        sq = squares(3, 1)
-        early = for_gpsimd(3, sq30)
+        sq3 = [squares(3, a) for a in range(2)]
         bank = product([(0, 2), (3, 0)], 3)
-        yd = copied(bank[:, first], 60)
-        ye = copied(bank[:, second])
+        yd = copied(bank)
         place(0, yd[:, first], 2 * G)
         h3 = rounded_h(3)
-        hidden_shared(3, h3, early, sq)
+        hidden_group(3, h3, sq3)
         quantise_h(3, h3)
 
         page[3] = reused([P, S], F32, "page3", 60)
-        place(3, ye[:, first], 0)
+        place(3, yd[:, second], 0)
         rest = held([P, 3 * G], F32, "rest")
         bank = product([(0, 3), (3, 3)], 7)
         yf = copied(bank[:, first])

@@ -149,10 +149,10 @@ def tile_list_delay_sensitivity_rows_kernel(
 
         def round_adj(g):
             width = adj_cols[g].stop - adj_cols[g].start
-            rounded = reused([P, 4 * width], BF16, f"adj_bf{g}", (28, 70, 72, 30)[g])
+            rounded = reused([P, 4 * width], BF16, f"adj_bf{g}", (28, 70, 72, 84)[g])
             dst = rounded[:].rearrange("p (c e i) -> p c i e", e=4, i=4)
             src = adj_raw[g][:].rearrange("p i (c e) -> p c i e", e=4)
-            if g == 0:
+            if g in (0, 3):
                 nc.vector.tensor_copy(dst, src)
             else:
                 nc.scalar.copy(dst, src)
@@ -161,9 +161,10 @@ def tile_list_delay_sensitivity_rows_kernel(
         def quantise_adj(g, rounded):
             nc.vector.quantize_mx(out=adj_q[:, adj_cols[g]].bitcast(FP8X4), scales=adj_sc[:, adj_cols[g]], in_=rounded[:])
 
-        def squares(g, a):
-            state = ring.tile([P, G, 4], F32, name="state")
-            for u in range(2):
+        def states(g, a, halves=(0, 1), state=None):
+            if state is None:
+                state = ring.tile([P, G, 4], F32, name="state")
+            for u in halves:
                 j0 = G * g + U * u
                 e, j1 = divmod(j0, HALF)
                 bank = in_bank([P, 4, U], f"x{g}{a}{u}", 3 if (g, a, u) == (3, 1, 1) else (4 * g + 2 * a + u) % 3)
@@ -180,12 +181,21 @@ def tile_list_delay_sensitivity_rows_kernel(
                             stop=(k == 1 and t == 3),
                         )
                 nc.scalar.activation(state[:, U * u : U * (u + 1), :], bank[:].rearrange("p t j -> p j t"), ACT.Tanh)
-            sq = ring.tile([P, G, 4], F32, name="sq", bufs=4)
+            return state
+
+        def squared(g, a, state):
+            if (g, a) == (1, 0):
+                sq = reused([P, G, 4], F32, "sq10", 84)
+            else:
+                sq = ring.tile([P, G, 4], F32, name="sq", bufs=4)
             nc.scalar.activation(sq[:], state[:], ACT.Square)
             return sq
 
+        def squares(g, a):
+            return squared(g, a, states(g, a))
+
         def adjoint(g, a, u):
-            bank = in_bank([P, 4, U], f"b{g}{a}{u}", 2 if (g, a, u) == (3, 0, 0) else 3 + u + 2 * a)
+            bank = in_bank([P, 4, U], f"b{g}{a}{u}", 3 + u + 2 * a if g < 3 else u + 4 * a)
             j0 = G * g + U * u
             for t in range(4):
                 nc.tensor.matmul_mx(
@@ -208,6 +218,18 @@ def tile_list_delay_sensitivity_rows_kernel(
                 op0=ALU.subtract,
                 op1=ALU.mult,
             )
+
+        def less_one(out, sq):
+            nc.gpsimd.tensor_scalar(out, sq, 1.0, -1.0, ALU.mult, ALU.add)
+
+        def copied_adjoint(g, a, u):
+            b = ring.tile([P, U, 4], F32, name="b", bufs=3)
+            nc.scalar.copy(b[:], adjoint(g, a, u))
+            return b
+
+        def hidden_on_gpsimd(a, u, slope, b, rounded):
+            cols = slice(U * u, U * (u + 1))
+            nc.gpsimd.tensor_tensor(rounded[:, a, cols, :], slope[:, cols, :], b[:], ALU.mult)
 
         def rounded_h(g):
             return reused([P, 2, G, 4], BF16, f"h_bf{g}", (74, 78, 54, 60)[g])
@@ -244,6 +266,12 @@ def tile_list_delay_sensitivity_rows_kernel(
             j1 = j0 + y.shape[1]
             nc.vector.tensor_tensor(page[c][:].indirect(idx2[:, j0 // 16 : j1 // 16]), y, step[:, j0:j1], ALU.mult)
 
+        def weigh(engine, out, y, j0):
+            engine.tensor_tensor(out, y, step[:, j0 : j0 + y.shape[1]], ALU.mult)
+
+        def put(c, y, j0):
+            nc.vector.tensor_copy(page[c][:].indirect(idx2[:, j0 // 16 : (j0 + y.shape[1]) // 16]), y)
+
         def open_sums(c):
             banks = []
             for e in range(2):
@@ -279,17 +307,12 @@ def tile_list_delay_sensitivity_rows_kernel(
 
         first, second = slice(0, G), slice(G, 2 * G)
 
-        def hidden_group(g, h, sqs):
-            for a in range(2):
-                for u in range(2):
-                    hidden_on_vector(g, a, u, sqs[a], h)
-
         sq0 = [squares(0, a) for a in range(2)]
         quantise_w2(0, round_w2(0))
         quantise_adj(0, round_adj(0))
         load_adj(2)
-        nc.sync.dma_start(out=step[:], in_=wgo)
         load_adj(3)
+        nc.sync.dma_start(out=step[:], in_=wgo)
         h0 = rounded_h(0)
         hidden_on_vector(0, 0, 0, sq0[0], h0)
         w2_late = round_w2(1)
@@ -305,40 +328,65 @@ def tile_list_delay_sensitivity_rows_kernel(
         quantise_h(0, h0)
         nc.sync.dma_start(out=base[:], in_=x0.rearrange("(c p) j -> p c j", p=P))
         adj2 = round_adj(2)
-        ya = copied(product([(0, 0), (1, 0)], 7))
+        bank = product([(0, 0), (1, 0)], 7)
+        ya = copied(bank[:, first])
         hidden_on_vector(1, 0, 1, sq1[0], h1)
+        adj3 = round_adj(3)
         for u in range(2):
             hidden_on_vector(1, 1, u, sq1[1], h1)
         quantise_adj(2, adj2)
         quantise_h(1, h1)
-
-        page[0] = reused([P, S], F32, "page0", 76)
-        page[1] = reused([P, S], F32, "page1", 80)
-        place(0, ya[:, first], 0)
-        place(1, ya[:, second], 0)
-        yb = copied(product([(0, 1), (1, 1)], 7))
-        sq2 = [squares(2, a) for a in range(2)]
-        place(0, yb[:, first], G)
-        place(1, yb[:, second], G)
-        yc = copied(product([(2, 0), (2, 1)], 7))
-        adj3 = round_adj(3)
-        h2 = rounded_h(2)
-        hidden_group(2, h2, sq2)
         quantise_adj(3, adj3)
+
+        page[0] = reused([P, S], F32, "page0", 75)
+        page[1] = reused([P, S], F32, "page1", 80)
+        weighed = reused([P, G], F32, "weighed", 79)
+        weigh(nc.vector, weighed[:], bank[:, second], 0)
+        place(0, ya[:, first], 0)
+        put(1, weighed[:], 0)
+        sq20 = squares(2, 0)
+        raw = copied(product([(0, 1), (1, 1)], 0), 88)
+        yb = staging()
+        for half in (first, second):
+            weigh(nc.gpsimd, yb[:, half], raw[:, half], G)
+        slope = reused([P, U, 4], F32, "slope2", 88)
+        less_one(slope[:], sq20[:, 0:U, :])
+        h2 = rounded_h(2)
+        hidden_on_gpsimd(0, 0, slope, copied_adjoint(2, 0, 0), h2)
+        put(0, yb[:, first], G)
+        put(1, yb[:, second], G)
+        yc = copied(product([(2, 0), (2, 1)], 7))
+        sq21 = squares(2, 1)
+        weigh(nc.gpsimd, yc[:], yc[:], 0)
+        hidden_on_vector(2, 0, 1, sq20, h2)
+        for u in range(2):
+            hidden_on_vector(2, 1, u, sq21, h2)
         quantise_h(2, h2)
 
         page[2] = reused([P, S], F32, "page2", 52)
-        place(2, yc[:], 0)
-        sq3 = [squares(3, a) for a in range(2)]
-        bank = product([(0, 2), (3, 0)], 3)
-        yd = copied(bank)
-        place(0, yd[:, first], 2 * G)
+        put(2, yc[:], 0)
+        sq30 = squares(3, 0)
+        slope = reused([P, G, 4], F32, "slope3", 56)
+        less_one(slope[:], sq30[:])
+        b30 = [copied_adjoint(3, 0, 0)]
+        state = states(3, 1, (0,))
+        bank = product([(0, 2), (3, 0)], 2)
+        raw = copied(bank[:, first], 60)
+        b30.append(copied_adjoint(3, 0, 1))
+        sq31 = squared(3, 1, states(3, 1, (1,), state))
+        ye = copied(bank[:, second])
+        yd = staging()
+        weigh(nc.gpsimd, yd[:, first], raw[:, first], 2 * G)
         h3 = rounded_h(3)
-        hidden_group(3, h3, sq3)
+        for u in range(2):
+            hidden_on_gpsimd(0, u, slope, b30[u], h3)
+        put(0, yd[:, first], 2 * G)
+        for u in range(2):
+            hidden_on_vector(3, 1, u, sq31, h3)
         quantise_h(3, h3)
 
         page[3] = reused([P, S], F32, "page3", 60)
-        place(3, yd[:, second], 0)
+        place(3, ye[:, first], 0)
         rest = held([P, 3 * G], F32, "rest")
         bank = product([(0, 3), (3, 3)], 7)
         yf = copied(bank[:, first])

@@ -132,7 +132,7 @@ def tile_list_delay_sensitivity_rows_kernel(
         w2_sc = [held([P, 512], U8, f"w2_sc{a}") for a in range(2)]
         adj_q = held([P, S], U32, "adj_q")
         adj_sc = held([P, S], U8, "adj_sc")
-        h_q = [held([P, 2 * G], U32, f"h_q{g}") for g in range(4)]
+        h_q = {g: held([P, 2 * G], U32, f"h_q{g}") for g in (0, 1, 3)}
         h_sc = [held([P, 2 * G], U8, f"h_sc{g}") for g in range(4)]
         page = {}
 
@@ -152,7 +152,7 @@ def tile_list_delay_sensitivity_rows_kernel(
             rounded = reused([P, 4 * width], BF16, f"adj_bf{g}", (28, 70, 72, 84)[g])
             dst = rounded[:].rearrange("p (c e i) -> p c i e", e=4, i=4)
             src = adj_raw[g][:].rearrange("p i (c e) -> p c i e", e=4)
-            if g in (0, 3):
+            if g == 0:
                 nc.vector.tensor_copy(dst, src)
             else:
                 nc.scalar.copy(dst, src)
@@ -162,7 +162,9 @@ def tile_list_delay_sensitivity_rows_kernel(
             nc.vector.quantize_mx(out=adj_q[:, adj_cols[g]].bitcast(FP8X4), scales=adj_sc[:, adj_cols[g]], in_=rounded[:])
 
         def states(g, a, halves=(0, 1), state=None):
-            if state is None:
+            if (g, a) == (2, 1):
+                state = reused([P, G, 4], F32, "state21", 84)
+            elif state is None:
                 state = ring.tile([P, G, 4], F32, name="state")
             for u in halves:
                 j0 = G * g + U * u
@@ -184,10 +186,7 @@ def tile_list_delay_sensitivity_rows_kernel(
             return state
 
         def squared(g, a, state):
-            if (g, a) == (1, 0):
-                sq = reused([P, G, 4], F32, "sq10", 84)
-            else:
-                sq = ring.tile([P, G, 4], F32, name="sq", bufs=4)
+            sq = ring.tile([P, G, 4], F32, name="sq", bufs=4)
             nc.scalar.activation(sq[:], state[:], ACT.Square)
             return sq
 
@@ -195,7 +194,7 @@ def tile_list_delay_sensitivity_rows_kernel(
             return squared(g, a, states(g, a))
 
         def adjoint(g, a, u):
-            bank = in_bank([P, 4, U], f"b{g}{a}{u}", 3 + u + 2 * a if g < 3 else u + 4 * a)
+            bank = in_bank([P, 4, U], f"b{g}{a}{u}", 3 + u + 2 * a if g < 3 else ((0, 1), (2, 1))[a][u])
             j0 = G * g + U * u
             for t in range(4):
                 nc.tensor.matmul_mx(
@@ -331,12 +330,10 @@ def tile_list_delay_sensitivity_rows_kernel(
         bank = product([(0, 0), (1, 0)], 7)
         ya = copied(bank[:, first])
         hidden_on_vector(1, 0, 1, sq1[0], h1)
-        adj3 = round_adj(3)
         for u in range(2):
             hidden_on_vector(1, 1, u, sq1[1], h1)
         quantise_adj(2, adj2)
         quantise_h(1, h1)
-        quantise_adj(3, adj3)
 
         page[0] = reused([P, S], F32, "page0", 75)
         page[1] = reused([P, S], F32, "page1", 80)
@@ -357,10 +354,13 @@ def tile_list_delay_sensitivity_rows_kernel(
         put(1, yb[:, second], G)
         yc = copied(product([(2, 0), (2, 1)], 7))
         sq21 = squares(2, 1)
+        adj3 = round_adj(3)
         weigh(nc.gpsimd, yc[:], yc[:], 0)
         hidden_on_vector(2, 0, 1, sq20, h2)
         for u in range(2):
             hidden_on_vector(2, 1, u, sq21, h2)
+        quantise_adj(3, adj3)
+        h_q[2] = reused([P, 2 * G], U32, "h_q2", 84)
         quantise_h(2, h2)
 
         page[2] = reused([P, S], F32, "page2", 52)
@@ -370,11 +370,10 @@ def tile_list_delay_sensitivity_rows_kernel(
         less_one(slope[:], sq30[:])
         b30 = [copied_adjoint(3, 0, 0)]
         state = states(3, 1, (0,))
-        bank = product([(0, 2), (3, 0)], 2)
-        raw = copied(bank[:, first], 60)
+        raw = copied(product([(0, 2)], 2), 60)
         b30.append(copied_adjoint(3, 0, 1))
         sq31 = squared(3, 1, states(3, 1, (1,), state))
-        ye = copied(bank[:, second])
+        ye = copied(product([(3, 0)], 3))
         yd = staging()
         weigh(nc.gpsimd, yd[:, first], raw[:, first], 2 * G)
         h3 = rounded_h(3)
@@ -388,10 +387,9 @@ def tile_list_delay_sensitivity_rows_kernel(
         page[3] = reused([P, S], F32, "page3", 60)
         place(3, ye[:, first], 0)
         rest = held([P, 3 * G], F32, "rest")
-        bank = product([(0, 3), (3, 3)], 7)
-        yf = copied(bank[:, first])
-        nc.scalar.copy(rest[:, 2 * G :], bank[:, second])
+        yf = copied(product([(0, 3)], 7))
         ys = [copied(product([(c, 2), (c, 3)], c)) for c in (1, 2)]
+        nc.scalar.copy(rest[:, 2 * G :], product([(3, 3)], 7))
         nc.scalar.copy(rest[:, 0 : 2 * G], product([(3, 1), (3, 2)], 7))
         for c, (y, j0) in enumerate(((yf[:, first], 3 * G), (ys[0][:], 2 * G), (ys[1][:], 2 * G))):
             banks = open_sums(c)

@@ -130,8 +130,8 @@ def tile_list_delay_sensitivity_rows_kernel(
 
         w2_q = [held([P, 512], U32, f"w2_q{a}") for a in range(2)]
         w2_sc = [held([P, 512], U8, f"w2_sc{a}") for a in range(2)]
-        adj_q = held([P, S], U32, "adj_q")
-        adj_sc = held([P, S], U8, "adj_sc")
+        adj_q = {}
+        adj_sc = [held([P, G], U8, f"adj_sc{g}") for g in range(4)]
         h_q = {g: held([P, 2 * G], U32, f"h_q{g}") for g in (0, 1, 3)}
         h_sc = [held([P, 2 * G], U8, f"h_sc{g}") for g in range(4)]
         page = {}
@@ -149,7 +149,7 @@ def tile_list_delay_sensitivity_rows_kernel(
 
         def round_adj(g):
             width = adj_cols[g].stop - adj_cols[g].start
-            rounded = reused([P, 4 * width], BF16, f"adj_bf{g}", (28, 70, 72, 84)[g])
+            rounded = reused([P, 4 * width], BF16, f"adj_bf{g}", (28, 74, 70, 84)[g])
             dst = rounded[:].rearrange("p (c e i) -> p c i e", e=4, i=4)
             src = adj_raw[g][:].rearrange("p i (c e) -> p c i e", e=4)
             if g == 0:
@@ -159,11 +159,12 @@ def tile_list_delay_sensitivity_rows_kernel(
             return rounded
 
         def quantise_adj(g, rounded):
-            nc.vector.quantize_mx(out=adj_q[:, adj_cols[g]].bitcast(FP8X4), scales=adj_sc[:, adj_cols[g]], in_=rounded[:])
+            adj_q[g] = reused([P, G], U32, f"adj_q{g}", (92, 79)[g - 1]) if g in (1, 2) else held([P, G], U32, f"adj_q{g}")
+            nc.vector.quantize_mx(out=adj_q[g][:].bitcast(FP8X4), scales=adj_sc[g][:], in_=rounded[:])
 
         def states(g, a, halves=(0, 1), state=None):
-            if (g, a) == (2, 1):
-                state = reused([P, G, 4], F32, "state21", 84)
+            if (g, a) in ((1, 1), (2, 1)):
+                state = reused([P, G, 4], F32, f"state{g}{a}", (70, 84)[g - 1])
             elif state is None:
                 state = ring.tile([P, G, 4], F32, name="state")
             for u in halves:
@@ -186,8 +187,12 @@ def tile_list_delay_sensitivity_rows_kernel(
             return state
 
         def squared(g, a, state):
-            sq = ring.tile([P, G, 4], F32, name="sq", bufs=4)
-            nc.scalar.activation(sq[:], state[:], ACT.Square)
+            if (g, a) == (0, 1):
+                sq = reused([P, G, 4], F32, "sq01", 92)
+            else:
+                sq = ring.tile([P, G, 4], F32, name="sq", bufs=3)
+            for cols in (slice(0, U), slice(U, G)) if (g, a) == (1, 1) else (slice(0, G),):
+                nc.scalar.activation(sq[:, cols, :], state[:, cols, :], ACT.Square)
             return sq
 
         def squares(g, a):
@@ -195,14 +200,14 @@ def tile_list_delay_sensitivity_rows_kernel(
 
         def adjoint(g, a, u):
             bank = in_bank([P, 4, U], f"b{g}{a}{u}", 3 + u + 2 * a if g < 3 else ((0, 1), (2, 1))[a][u])
-            j0 = G * g + U * u
+            j0 = U * u
             for t in range(4):
                 nc.tensor.matmul_mx(
                     out=bank[:, t, :],
                     lhsT=w2_q[a][:, P * t : P * (t + 1)].bitcast(FP8X4),
                     lhsT_scale=w2_sc[a][:, P * t : P * (t + 1)],
-                    rhs=adj_q[:, j0 : j0 + U].bitcast(FP8X4),
-                    rhs_scale=adj_sc[:, j0 : j0 + U],
+                    rhs=adj_q[g][:, j0 : j0 + U].bitcast(FP8X4),
+                    rhs_scale=adj_sc[g][:, j0 : j0 + U],
                     start=True,
                     stop=True,
                 )
@@ -231,7 +236,7 @@ def tile_list_delay_sensitivity_rows_kernel(
             nc.gpsimd.tensor_tensor(rounded[:, a, cols, :], slope[:, cols, :], b[:], ALU.mult)
 
         def rounded_h(g):
-            return reused([P, 2, G, 4], BF16, f"h_bf{g}", (74, 78, 54, 60)[g])
+            return reused([P, 2, G, 4], BF16, f"h_bf{g}", (4, 78, 54, 60)[g])
 
         def quantise_h(g, rounded):
             nc.vector.quantize_mx(
@@ -310,35 +315,35 @@ def tile_list_delay_sensitivity_rows_kernel(
         quantise_w2(0, round_w2(0))
         quantise_adj(0, round_adj(0))
         load_adj(2)
-        load_adj(3)
         nc.sync.dma_start(out=step[:], in_=wgo)
+        load_adj(3)
+        w2_late = round_w2(1)
         h0 = rounded_h(0)
         hidden_on_vector(0, 0, 0, sq0[0], h0)
-        w2_late = round_w2(1)
-        hidden_on_vector(0, 0, 1, sq0[0], h0)
         quantise_w2(1, w2_late)
+        hidden_on_vector(0, 0, 1, sq0[0], h0)
+        state = states(1, 0)
         adj1 = round_adj(1)
-        sq1 = [squares(1, a) for a in range(2)]
-        quantise_adj(1, adj1)
+        sq1 = [squared(1, 0, state), squares(1, 1)]
         for u in range(2):
             hidden_on_vector(0, 1, u, sq0[1], h0)
-        h1 = rounded_h(1)
-        hidden_on_vector(1, 0, 0, sq1[0], h1)
+        quantise_adj(1, adj1)
         quantise_h(0, h0)
         nc.sync.dma_start(out=base[:], in_=x0.rearrange("(c p) j -> p c j", p=P))
         adj2 = round_adj(2)
         bank = product([(0, 0), (1, 0)], 7)
         ya = copied(bank[:, first])
-        hidden_on_vector(1, 0, 1, sq1[0], h1)
-        for u in range(2):
-            hidden_on_vector(1, 1, u, sq1[1], h1)
-        quantise_adj(2, adj2)
+        h1 = rounded_h(1)
+        for a in range(2):
+            for u in range(2):
+                hidden_on_vector(1, a, u, sq1[a], h1)
+        weighed = held([P, G], F32, "weighed")
+        weigh(nc.vector, weighed[:], bank[:, second], 0)
         quantise_h(1, h1)
+        quantise_adj(2, adj2)
 
         page[0] = reused([P, S], F32, "page0", 75)
         page[1] = reused([P, S], F32, "page1", 80)
-        weighed = reused([P, G], F32, "weighed", 79)
-        weigh(nc.vector, weighed[:], bank[:, second], 0)
         place(0, ya[:, first], 0)
         put(1, weighed[:], 0)
         sq20 = squares(2, 0)

@@ -191,9 +191,21 @@ def tile_list_delay_sensitivity_rows_kernel(
                 sq = reused([P, G, 4], F32, "sq01", 92)
             else:
                 sq = ring.tile([P, G, 4], F32, name="sq", bufs=3)
-            for cols in (slice(0, U), slice(U, G)) if (g, a) == (1, 1) else (slice(0, G),):
-                nc.scalar.activation(sq[:, cols, :], state[:, cols, :], ACT.Square)
+            nc.scalar.activation(sq[:], state[:], ACT.Square)
             return sq
+
+        def squared_in_halves(a, state):
+            halves = []
+            for u in range(2):
+                part = state[:, U * u : U * (u + 1), :]
+                if u == a:
+                    sq = reused([P, U, 4], F32, f"sq1{a}_gpsimd", (66, 6)[a])
+                    nc.gpsimd.tensor_tensor(sq[:], part, part, ALU.mult)
+                else:
+                    sq = held([P, U, 4], F32, f"sq1{a}_scalar")
+                    nc.scalar.activation(sq[:], part, ACT.Square)
+                halves.append(sq)
+            return halves
 
         def squares(g, a):
             return squared(g, a, states(g, a))
@@ -216,7 +228,7 @@ def tile_list_delay_sensitivity_rows_kernel(
         def hidden_on_vector(g, a, u, sq, rounded):
             nc.vector.scalar_tensor_tensor(
                 out=rounded[:, a, U * u : U * (u + 1), :],
-                in0=sq[:, U * u : U * (u + 1), :],
+                in0=sq[u][:] if g == 1 else sq[:, U * u : U * (u + 1), :],
                 scalar=1.0,
                 in1=adjoint(g, a, u),
                 op0=ALU.subtract,
@@ -324,12 +336,13 @@ def tile_list_delay_sensitivity_rows_kernel(
         hidden_on_vector(0, 0, 1, sq0[0], h0)
         state = states(1, 0)
         adj1 = round_adj(1)
-        sq1 = [squared(1, 0, state), squares(1, 1)]
+        sq1 = [squared_in_halves(0, state)]
+        state = states(1, 1)
         for u in range(2):
             hidden_on_vector(0, 1, u, sq0[1], h0)
         quantise_adj(1, adj1)
         quantise_h(0, h0)
-        nc.sync.dma_start(out=base[:], in_=x0.rearrange("(c p) j -> p c j", p=P))
+        sq1.append(squared_in_halves(1, state))
         adj2 = round_adj(2)
         bank = product([(0, 0), (1, 0)], 7)
         ya = copied(bank[:, first])
@@ -341,6 +354,7 @@ def tile_list_delay_sensitivity_rows_kernel(
         weigh(nc.vector, weighed[:], bank[:, second], 0)
         quantise_h(1, h1)
         quantise_adj(2, adj2)
+        nc.sync.dma_start(out=base[:], in_=x0.rearrange("(c p) j -> p c j", p=P))
 
         page[0] = reused([P, S], F32, "page0", 75)
         page[1] = reused([P, S], F32, "page1", 80)

@@ -20,6 +20,25 @@ ACT = mybir.ActivationFunctionType
 P = 128
 G = 256
 U = 128
+HALF = S // 2
+SHARE = 80
+
+AT = {
+    "tab0": 0, "tab1": 16,
+    "w2_late0": 0, "w2_late1": 6, "picked1": 11, "adj2": 11.25,
+    "w8": 16, "step": 20, "adj3": 24, "base": 31,
+    "w4_0": 136, "picked0": 137.75, "w4_raw1": 138, "w4_1": 144, "w2_early": 47, "w4_raw0": 54, "adj01": 55,
+    "state00": 64, "state10": 68, "state01": 72, "state110": 76, "state111": 8,
+    "w2_bf1": 68, "sq00": 80, "sq10": 84, "sq010": 88, "sq011": 5, "sq110": 90, "sq111": 92,
+    "w2_bf0": 96, "adj_bf0": 100, "adj_bf1": 102, "h_a0": 104, "h01": 108, "h11": 110,
+    "adj_bf2": 104, "ya": 93, "page0": 148, "page1": 140,
+    "state20": 64, "state21": 72, "sq20": 80, "sq210": 84, "sq211": 120, "slope20": 110.5, "slope210": 86,
+    "b20": 48, "b210": 28, "h2": 96, "yb": 52, "yb_w": 54, "y20": 56, "y21": 57, "yc_w": 108.5, "adj_bf3": 100, "page2": 25,
+    "state30": 64, "state31": 132, "sq30": 80, "sq310": 84, "sq311": 128, "slope30": 152, "slope310": 86,
+    "b30": 48, "b310": 124, "h3": 112, "yd": 0, "yd_w": 1, "ye": 60, "ye_w": 62, "yf": 58, "yf_w": 99, "page3": 125,
+    "yg": 52, "yg_w": 53, "yh": 54, "yh_w": 56, "yi": 116, "yi_w": 120, "total0": 114, "total2": 148, "total3": 25,
+    "h_a0_sc": 7, "adj2_sc": 90, "adj3_sc": 29.5,
+}
 
 
 def tile_list_delay_sensitivity_rows_kernel(
@@ -35,16 +54,14 @@ def tile_list_delay_sensitivity_rows_kernel(
         def held(shape, dtype, name):
             return keep.tile(shape, dtype, name=name, align_bytes=64)
 
-        idx = keep.tile([P, S // 16], U16, name="idx")
-        idx2 = keep.tile([P, S // 16], U16, name="idx2")
-
-        def reused(shape, dtype, name, kib):
-            return turns.tile(shape, dtype, name=name, offset=1024 * kib, align_bytes=64)
+        def placed(shape, dtype, name):
+            return turns.tile(shape, dtype, name=name, offset=int(1024 * AT[name]), align_bytes=64)
 
         def in_bank(shape, name, bank):
             return psum.tile(shape, F32, name=name, offset=2048 * bank)
 
-        HALF = S // 2
+        idx = keep.tile([P, S // 16], U16, name="idx")
+        idx2 = keep.tile([P, S // 16], U16, name="idx2")
         rows = (HALF + H, HALF + N)
         tab_sc = held([P, T], U8, "tab_sc")
         w4_sc_raw = held([P, H], U8, "w4_sc_raw")
@@ -63,357 +80,379 @@ def tile_list_delay_sensitivity_rows_kernel(
         for e in range(2):
             nc.vector.memset(planes[e][:].bitcast(I32), 0)
 
-        w4_raw = reused([P, 2, 2 * H], U8, "w4_raw", 34)
-        nc.sync.dma_start(out=w4_raw[:].bitcast(I32), in_=w4_words.bitcast(I32).rearrange("a p c -> p a c"))
-        tab = [reused([P, T], U32, f"tab{a}", 16 * a) for a in range(2)]
+        def load_w4(a):
+            raw = placed([P, 2, H], U8, f"w4_raw{a}")
+            nc.sync.dma_start(
+                out=raw[:].bitcast(I32),
+                in_=w4_words[:, :, H * a : H * (a + 1)].bitcast(I32).rearrange("k p c -> p k c"),
+            )
+            return raw
+
+        def load_rows(name, src, cols):
+            raw = placed([P, 4, cols.stop - cols.start], F32, name)
+            nc.sync.dma_start(out=raw[:], in_=src[:, cols].rearrange("(p i) c -> p i c", i=4))
+            return raw
+
+        w4_raw = load_w4(0)
+        tab = [placed([P, T], U32, f"tab{a}") for a in range(2)]
         for a in range(2):
             nc.sync.dma_start(
                 out=tab[a][:].bitcast(I32), in_=tab_words[a].rearrange("p t i -> p (t i)").bitcast(I32)
             )
 
-        def carry_scales(e, kib, queue):
-            picked_sc = reused([P, HALF], U8, f"picked_sc{e}", kib)
-            nc.vector.tensor_copy(picked_sc[:], tab_sc[:].indirect(idx[:, 32 * e : 32 * (e + 1)]))
-            nc.vector.tensor_copy(staged[e][0:32, 0:HALF].bitcast(I32), picked_sc[0:32, :].bitcast(I32))
+        def pick_scales(e):
+            picked = placed([P, HALF], U8, f"picked{e}")
+            nc.vector.tensor_copy(picked[:], tab_sc[:].indirect(idx[:, 32 * e : 32 * (e + 1)]))
+            return picked
+
+        def stage(e, picked):
+            nc.vector.tensor_copy(staged[e][0:32, 0 : picked.shape[1]].bitcast(I32), picked.bitcast(I32))
+
+        def carry(e):
             for q in range(4):
-                queue.dma_start(
+                nc.sync.dma_start(
                     out=planes[e][32 * q : 32 * q + 4, :].bitcast(I32).rearrange("r (a c) -> r a c", a=2),
                     in_=staged[e][8 * q : 8 * q + 8, :].bitcast(I32),
                 )
 
+        def order_w4(a, raw):
+            words = placed([P, 2 * H], U8, f"w4_{a}")
+            nc.vector.tensor_copy(
+                words[:].bitcast(U16).rearrange("p (k t u m) -> p k u t m", k=2, t=4, m=8),
+                raw[:].rearrange("p k c -> p (k c)").bitcast(U16).rearrange("p (k u m t) -> p k u t m", k=2, t=4, m=8),
+            )
+            return words
+
         nc.vector.tensor_copy(
-            staged[0][:, HALF:].rearrange("p (b t u m) -> p b u t m", b=2, t=4, m=16),
-            w4_sc_raw[:].rearrange("p (b u m t) -> p b u t m", b=2, t=4, m=16),
+            staged[0][:, HALF:].rearrange("p (a t u m) -> p a u t m", a=2, t=4, m=16),
+            w4_sc_raw[:].rearrange("p (a u m t) -> p a u t m", a=2, t=4, m=16),
         )
-        carry_scales(0, 64, nc.sync)
-        w4 = held([P, 4 * H], U8, "w4")
-        nc.vector.tensor_copy(
-            w4[:].bitcast(U16).rearrange("p (b t u m) -> p b u t m", b=4, t=4, m=8),
-            w4_raw[:].rearrange("p a c -> p (a c)").bitcast(U16).rearrange("p (b u m t) -> p b u t m", b=4, t=4, m=8),
-        )
+        stage(0, pick_scales(0)[0:32, :])
+        w4 = [order_w4(0, w4_raw)]
+        carry(0)
+        w4_raw = load_w4(1)
+        w2_early = load_rows("w2_early", w2, slice(0, 512))
+        adj01 = load_rows("adj01", adj, slice(0, 2 * G))
         v = [held([P, S], U32, f"v{a}") for a in range(2)]
         nc.vector.tensor_copy(v[0][:], tab[0][:].indirect(idx[:]))
-        for e in range(2):
-            nc.vector.tensor_copy(v[1][:, 512 * e : 512 * (e + 1)], tab[1][:].indirect(idx[:, 32 * e : 32 * (e + 1)]))
-
-        w2_raw = [reused([P, 4, 512], F32, f"w2_raw{a}", kib) for a, kib in enumerate((36, 0))]
-        adj_cols = [slice(G * g, G * (g + 1)) for g in range(4)]
-        adj_raw = [
-            reused([P, 4, cols.stop - cols.start], F32, f"adj_raw{g}", kib)
-            for g, (cols, kib) in enumerate(zip(adj_cols, (32, 8, 36, 40)))
-        ]
-        w8 = reused([P, 2, N], U32, "w8", 20)
-        step = reused([P, S], F32, "step", 24)
-        base = reused([P, 4, S], F32, "base", 0)
-
-        def load_w2(a):
-            nc.sync.dma_start(
-                out=w2_raw[a][:], in_=w2[:, 512 * a : 512 * (a + 1)].rearrange("(p i) c -> p i c", i=4)
-            )
-
-        def load_adj(g):
-            nc.sync.dma_start(
-                out=adj_raw[g][:], in_=adj[:, adj_cols[g]].rearrange("(p i) c -> p i c", i=4)
-            )
-
-        load_w2(0)
-        load_adj(0)
-        load_w2(1)
-        load_adj(1)
-        carry_scales(1, 14, nc.sync)
-        nc.sync.dma_start(
-            out=w8[:].bitcast(I32), in_=w8_words.rearrange("a p c i -> p a (c i)").bitcast(I32)
-        )
+        stage(1, pick_scales(1)[0:32, :])
+        cut = 512 + 4 * SHARE
+        w2_late = [load_rows("w2_late0", w2, slice(512, cut)), load_rows("w2_late1", w2, slice(cut, H))]
+        carry(1)
+        adj2 = load_rows("adj2", adj, slice(2 * G, 3 * G))
+        for cols in (slice(0, G), slice(G, S)):
+            nc.vector.tensor_copy(v[1][:, cols], tab[1][:].indirect(idx[:, cols.start // 16 : cols.stop // 16]))
+        w4.append(order_w4(1, w4_raw))
+        w8 = placed([P, 2, N], U32, "w8")
+        nc.sync.dma_start(out=w8[:].bitcast(I32), in_=w8_words.rearrange("a p c i -> p a (c i)").bitcast(I32))
+        step = placed([P, S], F32, "step")
+        nc.sync.dma_start(out=step[:], in_=wgo)
+        adj3 = load_rows("adj3", adj, slice(3 * G, S))
+        base = placed([P, 4, S], F32, "base")
+        nc.sync.dma_start(out=base[:], in_=x0.rearrange("(c p) j -> p c j", p=P))
 
         ident = held([P, P], F32, "ident")
         make_identity(nc, ident[:])
 
         w2_q = [held([P, 512], U32, f"w2_q{a}") for a in range(2)]
         w2_sc = [held([P, 512], U8, f"w2_sc{a}") for a in range(2)]
-        adj_q = {}
-        adj_sc = [held([P, G], U8, f"adj_sc{g}") for g in range(4)]
-        h_q = {g: held([P, 2 * G], U32, f"h_q{g}") for g in (0, 1, 3)}
-        h_sc = [held([P, 2 * G], U8, f"h_sc{g}") for g in range(4)]
-        page = {}
+        adj_q, adj_sc, h_q, h_sc, page = {}, {}, {}, {}, {}
 
-        def round_w2(a):
-            rounded = reused([P, 2048], BF16, f"w2_bf{a}", (24, 66)[a])
-            nc.vector.tensor_copy(
-                rounded[:].rearrange("p (t m i) -> p m t i", t=4, i=4),
-                w2_raw[a][:].rearrange("p i (m t) -> p m t i", t=4),
+        def dealt(rounded):
+            return rounded[:].rearrange("p (t m i) -> p m t i", t=4, i=4)
+
+        def by_channel(raw):
+            return raw[:].rearrange("p i (m t) -> p m t i", t=4)
+
+        def quantise(name, rounded):
+            width = rounded.shape[1] // 4
+            words = held([P, width], U32, name + "_q")
+            scales = (placed if name + "_sc" in AT else held)([P, width], U8, name + "_sc")
+            nc.vector.quantize_mx(out=words[:].bitcast(FP8X4), scales=scales[:], in_=rounded)
+            return words, scales
+
+        def quantise_w2(a, rounded, cols):
+            nc.vector.quantize_mx(
+                out=w2_q[a][:, cols].bitcast(FP8X4), scales=w2_sc[a][:, cols], in_=rounded[:, 4 * cols.start : 4 * cols.stop]
             )
-            return rounded
 
-        def quantise_w2(a, rounded):
-            nc.vector.quantize_mx(out=w2_q[a][:].bitcast(FP8X4), scales=w2_sc[a][:], in_=rounded[:])
-
-        def round_adj(g):
-            width = adj_cols[g].stop - adj_cols[g].start
-            rounded = reused([P, 4 * width], BF16, f"adj_bf{g}", (28, 74, 70, 84)[g])
-            dst = rounded[:].rearrange("p (c e i) -> p c i e", e=4, i=4)
-            src = adj_raw[g][:].rearrange("p i (c e) -> p c i e", e=4)
-            if g == 0:
-                nc.vector.tensor_copy(dst, src)
-            else:
-                nc.scalar.copy(dst, src)
+        def round_adj(g, raw, copy):
+            rounded = placed([P, 4 * G], BF16, f"adj_bf{g}")
+            copy(rounded[:].rearrange("p (c e i) -> p c i e", e=4, i=4), raw.rearrange("p i (c e) -> p c i e", e=4))
             return rounded
 
         def quantise_adj(g, rounded):
-            adj_q[g] = reused([P, G], U32, f"adj_q{g}", (92, 79)[g - 1]) if g in (1, 2) else held([P, G], U32, f"adj_q{g}")
-            nc.vector.quantize_mx(out=adj_q[g][:].bitcast(FP8X4), scales=adj_sc[g][:], in_=rounded[:])
+            adj_q[g], adj_sc[g] = quantise(f"adj{g}", rounded[:])
 
-        def states(g, a, halves=(0, 1), state=None):
-            if (g, a) in ((1, 1), (2, 1)):
-                state = reused([P, G, 4], F32, f"state{g}{a}", (70, 84)[g - 1])
-            elif state is None:
-                state = ring.tile([P, G, 4], F32, name="state")
-            for u in halves:
-                j0 = G * g + U * u
-                e, j1 = divmod(j0, HALF)
-                bank = in_bank([P, 4, U], f"x{g}{a}{u}", 3 if (g, a, u) == (3, 1, 1) else (4 * g + 2 * a + u) % 3)
-                for k in range(2):
-                    for t in range(4):
-                        c0 = 512 * a + P * t
-                        nc.tensor.matmul_mx(
-                            out=bank[:, t, :],
-                            lhsT=w4[:, 2 * (H * k + c0) : 2 * (H * k + c0 + P)].bitcast(FP4X4),
-                            lhsT_scale=planes[0][:, rows[0] * k + HALF + c0 : rows[0] * k + HALF + c0 + P],
-                            rhs=v[k][:, j0 : j0 + U].bitcast(FP8X4),
-                            rhs_scale=planes[e][:, rows[e] * k + j1 : rows[e] * k + j1 + U],
-                            start=(k == 0 and t == 0),
-                            stop=(k == 1 and t == 3),
-                        )
-                nc.scalar.activation(state[:, U * u : U * (u + 1), :], bank[:].rearrange("p t j -> p j t"), ACT.Tanh)
-            return state
+        def quantise_h(name, rounded, parts):
+            words, scales = quantise(name, rounded)
+            for e, part in enumerate(parts):
+                h_q[part], h_sc[part] = words[:, G * e : G * (e + 1)], scales[:, G * e : G * (e + 1)]
 
-        def squared(g, a, state):
-            if (g, a) == (0, 1):
-                sq = reused([P, G, 4], F32, "sq01", 92)
-            else:
-                sq = ring.tile([P, G, 4], F32, name="sq", bufs=3)
-            nc.scalar.activation(sq[:], state[:], ACT.Square)
+        def flat(ap):
+            return ap.rearrange("p j t -> p (j t)")
+
+        def tanh(g, a, u, state, bank):
+            j0 = G * g + U * u
+            e, j1 = divmod(j0, HALF)
+            sums = in_bank([P, 4, U], f"x{g}{a}{u}", bank)
+            for k in range(2):
+                for t in range(4):
+                    c0 = rows[0] * k + HALF * (a + 1) + P * t
+                    nc.tensor.matmul_mx(
+                        out=sums[:, t, :],
+                        lhsT=w4[a][:, H * k + 2 * P * t : H * k + 2 * P * (t + 1)].bitcast(FP4X4),
+                        lhsT_scale=planes[0][:, c0 : c0 + P],
+                        rhs=v[k][:, j0 : j0 + U].bitcast(FP8X4),
+                        rhs_scale=planes[e][:, rows[e] * k + j1 : rows[e] * k + j1 + U],
+                        start=(k == 0 and t == 0),
+                        stop=(k == 1 and t == 3),
+                    )
+            nc.scalar.activation(state, sums[:].rearrange("p t j -> p j t"), ACT.Tanh)
+
+        def square(name, state):
+            sq = placed(state.shape, F32, name)
+            nc.scalar.activation(sq[:], state, ACT.Square)
             return sq
 
-        def squared_in_halves(a, state):
-            halves = []
-            for u in range(2):
-                part = state[:, U * u : U * (u + 1), :]
-                if u == a:
-                    sq = reused([P, U, 4], F32, f"sq1{a}_gpsimd", (66, 6)[a])
-                    nc.gpsimd.tensor_tensor(sq[:], part, part, ALU.mult)
-                else:
-                    sq = held([P, U, 4], F32, f"sq1{a}_scalar")
-                    nc.scalar.activation(sq[:], part, ACT.Square)
-                halves.append(sq)
-            return halves
+        def squares(name, state):
+            sq = placed([P, G, 4], F32, name)
+            for half in halves:
+                nc.scalar.activation(sq[:, half, :], state[:, half, :], ACT.Square)
+            return sq
 
-        def squares(g, a):
-            return squared(g, a, states(g, a))
+        def less_one(name, sq):
+            slope = placed(sq.shape, F32, name)
+            nc.scalar.activation(slope[:], sq[:], ACT.Copy, bias=-1.0)
+            return slope
 
-        def adjoint(g, a, u):
-            bank = in_bank([P, 4, U], f"b{g}{a}{u}", 3 + u + 2 * a if g < 3 else ((0, 1), (2, 1))[a][u])
-            j0 = U * u
+        def adjoint(g, a, u, bank):
+            sums = in_bank([P, 4, U], f"b{g}{a}{u}", bank)
             for t in range(4):
                 nc.tensor.matmul_mx(
-                    out=bank[:, t, :],
+                    out=sums[:, t, :],
                     lhsT=w2_q[a][:, P * t : P * (t + 1)].bitcast(FP8X4),
                     lhsT_scale=w2_sc[a][:, P * t : P * (t + 1)],
-                    rhs=adj_q[g][:, j0 : j0 + U].bitcast(FP8X4),
-                    rhs_scale=adj_sc[g][:, j0 : j0 + U],
+                    rhs=adj_q[g][:, U * u : U * (u + 1)].bitcast(FP8X4),
+                    rhs_scale=adj_sc[g][:, U * u : U * (u + 1)],
                     start=True,
                     stop=True,
                 )
-            return bank[:].rearrange("p t j -> p j t")
+            return sums[:].rearrange("p t j -> p j t")
 
-        def hidden_on_vector(g, a, u, sq, rounded):
-            nc.vector.scalar_tensor_tensor(
-                out=rounded[:, a, U * u : U * (u + 1), :],
-                in0=sq[u][:] if g == 1 else sq[:, U * u : U * (u + 1), :],
-                scalar=1.0,
-                in1=adjoint(g, a, u),
-                op0=ALU.subtract,
-                op1=ALU.mult,
-            )
+        def hidden(rounded, sq, b):
+            nc.vector.scalar_tensor_tensor(out=rounded, in0=sq, scalar=1.0, in1=b, op0=ALU.subtract, op1=ALU.mult)
 
-        def less_one(out, sq):
-            nc.gpsimd.tensor_scalar(out, sq, 1.0, -1.0, ALU.mult, ALU.add)
-
-        def copied_adjoint(g, a, u):
-            b = ring.tile([P, U, 4], F32, name="b", bufs=3)
-            nc.scalar.copy(b[:], adjoint(g, a, u))
-            return b
-
-        def hidden_on_gpsimd(a, u, slope, b, rounded):
-            cols = slice(U * u, U * (u + 1))
-            nc.gpsimd.tensor_tensor(rounded[:, a, cols, :], slope[:, cols, :], b[:], ALU.mult)
-
-        def rounded_h(g):
-            return reused([P, 2, G, 4], BF16, f"h_bf{g}", (4, 78, 54, 60)[g])
-
-        def quantise_h(g, rounded):
-            nc.vector.quantize_mx(
-                out=h_q[g][:].bitcast(FP8X4), scales=h_sc[g][:], in_=rounded[:].rearrange("p a j t -> p (a j t)")
-            )
-
-        def product(pairs, at):
-            bank = in_bank([P, 2, G], f"y{pairs[0][0]}{pairs[0][1]}", at)
+        def product(pairs, bank):
+            sums = in_bank([P, 2, G], f"y{pairs[0][0]}{pairs[0][1]}", bank)
             for e, (c, g) in enumerate(pairs):
                 for a in range(2):
                     nc.tensor.matmul_mx(
-                        out=bank[:, e, :],
+                        out=sums[:, e, :],
                         lhsT=w8[:, a, P * c : P * (c + 1)].bitcast(FP8X4),
                         lhsT_scale=planes[1][:, rows[1] * a + HALF + P * c : rows[1] * a + HALF + P * (c + 1)],
-                        rhs=h_q[g][:, G * a : G * (a + 1)].bitcast(FP8X4),
-                        rhs_scale=h_sc[g][:, G * a : G * (a + 1)],
+                        rhs=h_q[g, a].bitcast(FP8X4),
+                        rhs_scale=h_sc[g, a],
                         start=(a == 0),
                         stop=(a == 1),
                     )
-            return bank[:].rearrange("p e j -> p (e j)")[:, 0 : G * len(pairs)]
+            return sums[:].rearrange("p e j -> p (e j)")[:, 0 : G * len(pairs)]
 
-        def staging():
-            return ring.tile([P, 2 * G], F32, name="y", bufs=9)
-
-        def copied(bank, kib=None):
-            y = staging() if kib is None else reused([P, 2 * G], F32, f"y_at{kib}", kib)
-            nc.scalar.copy(y[:, 0 : bank.shape[1]], bank)
+        def copied(name, sums):
+            y = placed(sums.shape, F32, name)
+            nc.scalar.copy(y[:], sums)
             return y
 
-        def place(c, y, j0):
-            j1 = j0 + y.shape[1]
-            nc.vector.tensor_tensor(page[c][:].indirect(idx2[:, j0 // 16 : j1 // 16]), y, step[:, j0:j1], ALU.mult)
+        def offsets(j0, y):
+            return idx2[:, j0 // 16 : (j0 + y.shape[1]) // 16]
 
-        def weigh(engine, out, y, j0):
-            engine.tensor_tensor(out, y, step[:, j0 : j0 + y.shape[1]], ALU.mult)
+        def place(c, y, j0):
+            nc.vector.tensor_tensor(page[c][:].indirect(offsets(j0, y)), y, step[:, j0 : j0 + y.shape[1]], ALU.mult)
 
         def put(c, y, j0):
-            nc.vector.tensor_copy(page[c][:].indirect(idx2[:, j0 // 16 : (j0 + y.shape[1]) // 16]), y)
+            nc.vector.tensor_copy(page[c][:].indirect(offsets(j0, y)), y)
 
-        def open_sums(c):
-            banks = []
+        def weigh_pair(name, y, g):
+            weighed = placed([P, 2, G], F32, name)
+            nc.gpsimd.tensor_tensor(
+                weighed[:],
+                y[:].rearrange("p (e j) -> p e j", e=2),
+                step[:, G * g : G * (g + 1)].unsqueeze(1).to_broadcast([P, 2, G]),
+                ALU.mult,
+            )
+            return weighed
+
+        def weigh_run(name, y, j0):
+            weighed = placed(y.shape, F32, name)
+            nc.gpsimd.tensor_tensor(weighed[:], y[:], step[:, j0 : j0 + y.shape[1]], ALU.mult)
+            return weighed
+
+        def open_sums(c, banks):
+            turned = []
             for e in range(2):
-                turned = in_bank([P, 4, P], f"turned{c}{e}", ((0, 3), (4, 7))[c % 2][e])
+                sums = in_bank([P, 4, P], f"turned{c}{e}", banks[e])
                 for b in range(4):
                     cols = slice(512 * e + P * b, 512 * e + P * (b + 1))
-                    nc.tensor.matmul(turned[:, b, :], base[:, c, cols], ident[:], start=(b == 0), stop=False, is_transpose=True)
-                banks.append(turned)
-            return banks
+                    nc.tensor.matmul(sums[:, b, :], base[:, c, cols], ident[:], start=(b == 0), stop=False, is_transpose=True)
+                turned.append(sums)
+            return turned
 
-        def finish_on_tensor(c, banks):
+        def finish_on_tensor(c, turned, banks):
             sums = []
             for e in range(2):
                 for b in range(4):
                     cols = slice(512 * e + P * b, 512 * e + P * (b + 1))
-                    nc.tensor.matmul(banks[e][:, b, :], page[c][:, cols], ident[:], start=False, stop=(b == 3), is_transpose=True)
-                total_t = ring.tile([P, 4, P], F32, name="total_t", bufs=4)
-                nc.scalar.copy(total_t[:], banks[e][:])
+                    nc.tensor.matmul(turned[e][:, b, :], page[c][:, cols], ident[:], start=False, stop=(b == 3), is_transpose=True)
+                total_t = ring.tile([P, 4, P], F32, name="total_t", bufs=2)
+                nc.scalar.copy(total_t[:], turned[e][:])
                 sums.append(total_t)
-            total = ring.tile([P, S], F32, name="total", bufs=3)
+            total = ring.tile([P, S], F32, name="total", bufs=1)
             for e in range(2):
-                back = in_bank([P, 4, P], f"back{c}{e}", ((5, 6), (1, 2))[c % 2][e])
+                back = in_bank([P, 4, P], f"back{c}{e}", banks[e])
                 for b in range(4):
                     nc.tensor.transpose(back[:, b, :], sums[e][:, b, :], ident[:])
                 nc.scalar.copy(total[:, 512 * e : 512 * (e + 1)], back[:].rearrange("p b j -> p (b j)"))
             nc.scalar.dma_start(out=out[P * c : P * (c + 1), :], in_=total[:])
 
+        def finish_on_gpsimd(c):
+            total = placed([P, S], F32, f"total{c}")
+            for cols in (slice(0, HALF), slice(HALF, S)):
+                nc.gpsimd.tensor_tensor(total[:, cols], base[:, c, cols], page[c][:, cols], ALU.add)
+                nc.sync.dma_start(out=out[P * c : P * (c + 1), cols], in_=total[:, cols])
+
         def finish_on_vector(c):
-            total = held([P, S], F32, "last_total")
+            total = placed([P, S], F32, f"total{c}")
             for cols in (slice(0, 384), slice(384, 768), slice(768, S)):
                 nc.vector.tensor_tensor(total[:, cols], base[:, c, cols], page[c][:, cols], ALU.add)
                 nc.sync.dma_start(out=out[P * c : P * (c + 1), cols], in_=total[:, cols])
 
         first, second = slice(0, G), slice(G, 2 * G)
+        halves = (slice(0, U), slice(U, G))
 
-        sq0 = [squares(0, a) for a in range(2)]
-        quantise_w2(0, round_w2(0))
-        quantise_adj(0, round_adj(0))
-        load_adj(2)
-        nc.sync.dma_start(out=step[:], in_=wgo)
-        load_adj(3)
-        w2_late = round_w2(1)
-        h0 = rounded_h(0)
-        hidden_on_vector(0, 0, 0, sq0[0], h0)
-        quantise_w2(1, w2_late)
-        hidden_on_vector(0, 0, 1, sq0[0], h0)
-        state = states(1, 0)
-        adj1 = round_adj(1)
-        sq1 = [squared_in_halves(0, state)]
-        state = states(1, 1)
-        for u in range(2):
-            hidden_on_vector(0, 1, u, sq0[1], h0)
-        quantise_adj(1, adj1)
-        quantise_h(0, h0)
-        sq1.append(squared_in_halves(1, state))
-        adj2 = round_adj(2)
-        bank = product([(0, 0), (1, 0)], 7)
-        ya = copied(bank[:, first])
-        h1 = rounded_h(1)
-        for a in range(2):
+        state = {name: placed([P, G, 4], F32, "state" + name) for name in ("00", "10", "01")}
+        tanh(0, 0, 0, state["00"][:, halves[0], :], 0)
+        tanh(0, 0, 1, state["00"][:, halves[1], :], 1)
+        tanh(1, 0, 0, state["10"][:, halves[0], :], 2)
+        sq00 = square("sq00", state["00"][:])
+        tanh(1, 0, 1, state["10"][:, halves[1], :], 0)
+        tanh(0, 1, 0, state["01"][:, halves[0], :], 1)
+        sq10 = square("sq10", state["10"][:])
+        tanh(0, 1, 1, state["01"][:, halves[1], :], 2)
+        state110 = placed([P, U, 4], F32, "state110")
+        tanh(1, 1, 0, state110[:], 0)
+        sq010 = square("sq010", state["01"][:, halves[0], :])
+
+        w2_bf = placed([P, 2048], BF16, "w2_bf0")
+        for tiles in (slice(0, 2), slice(2, 4)):
+            nc.vector.tensor_copy(dealt(w2_bf)[:, :, tiles, :], by_channel(w2_early)[:, :, tiles, :])
+        for cols in (first, second):
+            quantise_w2(0, w2_bf, cols)
+        adj_bf = [round_adj(g, adj01[:, :, G * g : G * (g + 1)], nc.vector.tensor_copy) for g in range(2)]
+        for g in range(2):
+            quantise_adj(g, adj_bf[g])
+        h_a0 = placed([P, 2, G, 4], BF16, "h_a0")
+        for g, sq in enumerate((sq00, sq10)):
             for u in range(2):
-                hidden_on_vector(1, a, u, sq1[a], h1)
-        weighed = held([P, G], F32, "weighed")
-        weigh(nc.vector, weighed[:], bank[:, second], 0)
-        quantise_h(1, h1)
-        quantise_adj(2, adj2)
-        nc.sync.dma_start(out=base[:], in_=x0.rearrange("(c p) j -> p c j", p=P))
+                hidden(h_a0[:, g, halves[u], :], sq[:, halves[u], :], adjoint(g, 0, u, 3 + 2 * g + u))
 
-        page[0] = reused([P, S], F32, "page0", 75)
-        page[1] = reused([P, S], F32, "page1", 80)
-        place(0, ya[:, first], 0)
-        put(1, weighed[:], 0)
-        sq20 = squares(2, 0)
-        raw = copied(product([(0, 1), (1, 1)], 0), 88)
-        yb = staging()
+        w2_bf = placed([P, 2048], BF16, "w2_bf1")
+        nc.gpsimd.tensor_scalar(dealt(w2_bf)[:, 0:SHARE], by_channel(w2_late[0]), 1.0, 0.0, ALU.mult, ALU.add)
+        nc.scalar.copy(dealt(w2_bf)[:, SHARE:P], by_channel(w2_late[1]))
+        sq011 = square("sq011", state["01"][:, halves[1], :])
+        state111 = placed([P, U, 4], F32, "state111")
+        tanh(1, 1, 1, state111[:], 1)
+        sq110 = square("sq110", state110[:])
+        sq111 = square("sq111", state111[:])
+        quantise_w2(1, w2_bf, slice(0, 2 * G))
+        quantise_h("h_a0", h_a0[:].rearrange("p g j t -> p (g j t)"), [(0, 0), (1, 0)])
+        adj_bf2 = placed([P, 4 * G], BF16, "adj_bf2")
+        nc.gpsimd.tensor_scalar(
+            adj_bf2[:].rearrange("p (c i) -> p c i", i=4), adj2[:].rearrange("p i c -> p c i"), 1.0, 0.0, ALU.mult, ALU.add
+        )
+        h01, h11 = placed([P, G, 4], BF16, "h01"), placed([P, G, 4], BF16, "h11")
+        hidden(h01[:, halves[0], :], sq010[:], adjoint(0, 1, 0, 3))
+        hidden(h01[:, halves[1], :], sq011[:], adjoint(0, 1, 1, 4))
+        hidden(h11[:, halves[0], :], sq110[:], adjoint(1, 1, 0, 5))
+        quantise_h("h01", flat(h01[:]), [(0, 1)])
+        hidden(h11[:, halves[1], :], sq111[:], adjoint(1, 1, 1, 6))
+        state = {name: placed([P, G, 4], F32, "state" + name) for name in ("20", "21")}
+        tanh(2, 0, 0, state["20"][:, halves[0], :], 2)
+        tanh(2, 0, 1, state["20"][:, halves[1], :], 0)
+        sq20 = squares("sq20", state["20"])
+        sums = product([(0, 0), (1, 0)], 7)
+        y20 = copied("y20", product([(2, 0)], 0))
+        quantise_adj(2, adj_bf2)
+        quantise_h("h11", flat(h11[:]), [(1, 1)])
+        ya = placed([P, 2 * G], F32, "ya")
         for half in (first, second):
-            weigh(nc.gpsimd, yb[:, half], raw[:, half], G)
-        slope = reused([P, U, 4], F32, "slope2", 88)
-        less_one(slope[:], sq20[:, 0:U, :])
-        h2 = rounded_h(2)
-        hidden_on_gpsimd(0, 0, slope, copied_adjoint(2, 0, 0), h2)
-        put(0, yb[:, first], G)
-        put(1, yb[:, second], G)
-        yc = copied(product([(2, 0), (2, 1)], 7))
-        sq21 = squares(2, 1)
-        adj3 = round_adj(3)
-        weigh(nc.gpsimd, yc[:], yc[:], 0)
-        hidden_on_vector(2, 0, 1, sq20, h2)
-        for u in range(2):
-            hidden_on_vector(2, 1, u, sq21, h2)
-        quantise_adj(3, adj3)
-        h_q[2] = reused([P, 2 * G], U32, "h_q2", 84)
-        quantise_h(2, h2)
+            nc.vector.tensor_tensor(ya[:, half], sums[:, half], step[:, 0:G], ALU.mult)
+        page[0], page[1] = placed([P, S], F32, "page0"), placed([P, S], F32, "page1")
+        put(0, ya[:, first], 0)
+        put(1, ya[:, second], 0)
 
-        page[2] = reused([P, S], F32, "page2", 52)
+        slope = placed([P, G, 4], F32, "slope20")
+        nc.gpsimd.tensor_scalar(slope[:], sq20[:], 1.0, -1.0, ALU.mult, ALU.add)
+        yc = placed([P, 2 * G], F32, "yc_w")
+        nc.gpsimd.tensor_tensor(yc[:, first], y20[:], step[:, first], ALU.mult)
+        yb = weigh_pair("yb_w", copied("yb", product([(0, 1), (1, 1)], 3)), 1)
+        put(0, yb[:, 0, :], G)
+        put(1, yb[:, 1, :], G)
+        h2 = placed([P, 2, G, 4], BF16, "h2")
+        b = placed([P, G, 4], F32, "b20")
+        for u in range(2):
+            nc.scalar.copy(b[:, halves[u], :], adjoint(2, 0, u, 4 + u))
+        nc.gpsimd.tensor_tensor(yc[:, second], copied("y21", product([(2, 1)], 7))[:], step[:, second], ALU.mult)
+        nc.gpsimd.tensor_tensor(h2[:, 0], slope[:], b[:], ALU.mult)
+        tanh(2, 1, 0, state["21"][:, halves[0], :], 1)
+        tanh(2, 1, 1, state["21"][:, halves[1], :], 2)
+        sq210 = square("sq210", state["21"][:, halves[0], :])
+        b = copied("b210", adjoint(2, 1, 0, 6))
+        slope = less_one("slope210", sq210)
+        nc.gpsimd.tensor_tensor(h2[:, 1, halves[0], :], slope[:], b[:], ALU.mult)
+        sq211 = square("sq211", state["21"][:, halves[1], :])
+        hidden(h2[:, 1, halves[1], :], sq211[:], adjoint(2, 1, 1, 1))
+        adj_bf3 = round_adj(3, adj3[:], nc.scalar.copy)
+        quantise_h("h2", h2[:].rearrange("p a j t -> p (a j t)"), [(2, 0), (2, 1)])
+        quantise_adj(3, adj_bf3)
+        state = {name: placed([P, G, 4], F32, "state" + name) for name in ("30", "31")}
+        tanh(3, 0, 0, state["30"][:, halves[0], :], 2)
+        tanh(3, 0, 1, state["30"][:, halves[1], :], 0)
+        yf = copied("yf", product([(3, 0), (3, 1)], 4))
+        slope = less_one("slope30", squares("sq30", state["30"]))
+
+        page[2] = placed([P, S], F32, "page2")
         put(2, yc[:], 0)
-        sq30 = squares(3, 0)
-        slope = reused([P, G, 4], F32, "slope3", 56)
-        less_one(slope[:], sq30[:])
-        b30 = [copied_adjoint(3, 0, 0)]
-        state = states(3, 1, (0,))
-        raw = copied(product([(0, 2)], 2), 60)
-        b30.append(copied_adjoint(3, 0, 1))
-        sq31 = squared(3, 1, states(3, 1, (1,), state))
-        ye = copied(product([(3, 0)], 3))
-        yd = staging()
-        weigh(nc.gpsimd, yd[:, first], raw[:, first], 2 * G)
-        h3 = rounded_h(3)
+        yd = weigh_run("yd_w", copied("yd", product([(0, 2)], 6)), 2 * G)
+        ye = weigh_pair("ye_w", copied("ye", product([(1, 2), (2, 2)], 7)), 2)
+        yf = weigh_run("yf_w", yf, 0)
+        put(0, yd[:], 2 * G)
+        put(1, ye[:, 0, :], 2 * G)
+        h3 = placed([P, 2, G, 4], BF16, "h3")
+        b = placed([P, G, 4], F32, "b30")
         for u in range(2):
-            hidden_on_gpsimd(0, u, slope, b30[u], h3)
-        put(0, yd[:, first], 2 * G)
-        for u in range(2):
-            hidden_on_vector(3, 1, u, sq31, h3)
-        quantise_h(3, h3)
+            nc.scalar.copy(b[:, halves[u], :], adjoint(3, 0, u, (4, 2)[u]))
+        nc.gpsimd.tensor_tensor(h3[:, 0], slope[:], b[:], ALU.mult)
+        tanh(3, 1, 0, state["31"][:, halves[0], :], 3)
+        tanh(3, 1, 1, state["31"][:, halves[1], :], 5)
+        sq310 = square("sq310", state["31"][:, halves[0], :])
+        b = copied("b310", adjoint(3, 1, 0, 0))
+        slope = less_one("slope310", sq310)
+        nc.gpsimd.tensor_tensor(h3[:, 1, halves[0], :], slope[:], b[:], ALU.mult)
+        sq311 = square("sq311", state["31"][:, halves[1], :])
+        hidden(h3[:, 1, halves[1], :], sq311[:], adjoint(3, 1, 1, 1))
+        put(2, ye[:, 1, :], 2 * G)
+        turned = open_sums(1, (4, 2))
+        quantise_h("h3", h3[:].rearrange("p a j t -> p (a j t)"), [(3, 0), (3, 1)])
 
-        page[3] = reused([P, S], F32, "page3", 60)
-        place(3, ye[:, first], 0)
-        rest = held([P, 3 * G], F32, "rest")
-        yf = copied(product([(0, 3)], 7))
-        ys = [copied(product([(c, 2), (c, 3)], c)) for c in (1, 2)]
-        nc.scalar.copy(rest[:, 2 * G :], product([(3, 3)], 7))
-        nc.scalar.copy(rest[:, 0 : 2 * G], product([(3, 1), (3, 2)], 7))
-        for c, (y, j0) in enumerate(((yf[:, first], 3 * G), (ys[0][:], 2 * G), (ys[1][:], 2 * G))):
-            banks = open_sums(c)
-            place(c, y, j0)
-            finish_on_tensor(c, banks)
-        place(3, rest[:, 0 : 2 * G], G)
-        place(3, rest[:, 2 * G :], 3 * G)
+        page[3] = placed([P, S], F32, "page3")
+        put(3, yf[:], 0)
+        put(0, weigh_run("yg_w", copied("yg", product([(0, 3)], 6)), 3 * G)[:], 3 * G)
+        yh = weigh_pair("yh_w", copied("yh", product([(1, 3), (2, 3)], 7)), 3)
+        yi = weigh_run("yi_w", copied("yi", product([(3, 2), (3, 3)], 3)), 2 * G)
+        put(1, yh[:, 0, :], 3 * G)
+        put(2, yh[:, 1, :], 3 * G)
+        put(3, yi[:], 2 * G)
+        finish_on_gpsimd(0)
+        finish_on_tensor(1, turned, (5, 0))
+        finish_on_gpsimd(2)
         finish_on_vector(3)

@@ -29,15 +29,15 @@ AT = {
     "w8": 16, "step": 20, "adj3": 24, "base": 31,
     "w4_0": 136, "picked0": 137.75, "w4_raw1": 138, "w4_1": 144, "w2_early": 47, "w4_raw0": 54, "adj01": 55,
     "state00": 64, "state10": 68, "state01": 72, "state110": 76, "state111": 8,
-    "w2_bf1": 68, "sq00": 80, "sq10": 84, "sq010": 88, "sq011": 5, "sq110": 90, "sq111": 92,
+    "w2_bf1": 100, "sq00": 80, "sq10": 84, "sq010": 88, "sq011": 5, "sq110": 72, "sq111": 92,
     "w2_bf0": 96, "adj_bf0": 100, "adj_bf1": 102, "h_a0": 104, "h01": 108, "h11": 110,
     "adj_bf2": 104, "ya": 93, "page0": 148, "page1": 140,
-    "state20": 64, "state21": 72, "sq20": 80, "sq210": 84, "sq211": 120, "slope20": 110.5, "slope210": 86,
-    "b20": 48, "b210": 28, "h2": 96, "yb": 52, "yb_w": 54, "y20": 56, "y21": 57, "yc_w": 108.5, "adj_bf3": 100, "page2": 25,
+    "state20": 64, "state21": 156, "sq20": 80, "sq210": 84, "sq211": 120, "slope20": 110.5, "slope210": 86,
+    "b20": 48, "b210": 28, "h2": 96, "yb": 52, "yb_w": 54, "yc_w": 156, "adj_bf3": 52, "page2": 25,
     "state30": 64, "state31": 132, "sq30": 80, "sq310": 84, "sq311": 128, "slope30": 152, "slope310": 86,
-    "b30": 48, "b310": 124, "h3": 112, "yd": 0, "yd_w": 1, "ye": 60, "ye_w": 62, "yf": 58, "yf_w": 99, "page3": 125,
-    "yg": 52, "yg_w": 53, "yh": 54, "yh_w": 56, "yi": 116, "yi_w": 120, "total0": 114, "total2": 148, "total3": 25,
-    "h_a0_sc": 7, "adj2_sc": 90, "adj3_sc": 29.5,
+    "b30": 48, "b310": 124, "h3": 112, "yd": 0, "yd_w": 1, "ye": 60, "ye_w": 62, "yf": 58, "yf_w": 52, "page3": 125,
+    "yg": 64, "yg_w": 65, "yh": 66, "yh_w": 68, "yi": 116, "yi_w": 120, "total0": 114, "total2": 148, "total3": 25,
+    "h_a0_sc": 7, "adj2_sc": 72, "adj3_sc": 29.5, "h2_sc": 29, "h30_sc": 124, "h31_sc": 124.5,
 }
 
 
@@ -314,9 +314,9 @@ def tile_list_delay_sensitivity_rows_kernel(
                 nc.scalar.copy(total[:, 512 * e : 512 * (e + 1)], back[:].rearrange("p b j -> p (b j)"))
             nc.scalar.dma_start(out=out[P * c : P * (c + 1), :], in_=total[:])
 
-        def finish_on_gpsimd(c):
+        def finish_on_gpsimd(c, pieces):
             total = placed([P, S], F32, f"total{c}")
-            for cols in (slice(0, HALF), slice(HALF, S)):
+            for cols in pieces:
                 nc.gpsimd.tensor_tensor(total[:, cols], base[:, c, cols], page[c][:, cols], ALU.add)
                 nc.sync.dma_start(out=out[P * c : P * (c + 1), cols], in_=total[:, cols])
 
@@ -380,7 +380,6 @@ def tile_list_delay_sensitivity_rows_kernel(
         tanh(2, 0, 1, state["20"][:, halves[1], :], 0)
         sq20 = squares("sq20", state["20"])
         sums = product([(0, 0), (1, 0)], 7)
-        y20 = copied("y20", product([(2, 0)], 0))
         quantise_adj(2, adj_bf2)
         quantise_h("h11", flat(h11[:]), [(1, 1)])
         ya = placed([P, 2 * G], F32, "ya")
@@ -392,30 +391,29 @@ def tile_list_delay_sensitivity_rows_kernel(
 
         slope = placed([P, G, 4], F32, "slope20")
         nc.gpsimd.tensor_scalar(slope[:], sq20[:], 1.0, -1.0, ALU.mult, ALU.add)
-        yc = placed([P, 2 * G], F32, "yc_w")
-        nc.gpsimd.tensor_tensor(yc[:, first], y20[:], step[:, first], ALU.mult)
-        yb = weigh_pair("yb_w", copied("yb", product([(0, 1), (1, 1)], 3)), 1)
+        yb = weigh_pair("yb_w", copied("yb", product([(0, 1), (1, 1)], 2)), 1)
         put(0, yb[:, 0, :], G)
         put(1, yb[:, 1, :], G)
         h2 = placed([P, 2, G, 4], BF16, "h2")
         b = placed([P, G, 4], F32, "b20")
         for u in range(2):
             nc.scalar.copy(b[:, halves[u], :], adjoint(2, 0, u, 4 + u))
-        nc.gpsimd.tensor_tensor(yc[:, second], copied("y21", product([(2, 1)], 7))[:], step[:, second], ALU.mult)
         nc.gpsimd.tensor_tensor(h2[:, 0], slope[:], b[:], ALU.mult)
         tanh(2, 1, 0, state["21"][:, halves[0], :], 1)
-        tanh(2, 1, 1, state["21"][:, halves[1], :], 2)
+        tanh(2, 1, 1, state["21"][:, halves[1], :], 0)
         sq210 = square("sq210", state["21"][:, halves[0], :])
         b = copied("b210", adjoint(2, 1, 0, 6))
         slope = less_one("slope210", sq210)
         nc.gpsimd.tensor_tensor(h2[:, 1, halves[0], :], slope[:], b[:], ALU.mult)
         sq211 = square("sq211", state["21"][:, halves[1], :])
         hidden(h2[:, 1, halves[1], :], sq211[:], adjoint(2, 1, 1, 1))
+        yc = placed([P, 2 * G], F32, "yc_w")
+        nc.vector.tensor_tensor(yc[:], product([(2, 0), (2, 1)], 7), step[:, 0 : 2 * G], ALU.mult)
         adj_bf3 = round_adj(3, adj3[:], nc.scalar.copy)
-        quantise_h("h2", h2[:].rearrange("p a j t -> p (a j t)"), [(2, 0), (2, 1)])
         quantise_adj(3, adj_bf3)
+        quantise_h("h2", h2[:].rearrange("p a j t -> p (a j t)"), [(2, 0), (2, 1)])
         state = {name: placed([P, G, 4], F32, "state" + name) for name in ("30", "31")}
-        tanh(3, 0, 0, state["30"][:, halves[0], :], 2)
+        tanh(3, 0, 0, state["30"][:, halves[0], :], 3)
         tanh(3, 0, 1, state["30"][:, halves[1], :], 0)
         yf = copied("yf", product([(3, 0), (3, 1)], 4))
         slope = less_one("slope30", squares("sq30", state["30"]))
@@ -442,7 +440,8 @@ def tile_list_delay_sensitivity_rows_kernel(
         hidden(h3[:, 1, halves[1], :], sq311[:], adjoint(3, 1, 1, 1))
         put(2, ye[:, 1, :], 2 * G)
         turned = open_sums(1, (4, 2))
-        quantise_h("h3", h3[:].rearrange("p a j t -> p (a j t)"), [(3, 0), (3, 1)])
+        for a in range(2):
+            quantise_h(f"h3{a}", flat(h3[:, a]), [(3, a)])
 
         page[3] = placed([P, S], F32, "page3")
         put(3, yf[:], 0)
@@ -452,7 +451,7 @@ def tile_list_delay_sensitivity_rows_kernel(
         put(1, yh[:, 0, :], 3 * G)
         put(2, yh[:, 1, :], 3 * G)
         put(3, yi[:], 2 * G)
-        finish_on_gpsimd(0)
+        finish_on_gpsimd(0, [slice(0, S)])
         finish_on_tensor(1, turned, (5, 0))
-        finish_on_gpsimd(2)
+        finish_on_gpsimd(2, [slice(0, HALF), slice(HALF, S)])
         finish_on_vector(3)

@@ -21,23 +21,23 @@ P = 128
 G = 256
 U = 128
 HALF = S // 2
-SHARE = 80
+SHARE = 76
 
 AT = {
-    "tab0": 0, "tab1": 16,
-    "w2_late0": 0, "w2_late1": 6, "picked1": 11, "adj2": 11.25,
-    "w8": 16, "step": 20, "adj3": 24, "base": 31,
-    "w4_0": 136, "picked0": 137.75, "w4_raw1": 138, "w4_1": 144, "w2_early": 47, "w4_raw0": 54, "adj01": 55,
-    "state00": 64, "state10": 68, "state01": 72, "state110": 76, "state111": 8,
-    "w2_bf1": 100, "sq00": 80, "sq10": 84, "sq010": 88, "sq011": 5, "sq110": 72, "sq111": 92,
-    "w2_bf0": 96, "adj_bf0": 100, "adj_bf1": 102, "h_a0": 104, "h01": 108, "h11": 110,
-    "adj_bf2": 104, "ya": 93, "page0": 148, "page1": 140,
-    "state20": 64, "state21": 156, "sq20": 80, "sq210": 84, "sq211": 120, "slope20": 110.5, "slope210": 86,
-    "b20": 48, "b210": 28, "h2": 96, "yb": 52, "yb_w": 54, "yc_w": 156, "adj_bf3": 52, "page2": 25,
-    "state30": 64, "state31": 132, "sq30": 80, "sq310": 84, "sq311": 128, "slope30": 152, "slope310": 86,
-    "b30": 48, "b310": 124, "h3": 112, "yd": 0, "yd_w": 1, "ye": 60, "ye_w": 62, "yf": 58, "yf_w": 52, "page3": 125,
-    "yg": 64, "yg_w": 65, "yh": 66, "yh_w": 68, "yi": 116, "yi_w": 120, "total0": 114, "total2": 148, "total3": 25,
-    "h_a0_sc": 7, "adj2_sc": 72, "adj3_sc": 29.5, "h2_sc": 29, "h30_sc": 124, "h31_sc": 124.5,
+    "tab0": 0, "tab1": 20,
+    "w2_late0": 0, "w2_late1": 9, "picked1": 14, "adj2": 14.25,
+    "w8": 20, "step": 24, "adj3": 28, "base": 35,
+    "w4_0": 140, "picked0": 141.75, "w4_raw1": 142, "w4_1": 148, "w2_early": 51, "w4_raw0": 58, "adj01": 59,
+    "state00": 68, "state10": 72, "state01": 76, "state110": 80, "state111": 11.5,
+    "w2_bf1": 104, "sq00": 84, "sq10": 88, "sq01": 5.5, "sq110": 76, "sq111": 96,
+    "w2_bf0": 100, "adj_bf0": 104, "adj_bf1": 106, "h_a0": 108, "h01": 112, "h11": 114,
+    "adj_bf2": 108, "ya": 97, "page0": 152, "page1": 144,
+    "state20": 80, "state21": 160, "sq20": 84, "sq210": 88, "sq211": 124, "slope20": 114.5, "slope210": 90,
+    "b20": 52, "b210": 32, "h2": 100, "yb": 56, "yb_w": 58, "yc_w": 160, "adj_bf3": 56, "page2": 29,
+    "state30": 80, "state31": 136, "sq300": 84, "sq301": 86, "sq310": 88, "sq311": 92, "slope300": 156, "slope310": 90, "slope311": 94,
+    "b300": 52, "b310": 54, "b311": 128, "h3": 116, "yd": 2, "yd_w": 3, "ye": 64, "ye_w": 66, "yf": 62, "yf_w": 56, "page3": 129,
+    "yg": 68, "yg_w": 69, "yh": 70, "yh_w": 72, "y32": 124, "y33": 121, "yi_w": 116, "total0": 120, "total2": 152, "total3": 29,
+    "h_a0_q": 0, "h_a0_sc": 10, "adj2_sc": 76, "adj3_sc": 33.5, "h2_sc": 33,
 }
 
 
@@ -166,7 +166,7 @@ def tile_list_delay_sensitivity_rows_kernel(
 
         def quantise(name, rounded):
             width = rounded.shape[1] // 4
-            words = held([P, width], U32, name + "_q")
+            words = (placed if name + "_q" in AT else held)([P, width], U32, name + "_q")
             scales = (placed if name + "_sc" in AT else held)([P, width], U8, name + "_sc")
             nc.vector.quantize_mx(out=words[:].bitcast(FP8X4), scales=scales[:], in_=rounded)
             return words, scales
@@ -176,9 +176,12 @@ def tile_list_delay_sensitivity_rows_kernel(
                 out=w2_q[a][:, cols].bitcast(FP8X4), scales=w2_sc[a][:, cols], in_=rounded[:, 4 * cols.start : 4 * cols.stop]
             )
 
+        def interleave(copy, rounded, raw):
+            copy(rounded.rearrange("p (c e i) -> p c i e", e=4, i=4), raw.rearrange("p i (c e) -> p c i e", e=4))
+
         def round_adj(g, raw, copy):
             rounded = placed([P, 4 * G], BF16, f"adj_bf{g}")
-            copy(rounded[:].rearrange("p (c e i) -> p c i e", e=4, i=4), raw.rearrange("p i (c e) -> p c i e", e=4))
+            interleave(copy, rounded[:], raw)
             return rounded
 
         def quantise_adj(g, rounded):
@@ -311,8 +314,9 @@ def tile_list_delay_sensitivity_rows_kernel(
                 back = in_bank([P, 4, P], f"back{c}{e}", banks[e])
                 for b in range(4):
                     nc.tensor.transpose(back[:, b, :], sums[e][:, b, :], ident[:])
-                nc.scalar.copy(total[:, 512 * e : 512 * (e + 1)], back[:].rearrange("p b j -> p (b j)"))
-            nc.scalar.dma_start(out=out[P * c : P * (c + 1), :], in_=total[:])
+                cols = slice(512 * e, 512 * (e + 1))
+                nc.scalar.copy(total[:, cols], back[:].rearrange("p b j -> p (b j)"))
+                nc.scalar.dma_start(out=out[P * c : P * (c + 1), cols], in_=total[:, cols])
 
         def finish_on_gpsimd(c, pieces):
             total = placed([P, S], F32, f"total{c}")
@@ -339,17 +343,25 @@ def tile_list_delay_sensitivity_rows_kernel(
         sq10 = square("sq10", state["10"][:])
         tanh(0, 1, 1, state["01"][:, halves[1], :], 2)
         state110 = placed([P, U, 4], F32, "state110")
-        tanh(1, 1, 0, state110[:], 0)
-        sq010 = square("sq010", state["01"][:, halves[0], :])
+        tanh(1, 1, 0, state110[:], 7)
 
         w2_bf = placed([P, 2048], BF16, "w2_bf0")
         for tiles in (slice(0, 2), slice(2, 4)):
             nc.vector.tensor_copy(dealt(w2_bf)[:, :, tiles, :], by_channel(w2_early)[:, :, tiles, :])
         for cols in (first, second):
             quantise_w2(0, w2_bf, cols)
-        adj_bf = [round_adj(g, adj01[:, :, G * g : G * (g + 1)], nc.vector.tensor_copy) for g in range(2)]
-        for g in range(2):
-            quantise_adj(g, adj_bf[g])
+        adj_bf0 = placed([P, 2, 4 * U], BF16, "adj_bf0")
+        for u in range(2):
+            interleave(nc.vector.tensor_copy, adj_bf0[:, u, :], adj01[:, :, halves[u]])
+        adj_q[0], adj_sc[0] = held([P, G], U32, "adj0_q"), held([P, G], U8, "adj0_sc")
+
+        def quantise_adj0(u):
+            nc.vector.quantize_mx(out=adj_q[0][:, halves[u]].bitcast(FP8X4), scales=adj_sc[0][:, halves[u]], in_=adj_bf0[:, u, :])
+
+        quantise_adj0(0)
+        adj_bf1 = round_adj(1, adj01[:, :, second], nc.vector.tensor_copy)
+        quantise_adj0(1)
+        quantise_adj(1, adj_bf1)
         h_a0 = placed([P, 2, G, 4], BF16, "h_a0")
         for g, sq in enumerate((sq00, sq10)):
             for u in range(2):
@@ -358,28 +370,31 @@ def tile_list_delay_sensitivity_rows_kernel(
         w2_bf = placed([P, 2048], BF16, "w2_bf1")
         nc.gpsimd.tensor_scalar(dealt(w2_bf)[:, 0:SHARE], by_channel(w2_late[0]), 1.0, 0.0, ALU.mult, ALU.add)
         nc.scalar.copy(dealt(w2_bf)[:, SHARE:P], by_channel(w2_late[1]))
-        sq011 = square("sq011", state["01"][:, halves[1], :])
+        sq01 = square("sq01", state["01"][:])
         state111 = placed([P, U, 4], F32, "state111")
-        tanh(1, 1, 1, state111[:], 1)
+        tanh(1, 1, 1, state111[:], 0)
         sq110 = square("sq110", state110[:])
         sq111 = square("sq111", state111[:])
-        quantise_w2(1, w2_bf, slice(0, 2 * G))
+        for cols in (first, second):
+            quantise_w2(1, w2_bf, cols)
         quantise_h("h_a0", h_a0[:].rearrange("p g j t -> p (g j t)"), [(0, 0), (1, 0)])
         adj_bf2 = placed([P, 4 * G], BF16, "adj_bf2")
         nc.gpsimd.tensor_scalar(
             adj_bf2[:].rearrange("p (c i) -> p c i", i=4), adj2[:].rearrange("p i c -> p c i"), 1.0, 0.0, ALU.mult, ALU.add
         )
         h01, h11 = placed([P, G, 4], BF16, "h01"), placed([P, G, 4], BF16, "h11")
-        hidden(h01[:, halves[0], :], sq010[:], adjoint(0, 1, 0, 3))
-        hidden(h01[:, halves[1], :], sq011[:], adjoint(0, 1, 1, 4))
+        hidden(h01[:, halves[0], :], sq01[:, halves[0], :], adjoint(0, 1, 0, 3))
+        hidden(h01[:, halves[1], :], sq01[:, halves[1], :], adjoint(0, 1, 1, 4))
         hidden(h11[:, halves[0], :], sq110[:], adjoint(1, 1, 0, 5))
         quantise_h("h01", flat(h01[:]), [(0, 1)])
         hidden(h11[:, halves[1], :], sq111[:], adjoint(1, 1, 1, 6))
         state = {name: placed([P, G, 4], F32, "state" + name) for name in ("20", "21")}
         tanh(2, 0, 0, state["20"][:, halves[0], :], 2)
-        tanh(2, 0, 1, state["20"][:, halves[1], :], 0)
+        tanh(2, 0, 1, state["20"][:, halves[1], :], 1)
         sq20 = squares("sq20", state["20"])
         sums = product([(0, 0), (1, 0)], 7)
+        tanh(2, 1, 0, state["21"][:, halves[0], :], 0)
+        tanh(2, 1, 1, state["21"][:, halves[1], :], 3)
         quantise_adj(2, adj_bf2)
         quantise_h("h11", flat(h11[:]), [(1, 1)])
         ya = placed([P, 2 * G], F32, "ya")
@@ -399,59 +414,57 @@ def tile_list_delay_sensitivity_rows_kernel(
         for u in range(2):
             nc.scalar.copy(b[:, halves[u], :], adjoint(2, 0, u, 4 + u))
         nc.gpsimd.tensor_tensor(h2[:, 0], slope[:], b[:], ALU.mult)
-        tanh(2, 1, 0, state["21"][:, halves[0], :], 1)
-        tanh(2, 1, 1, state["21"][:, halves[1], :], 0)
         sq210 = square("sq210", state["21"][:, halves[0], :])
         b = copied("b210", adjoint(2, 1, 0, 6))
         slope = less_one("slope210", sq210)
         nc.gpsimd.tensor_tensor(h2[:, 1, halves[0], :], slope[:], b[:], ALU.mult)
         sq211 = square("sq211", state["21"][:, halves[1], :])
-        hidden(h2[:, 1, halves[1], :], sq211[:], adjoint(2, 1, 1, 1))
+        hidden(h2[:, 1, halves[1], :], sq211[:], adjoint(2, 1, 1, 0))
         yc = placed([P, 2 * G], F32, "yc_w")
         nc.vector.tensor_tensor(yc[:], product([(2, 0), (2, 1)], 7), step[:, 0 : 2 * G], ALU.mult)
         adj_bf3 = round_adj(3, adj3[:], nc.scalar.copy)
         quantise_adj(3, adj_bf3)
         quantise_h("h2", h2[:].rearrange("p a j t -> p (a j t)"), [(2, 0), (2, 1)])
         state = {name: placed([P, G, 4], F32, "state" + name) for name in ("30", "31")}
-        tanh(3, 0, 0, state["30"][:, halves[0], :], 3)
-        tanh(3, 0, 1, state["30"][:, halves[1], :], 0)
+        tanh(3, 0, 0, state["30"][:, halves[0], :], 1)
+        tanh(3, 0, 1, state["30"][:, halves[1], :], 3)
         yf = copied("yf", product([(3, 0), (3, 1)], 4))
-        slope = less_one("slope30", squares("sq30", state["30"]))
+        sq300 = square("sq300", state["30"][:, halves[0], :])
+        sq301 = square("sq301", state["30"][:, halves[1], :])
+        slope = less_one("slope300", sq300)
 
         page[2] = placed([P, S], F32, "page2")
         put(2, yc[:], 0)
+        tanh(3, 1, 0, state["31"][:, halves[0], :], 2)
         yd = weigh_run("yd_w", copied("yd", product([(0, 2)], 6)), 2 * G)
+        tanh(3, 1, 1, state["31"][:, halves[1], :], 5)
         ye = weigh_pair("ye_w", copied("ye", product([(1, 2), (2, 2)], 7)), 2)
         yf = weigh_run("yf_w", yf, 0)
         put(0, yd[:], 2 * G)
         put(1, ye[:, 0, :], 2 * G)
         h3 = placed([P, 2, G, 4], BF16, "h3")
-        b = placed([P, G, 4], F32, "b30")
+        nc.gpsimd.tensor_tensor(h3[:, 0, halves[0], :], slope[:], copied("b300", adjoint(3, 0, 0, 4))[:], ALU.mult)
+        hidden(h3[:, 0, halves[1], :], sq301[:], adjoint(3, 0, 1, 0))
         for u in range(2):
-            nc.scalar.copy(b[:, halves[u], :], adjoint(3, 0, u, (4, 2)[u]))
-        nc.gpsimd.tensor_tensor(h3[:, 0], slope[:], b[:], ALU.mult)
-        tanh(3, 1, 0, state["31"][:, halves[0], :], 3)
-        tanh(3, 1, 1, state["31"][:, halves[1], :], 5)
-        sq310 = square("sq310", state["31"][:, halves[0], :])
-        b = copied("b310", adjoint(3, 1, 0, 0))
-        slope = less_one("slope310", sq310)
-        nc.gpsimd.tensor_tensor(h3[:, 1, halves[0], :], slope[:], b[:], ALU.mult)
-        sq311 = square("sq311", state["31"][:, halves[1], :])
-        hidden(h3[:, 1, halves[1], :], sq311[:], adjoint(3, 1, 1, 1))
+            sq = square(f"sq31{u}", state["31"][:, halves[u], :])
+            b = copied(f"b31{u}", adjoint(3, 1, u, (1, 3)[u]))
+            nc.gpsimd.tensor_tensor(h3[:, 1, halves[u], :], less_one(f"slope31{u}", sq)[:], b[:], ALU.mult)
         put(2, ye[:, 1, :], 2 * G)
+        y32 = copied("y32", product([(3, 2)], 6))
         turned = open_sums(1, (4, 2))
-        for a in range(2):
-            quantise_h(f"h3{a}", flat(h3[:, a]), [(3, a)])
+        quantise_h("h3", h3[:].rearrange("p a j t -> p (a j t)"), [(3, 0), (3, 1)])
 
         page[3] = placed([P, S], F32, "page3")
         put(3, yf[:], 0)
+        yi = placed([P, 2 * G], F32, "yi_w")
+        nc.gpsimd.tensor_tensor(yi[:, first], y32[:], step[:, 2 * G : 3 * G], ALU.mult)
         put(0, weigh_run("yg_w", copied("yg", product([(0, 3)], 6)), 3 * G)[:], 3 * G)
         yh = weigh_pair("yh_w", copied("yh", product([(1, 3), (2, 3)], 7)), 3)
-        yi = weigh_run("yi_w", copied("yi", product([(3, 2), (3, 3)], 3)), 2 * G)
+        nc.gpsimd.tensor_tensor(yi[:, second], copied("y33", product([(3, 3)], 3))[:], step[:, 3 * G :], ALU.mult)
         put(1, yh[:, 0, :], 3 * G)
         put(2, yh[:, 1, :], 3 * G)
         put(3, yi[:], 2 * G)
         finish_on_gpsimd(0, [slice(0, S)])
-        finish_on_tensor(1, turned, (5, 0))
+        finish_on_tensor(1, turned, (5, 1))
         finish_on_gpsimd(2, [slice(0, HALF), slice(HALF, S)])
         finish_on_vector(3)

@@ -24,20 +24,21 @@ HALF = S // 2
 SHARE = 76
 
 AT = {
-    "tab0": 0, "tab1": 20,
-    "w2_late0": 0, "w2_late1": 9, "picked1": 14, "adj2": 14.25,
-    "w8": 20, "step": 24, "adj3": 28, "base": 35,
-    "w4_0": 140, "picked0": 141.75, "w4_raw1": 142, "w4_1": 148, "w2_early": 51, "w4_raw0": 58, "adj01": 59,
-    "state00": 68, "state10": 72, "state01": 76, "state110": 80, "state111": 11.5,
-    "w2_bf1": 104, "sq00": 84, "sq10": 88, "sq01": 5.5, "sq110": 76, "sq111": 96,
-    "w2_bf0": 100, "adj_bf0": 104, "adj_bf1": 106, "h_a0": 108, "h01": 112, "h11": 114,
-    "adj_bf2": 108, "ya": 97, "page0": 152, "page1": 144,
-    "state20": 80, "state21": 160, "sq20": 84, "sq210": 88, "sq211": 124, "slope20": 114.5, "slope210": 90,
-    "b20": 52, "b210": 32, "h2": 100, "yb": 56, "yb_w": 58, "yc_w": 160, "adj_bf3": 56, "page2": 29,
-    "state30": 80, "state31": 136, "sq300": 84, "sq301": 86, "sq310": 88, "sq311": 92, "slope300": 156, "slope310": 90, "slope311": 94,
-    "b300": 52, "b310": 54, "b311": 128, "h3": 116, "yd": 2, "yd_w": 3, "ye": 64, "ye_w": 66, "yf": 62, "yf_w": 56, "page3": 129,
-    "yg": 68, "yg_w": 69, "yh": 70, "yh_w": 72, "y32": 124, "y33": 121, "yi_w": 116, "total0": 120, "total2": 152, "total3": 29,
-    "h_a0_q": 0, "h_a0_sc": 10, "adj2_sc": 76, "adj3_sc": 33.5, "h2_sc": 33,
+    "tab0": 8, "tab1": 28, "picked0": 27.75, "w4_0": 26,
+    "w2_late0": 8.25, "w2_late1": 17, "picked1": 21.5, "adj2": 21.75,
+    "w8": 28, "step": 32, "adj3": 36, "base": 43,
+    "w4_raw1": 67.5, "w4_1": 156, "w2_early": 59, "w4_raw0": 66, "adj01": 0.25,
+    "state00": 76, "state10": 80, "state01": 84, "state110": 88, "state111": 19.5,
+    "w2_bf1": 112, "sq00": 92, "sq10": 96, "sq01": 13.5, "sq110": 84, "sq111": 104,
+    "w2_bf0": 108, "adj_bf0": 112, "adj_bf1": 114, "h_a0": 116, "h01": 120, "h11": 122,
+    "adj_bf2": 116, "ya": 105, "page0": 160, "page1": 152,
+    "state20": 88, "state21": 168, "sq20": 92, "sq210": 96, "sq211": 132, "slope20": 122.5, "slope210": 98,
+    "b20": 60, "b210": 40, "h2": 108, "yb": 64, "yb_w": 66, "yc_w": 168, "adj_bf3": 64, "page2": 37,
+    "state30": 170, "state31": 144, "sq300": 92, "sq301": 94, "sq310": 96, "sq311": 100, "slope300": 108, "slope310": 98, "slope311": 102,
+    "b300": 60, "b310": 62, "b311": 136, "h3": 124, "yd": 10.5, "yd_w": 11.5, "ye": 72, "ye_w": 74, "yf": 70, "yf_w": 64, "page3": 137,
+    "yg": 76, "yg_w": 77, "yh": 92, "yh_w": 80, "y32": 132, "y33": 129, "yi_w": 124,
+    "total0": 89, "total1": 93, "total2": 128, "total3": 37,
+    "h_a0_q": 8.25, "h_a0_sc": 18, "adj2_sc": 84, "adj3_sc": 41.5, "h2_sc": 41,
 }
 
 
@@ -48,7 +49,6 @@ def tile_list_delay_sensitivity_rows_kernel(
     with ExitStack() as ctx:
         keep = ctx.enter_context(tc.tile_pool(name="keep", bufs=1))
         turns = ctx.enter_context(tc.tile_pool(name="turns", bufs=1))
-        ring = ctx.enter_context(tc.tile_pool(name="ring", bufs=2))
         psum = ctx.enter_context(tc.psum_pool(name="psum", bufs=1))
 
         def held(shape, dtype, name):
@@ -74,11 +74,11 @@ def tile_list_delay_sensitivity_rows_kernel(
             out=staged[1][0:32, HALF:].bitcast(I32), in_=w8_scales.bitcast(I32).rearrange("a q t -> q a t")
         )
         nc.sync.dma_start(idx2[:], offs2)
-        for tile in (w4_sc_raw, tab_sc):
-            nc.vector.memset(tile[32:64, :].bitcast(I32), 0)
-            nc.vector.memset(tile[64:P, :].bitcast(I32), 0)
+        for engine, tile in ((nc.vector, tab_sc), (nc.gpsimd, w4_sc_raw)):
+            engine.memset(tile[32:64, :].bitcast(I32), 0)
+            engine.memset(tile[64:P, :].bitcast(I32), 0)
         for e in range(2):
-            nc.vector.memset(planes[e][:].bitcast(I32), 0)
+            nc.gpsimd.memset(planes[e][:].bitcast(I32), 0)
 
         def load_w4(a):
             raw = placed([P, 2, H], U8, f"w4_raw{a}")
@@ -95,10 +95,11 @@ def tile_list_delay_sensitivity_rows_kernel(
 
         w4_raw = load_w4(0)
         tab = [placed([P, T], U32, f"tab{a}") for a in range(2)]
-        for a in range(2):
-            nc.sync.dma_start(
-                out=tab[a][:].bitcast(I32), in_=tab_words[a].rearrange("p t i -> p (t i)").bitcast(I32)
-            )
+
+        def load_table(a):
+            nc.sync.dma_start(out=tab[a][:].bitcast(I32), in_=tab_words[a].rearrange("p t i -> p (t i)").bitcast(I32))
+
+        load_table(0)
 
         def pick_scales(e):
             picked = placed([P, HALF], U8, f"picked{e}")
@@ -130,17 +131,18 @@ def tile_list_delay_sensitivity_rows_kernel(
         stage(0, pick_scales(0)[0:32, :])
         w4 = [order_w4(0, w4_raw)]
         carry(0)
+        load_table(1)
         w4_raw = load_w4(1)
         w2_early = load_rows("w2_early", w2, slice(0, 512))
-        adj01 = load_rows("adj01", adj, slice(0, 2 * G))
         v = [held([P, S], U32, f"v{a}") for a in range(2)]
         nc.vector.tensor_copy(v[0][:], tab[0][:].indirect(idx[:]))
+        adj01 = load_rows("adj01", adj, slice(0, 2 * G))
         stage(1, pick_scales(1)[0:32, :])
         cut = 512 + 4 * SHARE
         w2_late = [load_rows("w2_late0", w2, slice(512, cut)), load_rows("w2_late1", w2, slice(cut, H))]
         carry(1)
         adj2 = load_rows("adj2", adj, slice(2 * G, 3 * G))
-        for cols in (slice(0, G), slice(G, S)):
+        for cols in (slice(0, G), slice(G, HALF), slice(HALF, S)):
             nc.vector.tensor_copy(v[1][:, cols], tab[1][:].indirect(idx[:, cols.start // 16 : cols.stop // 16]))
         w4.append(order_w4(1, w4_raw))
         w8 = placed([P, 2, N], U32, "w8")
@@ -229,6 +231,11 @@ def tile_list_delay_sensitivity_rows_kernel(
             nc.scalar.activation(slope[:], sq[:], ACT.Copy, bias=-1.0)
             return slope
 
+        def less_one_on_gpsimd(name, sq):
+            slope = placed(sq.shape, F32, name)
+            nc.gpsimd.tensor_scalar(slope[:], sq[:], 1.0, -1.0, ALU.mult, ALU.add)
+            return slope
+
         def adjoint(g, a, u, bank):
             sums = in_bank([P, 4, U], f"b{g}{a}{u}", bank)
             for t in range(4):
@@ -248,16 +255,16 @@ def tile_list_delay_sensitivity_rows_kernel(
 
         def product(pairs, bank):
             sums = in_bank([P, 2, G], f"y{pairs[0][0]}{pairs[0][1]}", bank)
-            for e, (c, g) in enumerate(pairs):
-                for a in range(2):
+            for a in range(2):
+                for e, (c, g) in enumerate(pairs):
                     nc.tensor.matmul_mx(
                         out=sums[:, e, :],
                         lhsT=w8[:, a, P * c : P * (c + 1)].bitcast(FP8X4),
                         lhsT_scale=planes[1][:, rows[1] * a + HALF + P * c : rows[1] * a + HALF + P * (c + 1)],
                         rhs=h_q[g, a].bitcast(FP8X4),
                         rhs_scale=h_sc[g, a],
-                        start=(a == 0),
-                        stop=(a == 1),
+                        start=(a == 0 and e == 0),
+                        stop=(a == 1 and e == len(pairs) - 1),
                     )
             return sums[:].rearrange("p e j -> p (e j)")[:, 0 : G * len(pairs)]
 
@@ -290,36 +297,26 @@ def tile_list_delay_sensitivity_rows_kernel(
             nc.gpsimd.tensor_tensor(weighed[:], y[:], step[:, j0 : j0 + y.shape[1]], ALU.mult)
             return weighed
 
-        def open_sums(c, banks):
-            turned = []
-            for e in range(2):
-                sums = in_bank([P, 4, P], f"turned{c}{e}", banks[e])
-                for b in range(4):
-                    cols = slice(512 * e + P * b, 512 * e + P * (b + 1))
-                    nc.tensor.matmul(sums[:, b, :], base[:, c, cols], ident[:], start=(b == 0), stop=False, is_transpose=True)
-                turned.append(sums)
+        def open_sum(c, cols, bank):
+            turned = in_bank([P, 4, P], f"turned{c}", bank)
+            for b in range(4):
+                block = slice(cols.start + P * b, cols.start + P * (b + 1))
+                nc.tensor.matmul(turned[:, b, :], base[:, c, block], ident[:], start=(b == 0), stop=False, is_transpose=True)
             return turned
 
-        def finish_on_tensor(c, turned, banks):
-            sums = []
-            for e in range(2):
-                for b in range(4):
-                    cols = slice(512 * e + P * b, 512 * e + P * (b + 1))
-                    nc.tensor.matmul(turned[e][:, b, :], page[c][:, cols], ident[:], start=False, stop=(b == 3), is_transpose=True)
-                total_t = ring.tile([P, 4, P], F32, name="total_t", bufs=2)
-                nc.scalar.copy(total_t[:], turned[e][:])
-                sums.append(total_t)
-            total = ring.tile([P, S], F32, name="total", bufs=1)
-            for e in range(2):
-                back = in_bank([P, 4, P], f"back{c}{e}", banks[e])
-                for b in range(4):
-                    nc.tensor.transpose(back[:, b, :], sums[e][:, b, :], ident[:])
-                cols = slice(512 * e, 512 * (e + 1))
-                nc.scalar.copy(total[:, cols], back[:].rearrange("p b j -> p (b j)"))
-                nc.scalar.dma_start(out=out[P * c : P * (c + 1), cols], in_=total[:, cols])
+        def finish_on_tensor(c, total, cols, turned, bank):
+            for b in range(4):
+                block = slice(cols.start + P * b, cols.start + P * (b + 1))
+                nc.tensor.matmul(turned[:, b, :], page[c][:, block], ident[:], start=False, stop=(b == 3), is_transpose=True)
+            total_t = held([P, 4, P], F32, f"total_t{c}")
+            nc.scalar.copy(total_t[:], turned[:])
+            back = in_bank([P, 4, P], f"back{c}", bank)
+            for b in range(4):
+                nc.tensor.transpose(back[:, b, :], total_t[:, b, :], ident[:])
+            nc.scalar.copy(total[:, cols], back[:].rearrange("p b j -> p (b j)"))
+            nc.scalar.dma_start(out=out[P * c : P * (c + 1), cols], in_=total[:, cols])
 
-        def finish_on_gpsimd(c, pieces):
-            total = placed([P, S], F32, f"total{c}")
+        def finish_on_gpsimd(c, total, pieces):
             for cols in pieces:
                 nc.gpsimd.tensor_tensor(total[:, cols], base[:, c, cols], page[c][:, cols], ALU.add)
                 nc.sync.dma_start(out=out[P * c : P * (c + 1), cols], in_=total[:, cols])
@@ -332,18 +329,19 @@ def tile_list_delay_sensitivity_rows_kernel(
 
         first, second = slice(0, G), slice(G, 2 * G)
         halves = (slice(0, U), slice(U, G))
+        left, right = slice(0, HALF), slice(HALF, S)
 
         state = {name: placed([P, G, 4], F32, "state" + name) for name in ("00", "10", "01")}
         tanh(0, 0, 0, state["00"][:, halves[0], :], 0)
         tanh(0, 0, 1, state["00"][:, halves[1], :], 1)
         tanh(1, 0, 0, state["10"][:, halves[0], :], 2)
         sq00 = square("sq00", state["00"][:])
-        tanh(1, 0, 1, state["10"][:, halves[1], :], 0)
-        tanh(0, 1, 0, state["01"][:, halves[0], :], 1)
+        tanh(1, 0, 1, state["10"][:, halves[1], :], 3)
+        tanh(0, 1, 0, state["01"][:, halves[0], :], 0)
         sq10 = square("sq10", state["10"][:])
-        tanh(0, 1, 1, state["01"][:, halves[1], :], 2)
+        tanh(0, 1, 1, state["01"][:, halves[1], :], 1)
         state110 = placed([P, U, 4], F32, "state110")
-        tanh(1, 1, 0, state110[:], 7)
+        tanh(1, 1, 0, state110[:], 2)
 
         w2_bf = placed([P, 2048], BF16, "w2_bf0")
         for tiles in (slice(0, 2), slice(2, 4)):
@@ -392,9 +390,8 @@ def tile_list_delay_sensitivity_rows_kernel(
         tanh(2, 0, 0, state["20"][:, halves[0], :], 2)
         tanh(2, 0, 1, state["20"][:, halves[1], :], 1)
         sq20 = squares("sq20", state["20"])
-        sums = product([(0, 0), (1, 0)], 7)
         tanh(2, 1, 0, state["21"][:, halves[0], :], 0)
-        tanh(2, 1, 1, state["21"][:, halves[1], :], 3)
+        sums = product([(0, 0), (1, 0)], 7)
         quantise_adj(2, adj_bf2)
         quantise_h("h11", flat(h11[:]), [(1, 1)])
         ya = placed([P, 2 * G], F32, "ya")
@@ -404,67 +401,68 @@ def tile_list_delay_sensitivity_rows_kernel(
         put(0, ya[:, first], 0)
         put(1, ya[:, second], 0)
 
-        slope = placed([P, G, 4], F32, "slope20")
-        nc.gpsimd.tensor_scalar(slope[:], sq20[:], 1.0, -1.0, ALU.mult, ALU.add)
+        slope = less_one_on_gpsimd("slope20", sq20)
         yb = weigh_pair("yb_w", copied("yb", product([(0, 1), (1, 1)], 2)), 1)
+        slope210 = less_one_on_gpsimd("slope210", square("sq210", state["21"][:, halves[0], :]))
         put(0, yb[:, 0, :], G)
         put(1, yb[:, 1, :], G)
         h2 = placed([P, 2, G, 4], BF16, "h2")
         b = placed([P, G, 4], F32, "b20")
         for u in range(2):
-            nc.scalar.copy(b[:, halves[u], :], adjoint(2, 0, u, 4 + u))
+            nc.scalar.copy(b[:, halves[u], :], adjoint(2, 0, u, (7, 0)[u]))
         nc.gpsimd.tensor_tensor(h2[:, 0], slope[:], b[:], ALU.mult)
-        sq210 = square("sq210", state["21"][:, halves[0], :])
-        b = copied("b210", adjoint(2, 1, 0, 6))
-        slope = less_one("slope210", sq210)
-        nc.gpsimd.tensor_tensor(h2[:, 1, halves[0], :], slope[:], b[:], ALU.mult)
+        tanh(2, 1, 1, state["21"][:, halves[1], :], 2)
+        b = copied("b210", adjoint(2, 1, 0, 7))
+        nc.gpsimd.tensor_tensor(h2[:, 1, halves[0], :], slope210[:], b[:], ALU.mult)
         sq211 = square("sq211", state["21"][:, halves[1], :])
-        hidden(h2[:, 1, halves[1], :], sq211[:], adjoint(2, 1, 1, 0))
+        hidden(h2[:, 1, halves[1], :], sq211[:], adjoint(2, 1, 1, 5))
         yc = placed([P, 2 * G], F32, "yc_w")
-        nc.vector.tensor_tensor(yc[:], product([(2, 0), (2, 1)], 7), step[:, 0 : 2 * G], ALU.mult)
+        nc.vector.tensor_tensor(yc[:], product([(2, 0), (2, 1)], 6), step[:, 0 : 2 * G], ALU.mult)
         adj_bf3 = round_adj(3, adj3[:], nc.scalar.copy)
         quantise_adj(3, adj_bf3)
         quantise_h("h2", h2[:].rearrange("p a j t -> p (a j t)"), [(2, 0), (2, 1)])
         state = {name: placed([P, G, 4], F32, "state" + name) for name in ("30", "31")}
-        tanh(3, 0, 0, state["30"][:, halves[0], :], 1)
+        tanh(3, 0, 0, state["30"][:, halves[0], :], 0)
         tanh(3, 0, 1, state["30"][:, halves[1], :], 3)
-        yf = copied("yf", product([(3, 0), (3, 1)], 4))
+        yf = copied("yf", product([(3, 0), (3, 1)], 2))
         sq300 = square("sq300", state["30"][:, halves[0], :])
         sq301 = square("sq301", state["30"][:, halves[1], :])
-        slope = less_one("slope300", sq300)
+        slope = less_one_on_gpsimd("slope300", sq300)
 
         page[2] = placed([P, S], F32, "page2")
         put(2, yc[:], 0)
-        tanh(3, 1, 0, state["31"][:, halves[0], :], 2)
-        yd = weigh_run("yd_w", copied("yd", product([(0, 2)], 6)), 2 * G)
-        tanh(3, 1, 1, state["31"][:, halves[1], :], 5)
-        ye = weigh_pair("ye_w", copied("ye", product([(1, 2), (2, 2)], 7)), 2)
+        tanh(3, 1, 0, state["31"][:, halves[0], :], 7)
+        yd = weigh_run("yd_w", copied("yd", product([(0, 2)], 1)), 2 * G)
+        tanh(3, 1, 1, state["31"][:, halves[1], :], 4)
+        ye = weigh_pair("ye_w", copied("ye", product([(1, 2), (2, 2)], 6)), 2)
         yf = weigh_run("yf_w", yf, 0)
         put(0, yd[:], 2 * G)
         put(1, ye[:, 0, :], 2 * G)
         h3 = placed([P, 2, G, 4], BF16, "h3")
-        nc.gpsimd.tensor_tensor(h3[:, 0, halves[0], :], slope[:], copied("b300", adjoint(3, 0, 0, 4))[:], ALU.mult)
-        hidden(h3[:, 0, halves[1], :], sq301[:], adjoint(3, 0, 1, 0))
+        nc.gpsimd.tensor_tensor(h3[:, 0, halves[0], :], slope[:], copied("b300", adjoint(3, 0, 0, 2))[:], ALU.mult)
+        hidden(h3[:, 0, halves[1], :], sq301[:], adjoint(3, 0, 1, 5))
         for u in range(2):
             sq = square(f"sq31{u}", state["31"][:, halves[u], :])
-            b = copied(f"b31{u}", adjoint(3, 1, u, (1, 3)[u]))
+            b = copied(f"b31{u}", adjoint(3, 1, u, (0, 3)[u]))
             nc.gpsimd.tensor_tensor(h3[:, 1, halves[u], :], less_one(f"slope31{u}", sq)[:], b[:], ALU.mult)
         put(2, ye[:, 1, :], 2 * G)
-        y32 = copied("y32", product([(3, 2)], 6))
-        turned = open_sums(1, (4, 2))
+        y32 = copied("y32", product([(3, 2)], 1))
+        turned = [open_sum(c, right, (2, 7)[c]) for c in range(2)]
         quantise_h("h3", h3[:].rearrange("p a j t -> p (a j t)"), [(3, 0), (3, 1)])
 
         page[3] = placed([P, S], F32, "page3")
         put(3, yf[:], 0)
         yi = placed([P, 2 * G], F32, "yi_w")
         nc.gpsimd.tensor_tensor(yi[:, first], y32[:], step[:, 2 * G : 3 * G], ALU.mult)
-        put(0, weigh_run("yg_w", copied("yg", product([(0, 3)], 6)), 3 * G)[:], 3 * G)
-        yh = weigh_pair("yh_w", copied("yh", product([(1, 3), (2, 3)], 7)), 3)
+        put(0, weigh_run("yg_w", copied("yg", product([(0, 3)], 1)), 3 * G)[:], 3 * G)
+        yh = weigh_pair("yh_w", copied("yh", product([(1, 3), (2, 3)], 6)), 3)
         nc.gpsimd.tensor_tensor(yi[:, second], copied("y33", product([(3, 3)], 3))[:], step[:, 3 * G :], ALU.mult)
         put(1, yh[:, 0, :], 3 * G)
         put(2, yh[:, 1, :], 3 * G)
         put(3, yi[:], 2 * G)
-        finish_on_gpsimd(0, [slice(0, S)])
-        finish_on_tensor(1, turned, (5, 1))
-        finish_on_gpsimd(2, [slice(0, HALF), slice(HALF, S)])
+        total = [placed([P, S], F32, f"total{c}") for c in range(3)]
+        for c in range(2):
+            finish_on_gpsimd(c, total[c], [left])
+            finish_on_tensor(c, total[c], right, turned[c], (5, 0)[c])
+        finish_on_gpsimd(2, total[2], [left, right])
         finish_on_vector(3)

@@ -21,7 +21,9 @@ P = 128
 G = 256
 U = 128
 HALF = S // 2
-SHARE = 76
+EARLY = 76
+ON_GPSIMD = 56
+ADJ_ON_GPSIMD = 192
 
 AT = {
     "tab0": 8, "tab1": 28, "picked0": 27.75, "w4_0": 26,
@@ -138,7 +140,7 @@ def tile_list_delay_sensitivity_rows_kernel(
         nc.vector.tensor_copy(v[0][:], tab[0][:].indirect(idx[:]))
         adj01 = load_rows("adj01", adj, slice(0, 2 * G))
         stage(1, pick_scales(1)[0:32, :])
-        cut = 512 + 4 * SHARE
+        cut = 512 + 4 * EARLY
         w2_late = [load_rows("w2_late0", w2, slice(512, cut)), load_rows("w2_late1", w2, slice(cut, H))]
         carry(1)
         adj2 = load_rows("adj2", adj, slice(2 * G, 3 * G))
@@ -366,8 +368,11 @@ def tile_list_delay_sensitivity_rows_kernel(
                 hidden(h_a0[:, g, halves[u], :], sq[:, halves[u], :], adjoint(g, 0, u, 3 + 2 * g + u))
 
         w2_bf = placed([P, 2048], BF16, "w2_bf1")
-        nc.gpsimd.tensor_scalar(dealt(w2_bf)[:, 0:SHARE], by_channel(w2_late[0]), 1.0, 0.0, ALU.mult, ALU.add)
-        nc.scalar.copy(dealt(w2_bf)[:, SHARE:P], by_channel(w2_late[1]))
+        nc.gpsimd.tensor_scalar(
+            dealt(w2_bf)[:, 0:ON_GPSIMD], by_channel(w2_late[0])[:, 0:ON_GPSIMD], 1.0, 0.0, ALU.mult, ALU.add
+        )
+        nc.scalar.copy(dealt(w2_bf)[:, ON_GPSIMD:EARLY], by_channel(w2_late[0])[:, ON_GPSIMD:EARLY])
+        nc.scalar.copy(dealt(w2_bf)[:, EARLY:P], by_channel(w2_late[1]))
         sq01 = square("sq01", state["01"][:])
         state111 = placed([P, U, 4], F32, "state111")
         tanh(1, 1, 1, state111[:], 0)
@@ -378,8 +383,14 @@ def tile_list_delay_sensitivity_rows_kernel(
         quantise_h("h_a0", h_a0[:].rearrange("p g j t -> p (g j t)"), [(0, 0), (1, 0)])
         adj_bf2 = placed([P, 4 * G], BF16, "adj_bf2")
         nc.gpsimd.tensor_scalar(
-            adj_bf2[:].rearrange("p (c i) -> p c i", i=4), adj2[:].rearrange("p i c -> p c i"), 1.0, 0.0, ALU.mult, ALU.add
+            adj_bf2[:, 0 : 4 * ADJ_ON_GPSIMD].rearrange("p (c i) -> p c i", i=4),
+            adj2[:, :, 0:ADJ_ON_GPSIMD].rearrange("p i c -> p c i"),
+            1.0,
+            0.0,
+            ALU.mult,
+            ALU.add,
         )
+        interleave(nc.scalar.copy, adj_bf2[:, 4 * ADJ_ON_GPSIMD :], adj2[:, :, ADJ_ON_GPSIMD:G])
         h01, h11 = placed([P, G, 4], BF16, "h01"), placed([P, G, 4], BF16, "h11")
         hidden(h01[:, halves[0], :], sq01[:, halves[0], :], adjoint(0, 1, 0, 3))
         hidden(h01[:, halves[1], :], sq01[:, halves[1], :], adjoint(0, 1, 1, 4))

@@ -21,17 +21,15 @@ P = 128
 G = 256
 U = 128
 HALF = S // 2
-EARLY = 76
-ON_GPSIMD = 56
-ADJ_ON_GPSIMD = 192
+W2_ON_GPSIMD = 56
 
 AT = {
     "tab0": 8, "tab1": 28, "picked0": 27.75, "w4_0": 26,
-    "w2_late0": 8.25, "w2_late1": 17, "picked1": 21.5, "adj2": 21.75,
+    "w2_late": 8.25, "picked1": 21.5, "adj2": 21.75,
     "w8": 28, "step": 32, "adj3": 36, "base": 43,
-    "w4_raw1": 67.5, "w4_1": 156, "w2_early": 59, "w4_raw0": 66, "adj01": 0.25,
-    "state00": 76, "state10": 80, "state01": 84, "state110": 88, "state111": 19.5,
-    "w2_bf1": 112, "sq00": 92, "sq10": 96, "sq01": 13.5, "sq110": 84, "sq111": 104,
+    "w4_1": 156, "w2_early": 59, "w4_raw": 66, "adj01": 0.25,
+    "state00": 76, "state10": 80, "state01": 84, "state110": 88, "state111": 14.25,
+    "w2_bf1": 112, "sq00": 92, "sq10": 96, "sq01": 10.25, "sq110": 84, "sq111": 104,
     "w2_bf0": 108, "adj_bf0": 112, "adj_bf1": 114, "h_a0": 116, "h01": 120, "h11": 122,
     "adj_bf2": 116, "ya": 105, "page0": 160, "page1": 152,
     "state20": 88, "state21": 168, "sq20": 92, "sq210": 96, "sq211": 132, "slope20": 122.5, "slope210": 98,
@@ -40,7 +38,7 @@ AT = {
     "b300": 60, "b310": 62, "b311": 136, "h3": 124, "yd": 10.5, "yd_w": 11.5, "ye": 72, "ye_w": 74, "yf": 70, "yf_w": 64, "page3": 137,
     "yg": 76, "yg_w": 77, "yh": 92, "yh_w": 80, "y32": 132, "y33": 129, "yi_w": 124,
     "total0": 89, "total1": 93, "total2": 128, "total3": 37,
-    "h_a0_q": 8.25, "h_a0_sc": 18, "adj2_sc": 84, "adj3_sc": 41.5, "h2_sc": 41,
+    "h_a0_q": 8.25, "adj2_sc": 84, "adj3_sc": 41.5, "h2_sc": 41,
 }
 
 
@@ -82,20 +80,13 @@ def tile_list_delay_sensitivity_rows_kernel(
         for e in range(2):
             nc.gpsimd.memset(planes[e][:].bitcast(I32), 0)
 
-        def load_w4(a):
-            raw = placed([P, 2, H], U8, f"w4_raw{a}")
-            nc.sync.dma_start(
-                out=raw[:].bitcast(I32),
-                in_=w4_words[:, :, H * a : H * (a + 1)].bitcast(I32).rearrange("k p c -> p k c"),
-            )
-            return raw
-
         def load_rows(name, src, cols):
             raw = placed([P, 4, cols.stop - cols.start], F32, name)
             nc.sync.dma_start(out=raw[:], in_=src[:, cols].rearrange("(p i) c -> p i c", i=4))
             return raw
 
-        w4_raw = load_w4(0)
+        w4_raw = placed([P, 2, 2 * H], U8, "w4_raw")
+        nc.sync.dma_start(out=w4_raw[:].bitcast(I32), in_=w4_words.bitcast(I32).rearrange("k p c -> p k c"))
         tab = [placed([P, T], U32, f"tab{a}") for a in range(2)]
 
         def load_table(a):
@@ -118,11 +109,11 @@ def tile_list_delay_sensitivity_rows_kernel(
                     in_=staged[e][8 * q : 8 * q + 8, :].bitcast(I32),
                 )
 
-        def order_w4(a, raw):
+        def order_w4(a):
             words = placed([P, 2 * H], U8, f"w4_{a}")
             nc.vector.tensor_copy(
                 words[:].bitcast(U16).rearrange("p (k t u m) -> p k u t m", k=2, t=4, m=8),
-                raw[:].rearrange("p k c -> p (k c)").bitcast(U16).rearrange("p (k u m t) -> p k u t m", k=2, t=4, m=8),
+                w4_raw[:, :, H * a : H * (a + 1)].bitcast(U16).rearrange("p k (u m t) -> p k u t m", t=4, m=8),
             )
             return words
 
@@ -131,22 +122,19 @@ def tile_list_delay_sensitivity_rows_kernel(
             w4_sc_raw[:].rearrange("p (a u m t) -> p a u t m", a=2, t=4, m=16),
         )
         stage(0, pick_scales(0)[0:32, :])
-        w4 = [order_w4(0, w4_raw)]
+        w4 = [order_w4(a) for a in range(2)]
         carry(0)
         load_table(1)
-        w4_raw = load_w4(1)
         w2_early = load_rows("w2_early", w2, slice(0, 512))
         v = [held([P, S], U32, f"v{a}") for a in range(2)]
         nc.vector.tensor_copy(v[0][:], tab[0][:].indirect(idx[:]))
         adj01 = load_rows("adj01", adj, slice(0, 2 * G))
         stage(1, pick_scales(1)[0:32, :])
-        cut = 512 + 4 * EARLY
-        w2_late = [load_rows("w2_late0", w2, slice(512, cut)), load_rows("w2_late1", w2, slice(cut, H))]
+        w2_late = load_rows("w2_late", w2, slice(512, H))
         carry(1)
         adj2 = load_rows("adj2", adj, slice(2 * G, 3 * G))
         for cols in (slice(0, G), slice(G, HALF), slice(HALF, S)):
             nc.vector.tensor_copy(v[1][:, cols], tab[1][:].indirect(idx[:, cols.start // 16 : cols.stop // 16]))
-        w4.append(order_w4(1, w4_raw))
         w8 = placed([P, 2, N], U32, "w8")
         nc.sync.dma_start(out=w8[:].bitcast(I32), in_=w8_words.rearrange("a p c i -> p a (c i)").bitcast(I32))
         step = placed([P, S], F32, "step")
@@ -325,7 +313,7 @@ def tile_list_delay_sensitivity_rows_kernel(
 
         def finish_on_vector(c):
             total = placed([P, S], F32, f"total{c}")
-            for cols in (slice(0, 384), slice(384, 768), slice(768, S)):
+            for cols in (slice(0, 384), slice(384, S)):
                 nc.vector.tensor_tensor(total[:, cols], base[:, c, cols], page[c][:, cols], ALU.add)
                 nc.sync.dma_start(out=out[P * c : P * (c + 1), cols], in_=total[:, cols])
 
@@ -369,10 +357,9 @@ def tile_list_delay_sensitivity_rows_kernel(
 
         w2_bf = placed([P, 2048], BF16, "w2_bf1")
         nc.gpsimd.tensor_scalar(
-            dealt(w2_bf)[:, 0:ON_GPSIMD], by_channel(w2_late[0])[:, 0:ON_GPSIMD], 1.0, 0.0, ALU.mult, ALU.add
+            dealt(w2_bf)[:, 0:W2_ON_GPSIMD], by_channel(w2_late)[:, 0:W2_ON_GPSIMD], 1.0, 0.0, ALU.mult, ALU.add
         )
-        nc.scalar.copy(dealt(w2_bf)[:, ON_GPSIMD:EARLY], by_channel(w2_late[0])[:, ON_GPSIMD:EARLY])
-        nc.scalar.copy(dealt(w2_bf)[:, EARLY:P], by_channel(w2_late[1]))
+        nc.scalar.copy(dealt(w2_bf)[:, W2_ON_GPSIMD:P], by_channel(w2_late)[:, W2_ON_GPSIMD:P])
         sq01 = square("sq01", state["01"][:])
         state111 = placed([P, U, 4], F32, "state111")
         tanh(1, 1, 1, state111[:], 0)
@@ -383,14 +370,8 @@ def tile_list_delay_sensitivity_rows_kernel(
         quantise_h("h_a0", h_a0[:].rearrange("p g j t -> p (g j t)"), [(0, 0), (1, 0)])
         adj_bf2 = placed([P, 4 * G], BF16, "adj_bf2")
         nc.gpsimd.tensor_scalar(
-            adj_bf2[:, 0 : 4 * ADJ_ON_GPSIMD].rearrange("p (c i) -> p c i", i=4),
-            adj2[:, :, 0:ADJ_ON_GPSIMD].rearrange("p i c -> p c i"),
-            1.0,
-            0.0,
-            ALU.mult,
-            ALU.add,
+            adj_bf2[:].rearrange("p (c i) -> p c i", i=4), adj2[:].rearrange("p i c -> p c i"), 1.0, 0.0, ALU.mult, ALU.add
         )
-        interleave(nc.scalar.copy, adj_bf2[:, 4 * ADJ_ON_GPSIMD :], adj2[:, :, ADJ_ON_GPSIMD:G])
         h01, h11 = placed([P, G, 4], BF16, "h01"), placed([P, G, 4], BF16, "h11")
         hidden(h01[:, halves[0], :], sq01[:, halves[0], :], adjoint(0, 1, 0, 3))
         hidden(h01[:, halves[1], :], sq01[:, halves[1], :], adjoint(0, 1, 1, 4))
@@ -434,8 +415,8 @@ def tile_list_delay_sensitivity_rows_kernel(
         quantise_h("h2", h2[:].rearrange("p a j t -> p (a j t)"), [(2, 0), (2, 1)])
         state = {name: placed([P, G, 4], F32, "state" + name) for name in ("30", "31")}
         tanh(3, 0, 0, state["30"][:, halves[0], :], 0)
-        tanh(3, 0, 1, state["30"][:, halves[1], :], 3)
-        yf = copied("yf", product([(3, 0), (3, 1)], 2))
+        tanh(3, 0, 1, state["30"][:, halves[1], :], 2)
+        yf = copied("yf", product([(3, 0), (3, 1)], 3))
         sq300 = square("sq300", state["30"][:, halves[0], :])
         sq301 = square("sq301", state["30"][:, halves[1], :])
         slope = less_one_on_gpsimd("slope300", sq300)
@@ -450,15 +431,15 @@ def tile_list_delay_sensitivity_rows_kernel(
         put(0, yd[:], 2 * G)
         put(1, ye[:, 0, :], 2 * G)
         h3 = placed([P, 2, G, 4], BF16, "h3")
-        nc.gpsimd.tensor_tensor(h3[:, 0, halves[0], :], slope[:], copied("b300", adjoint(3, 0, 0, 2))[:], ALU.mult)
+        nc.gpsimd.tensor_tensor(h3[:, 0, halves[0], :], slope[:], copied("b300", adjoint(3, 0, 0, 3))[:], ALU.mult)
         hidden(h3[:, 0, halves[1], :], sq301[:], adjoint(3, 0, 1, 5))
         for u in range(2):
             sq = square(f"sq31{u}", state["31"][:, halves[u], :])
-            b = copied(f"b31{u}", adjoint(3, 1, u, (0, 3)[u]))
+            b = copied(f"b31{u}", adjoint(3, 1, u, (0, 2)[u]))
             nc.gpsimd.tensor_tensor(h3[:, 1, halves[u], :], less_one(f"slope31{u}", sq)[:], b[:], ALU.mult)
         put(2, ye[:, 1, :], 2 * G)
         y32 = copied("y32", product([(3, 2)], 1))
-        turned = [open_sum(c, right, (2, 7)[c]) for c in range(2)]
+        turned = [open_sum(c, right, (3, 7)[c]) for c in range(2)]
         quantise_h("h3", h3[:].rearrange("p a j t -> p (a j t)"), [(3, 0), (3, 1)])
 
         page[3] = placed([P, S], F32, "page3")
@@ -467,7 +448,7 @@ def tile_list_delay_sensitivity_rows_kernel(
         nc.gpsimd.tensor_tensor(yi[:, first], y32[:], step[:, 2 * G : 3 * G], ALU.mult)
         put(0, weigh_run("yg_w", copied("yg", product([(0, 3)], 1)), 3 * G)[:], 3 * G)
         yh = weigh_pair("yh_w", copied("yh", product([(1, 3), (2, 3)], 6)), 3)
-        nc.gpsimd.tensor_tensor(yi[:, second], copied("y33", product([(3, 3)], 3))[:], step[:, 3 * G :], ALU.mult)
+        nc.gpsimd.tensor_tensor(yi[:, second], copied("y33", product([(3, 3)], 2))[:], step[:, 3 * G :], ALU.mult)
         put(1, yh[:, 0, :], 3 * G)
         put(2, yh[:, 1, :], 3 * G)
         put(3, yi[:], 2 * G)

from contextlib import ExitStack

import concourse.mybir as mybir
from concourse.masks import make_identity

K, M, H, N, T, S = 1024, 512, 1024, 512, 4096, 1024
FLOPS = 2 * (K * H * S + M * H * S + H * N * S)

F32 = mybir.dt.float32
BF16 = mybir.dt.bfloat16
I32 = mybir.dt.int32
U32 = mybir.dt.uint32
U16 = mybir.dt.uint16
U8 = mybir.dt.uint8
FP8X4 = mybir.dt.float8_e4m3fn_x4
FP4X4 = mybir.dt.float4_e2m1fn_x4
ALU = mybir.AluOpType
ACT = mybir.ActivationFunctionType

P = 128
G = 256
U = 128
HALF = S // 2
W2_ON_GPSIMD = 56

AT = {
    "tab0": 8, "tab1": 28, "picked0": 27.75, "w4_0": 26,
    "w2_late": 8.25, "picked1": 21.5, "adj2": 21.75,
    "w8": 28, "step": 32, "adj3": 36, "base": 43,
    "w4_1": 156, "w2_early": 59, "w4_raw": 66, "adj01": 0.25,
    "state00": 76, "state10": 80, "state01": 84, "state110": 88, "state111": 14.25,
    "w2_bf1": 112, "sq00": 92, "sq10": 96, "sq01": 10.25, "sq110": 84, "sq111": 104,
    "w2_bf0": 108, "adj_bf0": 112, "adj_bf1": 114, "h_a0": 116, "h01": 120, "h11": 122,
    "adj_bf2": 116, "ya": 105, "page0": 160, "page1": 152,
    "state20": 88, "state21": 168, "sq20": 92, "sq210": 96, "sq211": 132, "slope20": 122.5, "slope210": 98,
    "b20": 60, "b210": 40, "h2": 108, "yb": 64, "yb_w": 66, "yc_w": 168, "adj_bf3": 64, "page2": 37,
    "state30": 170, "state31": 144, "sq300": 92, "sq301": 94, "sq310": 96, "sq311": 100, "slope300": 108, "slope310": 98, "slope311": 102,
    "b300": 60, "b310": 62, "b311": 136, "h3": 124, "yd": 10.5, "yd_w": 11.5, "ye": 72, "ye_w": 74, "yf": 70, "yf_w": 64, "page3": 137,
    "yg": 76, "yg_w": 77, "yh": 92, "yh_w": 80, "y32": 132, "y33": 129, "yi_w": 124,
    "total0": 89, "total1": 93, "total2": 128, "total3": 37,
    "h_a0_q": 8.25, "adj2_sc": 84, "adj3_sc": 41.5, "h2_sc": 41,
}


def tile_list_delay_sensitivity_rows_kernel(
    tc, tab_words, tab_scales, offs, w4_words, w4_scales, adj, w2, w8_words, w8_scales, offs2, wgo, x0, out
):
    nc = tc.nc
    with ExitStack() as ctx:
        keep = ctx.enter_context(tc.tile_pool(name="keep", bufs=1))
        turns = ctx.enter_context(tc.tile_pool(name="turns", bufs=1))
        psum = ctx.enter_context(tc.psum_pool(name="psum", bufs=1))

        def held(shape, dtype, name):
            return keep.tile(shape, dtype, name=name, align_bytes=64)

        def placed(shape, dtype, name):
            return turns.tile(shape, dtype, name=name, offset=int(1024 * AT[name]), align_bytes=64)

        def in_bank(shape, name, bank):
            return psum.tile(shape, F32, name=name, offset=2048 * bank)

        idx = keep.tile([P, S // 16], U16, name="idx")
        idx2 = keep.tile([P, S // 16], U16, name="idx2")
        rows = (HALF + H, HALF + N)
        tab_sc = held([P, T], U8, "tab_sc")
        w4_sc_raw = held([P, H], U8, "w4_sc_raw")
        staged = [held([P, rows[e]], U8, f"staged{e}") for e in range(2)]
        planes = [held([P, 2 * rows[e]], U8, f"planes{e}") for e in range(2)]
        nc.sync.dma_start(idx[:], offs)
        nc.sync.dma_start(out=w4_sc_raw[0:32, :].bitcast(I32), in_=w4_scales.bitcast(I32).rearrange("a q t -> q a t"))
        nc.sync.dma_start(out=tab_sc[0:32, :].bitcast(I32), in_=tab_scales.bitcast(I32).rearrange("a q t -> q a t"))
        nc.sync.dma_start(
            out=staged[1][0:32, HALF:].bitcast(I32), in_=w8_scales.bitcast(I32).rearrange("a q t -> q a t")
        )
        nc.sync.dma_start(idx2[:], offs2)
        for engine, tile in ((nc.vector, tab_sc), (nc.gpsimd, w4_sc_raw)):
            engine.memset(tile[32:64, :].bitcast(I32), 0)
            engine.memset(tile[64:P, :].bitcast(I32), 0)
        for e in range(2):
            nc.gpsimd.memset(planes[e][:].bitcast(I32), 0)

        def load_rows(name, src, cols):
            raw = placed([P, 4, cols.stop - cols.start], F32, name)
            nc.sync.dma_start(out=raw[:], in_=src[:, cols].rearrange("(p i) c -> p i c", i=4))
            return raw

        w4_raw = placed([P, 2, 2 * H], U8, "w4_raw")
        nc.sync.dma_start(out=w4_raw[:].bitcast(I32), in_=w4_words.bitcast(I32).rearrange("k p c -> p k c"))
        tab = [placed([P, T], U32, f"tab{a}") for a in range(2)]

        def load_table(a):
            nc.sync.dma_start(out=tab[a][:].bitcast(I32), in_=tab_words[a].rearrange("p t i -> p (t i)").bitcast(I32))

        load_table(0)

        def pick_scales(e):
            picked = placed([P, HALF], U8, f"picked{e}")
            nc.vector.tensor_copy(picked[:], tab_sc[:].indirect(idx[:, 32 * e : 32 * (e + 1)]))
            return picked

        def stage(e, picked):
            nc.vector.tensor_copy(staged[e][0:32, 0 : picked.shape[1]].bitcast(I32), picked.bitcast(I32))

        def carry(e):
            for q in range(4):
                nc.sync.dma_start(
                    out=planes[e][32 * q : 32 * q + 4, :].bitcast(I32).rearrange("r (a c) -> r a c", a=2),
                    in_=staged[e][8 * q : 8 * q + 8, :].bitcast(I32),
                )

        def order_w4(a):
            words = placed([P, 2 * H], U8, f"w4_{a}")
            nc.vector.tensor_copy(
                words[:].bitcast(U16).rearrange("p (k t u m) -> p k u t m", k=2, t=4, m=8),
                w4_raw[:, :, H * a : H * (a + 1)].bitcast(U16).rearrange("p k (u m t) -> p k u t m", t=4, m=8),
            )
            return words

        nc.vector.tensor_copy(
            staged[0][:, HALF:].rearrange("p (a t u m) -> p a u t m", a=2, t=4, m=16),
            w4_sc_raw[:].rearrange("p (a u m t) -> p a u t m", a=2, t=4, m=16),
        )
        stage(0, pick_scales(0)[0:32, :])
        w4 = [order_w4(a) for a in range(2)]
        carry(0)
        load_table(1)
        w2_early = load_rows("w2_early", w2, slice(0, 512))
        v = [held([P, S], U32, f"v{a}") for a in range(2)]
        nc.vector.tensor_copy(v[0][:], tab[0][:].indirect(idx[:]))
        adj01 = load_rows("adj01", adj, slice(0, 2 * G))
        stage(1, pick_scales(1)[0:32, :])
        w2_late = load_rows("w2_late", w2, slice(512, H))
        carry(1)
        adj2 = load_rows("adj2", adj, slice(2 * G, 3 * G))
        for cols in (slice(0, G), slice(G, HALF), slice(HALF, S)):
            nc.vector.tensor_copy(v[1][:, cols], tab[1][:].indirect(idx[:, cols.start // 16 : cols.stop // 16]))
        w8 = placed([P, 2, N], U32, "w8")
        nc.sync.dma_start(out=w8[:].bitcast(I32), in_=w8_words.rearrange("a p c i -> p a (c i)").bitcast(I32))
        step = placed([P, S], F32, "step")
        nc.sync.dma_start(out=step[:], in_=wgo)
        adj3 = load_rows("adj3", adj, slice(3 * G, S))
        base = placed([P, 4, S], F32, "base")
        nc.sync.dma_start(out=base[:], in_=x0.rearrange("(c p) j -> p c j", p=P))

        ident = held([P, P], F32, "ident")
        make_identity(nc, ident[:])

        w2_q = [held([P, 512], U32, f"w2_q{a}") for a in range(2)]
        w2_sc = [held([P, 512], U8, f"w2_sc{a}") for a in range(2)]
        adj_q, adj_sc, h_q, h_sc, page = {}, {}, {}, {}, {}

        def dealt(rounded):
            return rounded[:].rearrange("p (t m i) -> p m t i", t=4, i=4)

        def by_channel(raw):
            return raw[:].rearrange("p i (m t) -> p m t i", t=4)

        def quantise(name, rounded):
            width = rounded.shape[1] // 4
            words = (placed if name + "_q" in AT else held)([P, width], U32, name + "_q")
            scales = (placed if name + "_sc" in AT else held)([P, width], U8, name + "_sc")
            nc.vector.quantize_mx(out=words[:].bitcast(FP8X4), scales=scales[:], in_=rounded)
            return words, scales

        def quantise_w2(a, rounded, cols):
            nc.vector.quantize_mx(
                out=w2_q[a][:, cols].bitcast(FP8X4), scales=w2_sc[a][:, cols], in_=rounded[:, 4 * cols.start : 4 * cols.stop]
            )

        def interleave(copy, rounded, raw):
            copy(rounded.rearrange("p (c e i) -> p c i e", e=4, i=4), raw.rearrange("p i (c e) -> p c i e", e=4))

        def round_adj(g, raw, copy):
            rounded = placed([P, 4 * G], BF16, f"adj_bf{g}")
            interleave(copy, rounded[:], raw)
            return rounded

        def quantise_adj(g, rounded):
            adj_q[g], adj_sc[g] = quantise(f"adj{g}", rounded[:])

        def quantise_h(name, rounded, parts):
            words, scales = quantise(name, rounded)
            for e, part in enumerate(parts):
                h_q[part], h_sc[part] = words[:, G * e : G * (e + 1)], scales[:, G * e : G * (e + 1)]

        def flat(ap):
            return ap.rearrange("p j t -> p (j t)")

        def tanh(g, a, u, state, bank):
            j0 = G * g + U * u
            e, j1 = divmod(j0, HALF)
            sums = in_bank([P, 4, U], f"x{g}{a}{u}", bank)
            for k in range(2):
                for t in range(4):
                    c0 = rows[0] * k + HALF * (a + 1) + P * t
                    nc.tensor.matmul_mx(
                        out=sums[:, t, :],
                        lhsT=w4[a][:, H * k + 2 * P * t : H * k + 2 * P * (t + 1)].bitcast(FP4X4),
                        lhsT_scale=planes[0][:, c0 : c0 + P],
                        rhs=v[k][:, j0 : j0 + U].bitcast(FP8X4),
                        rhs_scale=planes[e][:, rows[e] * k + j1 : rows[e] * k + j1 + U],
                        start=(k == 0 and t == 0),
                        stop=(k == 1 and t == 3),
                    )
            nc.scalar.activation(state, sums[:].rearrange("p t j -> p j t"), ACT.Tanh)

        def square(name, state):
            sq = placed(state.shape, F32, name)
            nc.scalar.activation(sq[:], state, ACT.Square)
            return sq

        def squares(name, state):
            sq = placed([P, G, 4], F32, name)
            for half in halves:
                nc.scalar.activation(sq[:, half, :], state[:, half, :], ACT.Square)
            return sq

        def less_one(name, sq):
            slope = placed(sq.shape, F32, name)
            nc.scalar.activation(slope[:], sq[:], ACT.Copy, bias=-1.0)
            return slope

        def less_one_on_gpsimd(name, sq):
            slope = placed(sq.shape, F32, name)
            nc.gpsimd.tensor_scalar(slope[:], sq[:], 1.0, -1.0, ALU.mult, ALU.add)
            return slope

        def adjoint(g, a, u, bank):
            sums = in_bank([P, 4, U], f"b{g}{a}{u}", bank)
            for t in range(4):
                nc.tensor.matmul_mx(
                    out=sums[:, t, :],
                    lhsT=w2_q[a][:, P * t : P * (t + 1)].bitcast(FP8X4),
                    lhsT_scale=w2_sc[a][:, P * t : P * (t + 1)],
                    rhs=adj_q[g][:, U * u : U * (u + 1)].bitcast(FP8X4),
                    rhs_scale=adj_sc[g][:, U * u : U * (u + 1)],
                    start=True,
                    stop=True,
                )
            return sums[:].rearrange("p t j -> p j t")

        def hidden(rounded, sq, b):
            nc.vector.scalar_tensor_tensor(out=rounded, in0=sq, scalar=1.0, in1=b, op0=ALU.subtract, op1=ALU.mult)

        def product(pairs, bank):
            sums = in_bank([P, 2, G], f"y{pairs[0][0]}{pairs[0][1]}", bank)
            for a in range(2):
                for e, (c, g) in enumerate(pairs):
                    nc.tensor.matmul_mx(
                        out=sums[:, e, :],
                        lhsT=w8[:, a, P * c : P * (c + 1)].bitcast(FP8X4),
                        lhsT_scale=planes[1][:, rows[1] * a + HALF + P * c : rows[1] * a + HALF + P * (c + 1)],
                        rhs=h_q[g, a].bitcast(FP8X4),
                        rhs_scale=h_sc[g, a],
                        start=(a == 0 and e == 0),
                        stop=(a == 1 and e == len(pairs) - 1),
                    )
            return sums[:].rearrange("p e j -> p (e j)")[:, 0 : G * len(pairs)]

        def copied(name, sums):
            y = placed(sums.shape, F32, name)
            nc.scalar.copy(y[:], sums)
            return y

        def offsets(j0, y):
            return idx2[:, j0 // 16 : (j0 + y.shape[1]) // 16]

        def place(c, y, j0):
            nc.vector.tensor_tensor(page[c][:].indirect(offsets(j0, y)), y, step[:, j0 : j0 + y.shape[1]], ALU.mult)

        def put(c, y, j0):
            nc.vector.tensor_copy(page[c][:].indirect(offsets(j0, y)), y)

        def weigh_pair(name, y, g):
            weighed = placed([P, 2, G], F32, name)
            nc.gpsimd.tensor_tensor(
                weighed[:],
                y[:].rearrange("p (e j) -> p e j", e=2),
                step[:, G * g : G * (g + 1)].unsqueeze(1).to_broadcast([P, 2, G]),
                ALU.mult,
            )
            return weighed

        def weigh_run(name, y, j0):
            weighed = placed(y.shape, F32, name)
            nc.gpsimd.tensor_tensor(weighed[:], y[:], step[:, j0 : j0 + y.shape[1]], ALU.mult)
            return weighed

        def open_sum(c, cols, bank):
            turned = in_bank([P, 4, P], f"turned{c}", bank)
            for b in range(4):
                block = slice(cols.start + P * b, cols.start + P * (b + 1))
                nc.tensor.matmul(turned[:, b, :], base[:, c, block], ident[:], start=(b == 0), stop=False, is_transpose=True)
            return turned

        def finish_on_tensor(c, total, cols, turned, bank):
            for b in range(4):
                block = slice(cols.start + P * b, cols.start + P * (b + 1))
                nc.tensor.matmul(turned[:, b, :], page[c][:, block], ident[:], start=False, stop=(b == 3), is_transpose=True)
            total_t = held([P, 4, P], F32, f"total_t{c}")
            nc.scalar.copy(total_t[:], turned[:])
            back = in_bank([P, 4, P], f"back{c}", bank)
            for b in range(4):
                nc.tensor.transpose(back[:, b, :], total_t[:, b, :], ident[:])
            nc.scalar.copy(total[:, cols], back[:].rearrange("p b j -> p (b j)"))
            nc.scalar.dma_start(out=out[P * c : P * (c + 1), cols], in_=total[:, cols])

        def finish_on_gpsimd(c, total, pieces):
            for cols in pieces:
                nc.gpsimd.tensor_tensor(total[:, cols], base[:, c, cols], page[c][:, cols], ALU.add)
                nc.sync.dma_start(out=out[P * c : P * (c + 1), cols], in_=total[:, cols])

        def finish_on_vector(c):
            total = placed([P, S], F32, f"total{c}")
            for cols in (slice(0, 384), slice(384, S)):
                nc.vector.tensor_tensor(total[:, cols], base[:, c, cols], page[c][:, cols], ALU.add)
                nc.sync.dma_start(out=out[P * c : P * (c + 1), cols], in_=total[:, cols])

        first, second = slice(0, G), slice(G, 2 * G)
        halves = (slice(0, U), slice(U, G))
        left, right = slice(0, HALF), slice(HALF, S)

        state = {name: placed([P, G, 4], F32, "state" + name) for name in ("00", "10", "01")}
        tanh(0, 0, 0, state["00"][:, halves[0], :], 0)
        tanh(0, 0, 1, state["00"][:, halves[1], :], 1)
        tanh(1, 0, 0, state["10"][:, halves[0], :], 2)
        sq00 = square("sq00", state["00"][:])
        tanh(1, 0, 1, state["10"][:, halves[1], :], 3)
        tanh(0, 1, 0, state["01"][:, halves[0], :], 0)
        sq10 = square("sq10", state["10"][:])
        tanh(0, 1, 1, state["01"][:, halves[1], :], 1)
        state110 = placed([P, U, 4], F32, "state110")
        tanh(1, 1, 0, state110[:], 2)

        w2_bf = placed([P, 2048], BF16, "w2_bf0")
        for tiles in (slice(0, 2), slice(2, 4)):
            nc.vector.tensor_copy(dealt(w2_bf)[:, :, tiles, :], by_channel(w2_early)[:, :, tiles, :])
        for cols in (first, second):
            quantise_w2(0, w2_bf, cols)
        adj_bf0 = placed([P, 2, 4 * U], BF16, "adj_bf0")
        for u in range(2):
            interleave(nc.vector.tensor_copy, adj_bf0[:, u, :], adj01[:, :, halves[u]])
        adj_q[0], adj_sc[0] = held([P, G], U32, "adj0_q"), held([P, G], U8, "adj0_sc")

        def quantise_adj0(u):
            nc.vector.quantize_mx(out=adj_q[0][:, halves[u]].bitcast(FP8X4), scales=adj_sc[0][:, halves[u]], in_=adj_bf0[:, u, :])

        quantise_adj0(0)
        adj_bf1 = round_adj(1, adj01[:, :, second], nc.vector.tensor_copy)
        quantise_adj0(1)
        quantise_adj(1, adj_bf1)
        h_a0 = placed([P, 2, G, 4], BF16, "h_a0")
        for g, sq in enumerate((sq00, sq10)):
            for u in range(2):
                hidden(h_a0[:, g, halves[u], :], sq[:, halves[u], :], adjoint(g, 0, u, 3 + 2 * g + u))

        w2_bf = placed([P, 2048], BF16, "w2_bf1")
        nc.gpsimd.tensor_scalar(
            dealt(w2_bf)[:, 0:W2_ON_GPSIMD], by_channel(w2_late)[:, 0:W2_ON_GPSIMD], 1.0, 0.0, ALU.mult, ALU.add
        )
        nc.scalar.copy(dealt(w2_bf)[:, W2_ON_GPSIMD:P], by_channel(w2_late)[:, W2_ON_GPSIMD:P])
        sq01 = square("sq01", state["01"][:])
        state111 = placed([P, U, 4], F32, "state111")
        tanh(1, 1, 1, state111[:], 0)
        sq110 = square("sq110", state110[:])
        sq111 = square("sq111", state111[:])
        for cols in (first, second):
            quantise_w2(1, w2_bf, cols)
        quantise_h("h_a0", h_a0[:].rearrange("p g j t -> p (g j t)"), [(0, 0), (1, 0)])
        adj_bf2 = placed([P, 4 * G], BF16, "adj_bf2")
        nc.gpsimd.tensor_scalar(
            adj_bf2[:].rearrange("p (c i) -> p c i", i=4), adj2[:].rearrange("p i c -> p c i"), 1.0, 0.0, ALU.mult, ALU.add
        )
        h01, h11 = placed([P, G, 4], BF16, "h01"), placed([P, G, 4], BF16, "h11")
        hidden(h01[:, halves[0], :], sq01[:, halves[0], :], adjoint(0, 1, 0, 3))
        hidden(h01[:, halves[1], :], sq01[:, halves[1], :], adjoint(0, 1, 1, 4))
        hidden(h11[:, halves[0], :], sq110[:], adjoint(1, 1, 0, 5))
        quantise_h("h01", flat(h01[:]), [(0, 1)])
        hidden(h11[:, halves[1], :], sq111[:], adjoint(1, 1, 1, 6))
        state = {name: placed([P, G, 4], F32, "state" + name) for name in ("20", "21")}
        tanh(2, 0, 0, state["20"][:, halves[0], :], 2)
        tanh(2, 0, 1, state["20"][:, halves[1], :], 1)
        sq20 = squares("sq20", state["20"])
        tanh(2, 1, 0, state["21"][:, halves[0], :], 0)
        sums = product([(0, 0), (1, 0)], 7)
        quantise_adj(2, adj_bf2)
        quantise_h("h11", flat(h11[:]), [(1, 1)])
        ya = placed([P, 2 * G], F32, "ya")
        for half in (first, second):
            nc.vector.tensor_tensor(ya[:, half], sums[:, half], step[:, 0:G], ALU.mult)
        page[0], page[1] = placed([P, S], F32, "page0"), placed([P, S], F32, "page1")
        put(0, ya[:, first], 0)
        put(1, ya[:, second], 0)

        slope = less_one_on_gpsimd("slope20", sq20)
        yb = weigh_pair("yb_w", copied("yb", product([(0, 1), (1, 1)], 2)), 1)
        slope210 = less_one_on_gpsimd("slope210", square("sq210", state["21"][:, halves[0], :]))
        put(0, yb[:, 0, :], G)
        put(1, yb[:, 1, :], G)
        h2 = placed([P, 2, G, 4], BF16, "h2")
        b = placed([P, G, 4], F32, "b20")
        for u in range(2):
            nc.scalar.copy(b[:, halves[u], :], adjoint(2, 0, u, (7, 0)[u]))
        nc.gpsimd.tensor_tensor(h2[:, 0], slope[:], b[:], ALU.mult)
        tanh(2, 1, 1, state["21"][:, halves[1], :], 2)
        b = copied("b210", adjoint(2, 1, 0, 7))
        nc.gpsimd.tensor_tensor(h2[:, 1, halves[0], :], slope210[:], b[:], ALU.mult)
        sq211 = square("sq211", state["21"][:, halves[1], :])
        hidden(h2[:, 1, halves[1], :], sq211[:], adjoint(2, 1, 1, 5))
        yc = placed([P, 2 * G], F32, "yc_w")
        nc.vector.tensor_tensor(yc[:], product([(2, 0), (2, 1)], 6), step[:, 0 : 2 * G], ALU.mult)
        adj_bf3 = round_adj(3, adj3[:], nc.scalar.copy)
        quantise_adj(3, adj_bf3)
        quantise_h("h2", h2[:].rearrange("p a j t -> p (a j t)"), [(2, 0), (2, 1)])
        state = {name: placed([P, G, 4], F32, "state" + name) for name in ("30", "31")}
        tanh(3, 0, 0, state["30"][:, halves[0], :], 0)
        tanh(3, 0, 1, state["30"][:, halves[1], :], 2)
        yf = copied("yf", product([(3, 0), (3, 1)], 3))
        sq300 = square("sq300", state["30"][:, halves[0], :])
        sq301 = square("sq301", state["30"][:, halves[1], :])
        slope = less_one_on_gpsimd("slope300", sq300)

        page[2] = placed([P, S], F32, "page2")
        put(2, yc[:], 0)
        tanh(3, 1, 0, state["31"][:, halves[0], :], 7)
        yd = weigh_run("yd_w", copied("yd", product([(0, 2)], 1)), 2 * G)
        tanh(3, 1, 1, state["31"][:, halves[1], :], 4)
        ye = weigh_pair("ye_w", copied("ye", product([(1, 2), (2, 2)], 6)), 2)
        yf = weigh_run("yf_w", yf, 0)
        put(0, yd[:], 2 * G)
        put(1, ye[:, 0, :], 2 * G)
        h3 = placed([P, 2, G, 4], BF16, "h3")
        nc.gpsimd.tensor_tensor(h3[:, 0, halves[0], :], slope[:], copied("b300", adjoint(3, 0, 0, 3))[:], ALU.mult)
        hidden(h3[:, 0, halves[1], :], sq301[:], adjoint(3, 0, 1, 5))
        for u in range(2):
            sq = square(f"sq31{u}", state["31"][:, halves[u], :])
            b = copied(f"b31{u}", adjoint(3, 1, u, (0, 2)[u]))
            nc.gpsimd.tensor_tensor(h3[:, 1, halves[u], :], less_one(f"slope31{u}", sq)[:], b[:], ALU.mult)
        put(2, ye[:, 1, :], 2 * G)
        y32 = copied("y32", product([(3, 2)], 1))
        turned = [open_sum(c, right, (3, 7)[c]) for c in range(2)]
        quantise_h("h3", h3[:].rearrange("p a j t -> p (a j t)"), [(3, 0), (3, 1)])

        page[3] = placed([P, S], F32, "page3")
        put(3, yf[:], 0)
        yi = placed([P, 2 * G], F32, "yi_w")
        nc.gpsimd.tensor_tensor(yi[:, first], y32[:], step[:, 2 * G : 3 * G], ALU.mult)
        put(0, weigh_run("yg_w", copied("yg", product([(0, 3)], 1)), 3 * G)[:], 3 * G)
        yh = weigh_pair("yh_w", copied("yh", product([(1, 3), (2, 3)], 6)), 3)
        nc.gpsimd.tensor_tensor(yi[:, second], copied("y33", product([(3, 3)], 2))[:], step[:, 3 * G :], ALU.mult)
        put(1, yh[:, 0, :], 3 * G)
        put(2, yh[:, 1, :], 3 * G)
        put(3, yi[:], 2 * G)
        total = [placed([P, S], F32, f"total{c}") for c in range(3)]
        for c in range(2):
            finish_on_gpsimd(c, total[c], [left])
            finish_on_tensor(c, total[c], right, turned[c], (5, 0)[c])
        finish_on_gpsimd(2, total[2], [left, right])
        finish_on_vector(3)
